import numpy as np, ml_dtypes
CORES = [3,11,19,27,35,43,51,59]
N = 8
BF = ml_dtypes.bfloat16
def gentries(a):
    return np.ascontiguousarray(a.reshape(8, 16, -1).transpose(0, 2, 1)).reshape(8, -1)
def gtable(e):
    e = np.asarray(e); return np.ascontiguousarray(e.reshape(8, -1, 16).transpose(0, 2, 1)).reshape(128, -1).astype(np.int32)
B0, S, RO, DA = 1152, 224, 3, 512
TS, TE, TC = 11, 8, 12
JUMPS = [1, 5, 3]
W = B0 + RO * S
QC = 0.15
def parts(rng):
    x = rng.integers(0, 256, (N, 8, 16, B0)); x = np.where(rng.random((N, 8, 1, B0)) < 0.02, x >> 4, x)
    par = (np.arange(B0) - 1 - rng.integers(0, B0 >> 4, (N, 8, B0))) % B0
    p = np.zeros((N, 8, 16, B0), np.int64); p[:, :, 0] = np.arange(B0)
    for k in range(1, 16): p[:, :, k] = np.take_along_axis(par, p[:, :, k - 1], 2)
    v = rng.integers(0, B0, (N, 8, S))
    near = np.take_along_axis(v, rng.integers(0, S, (N, 8, B0)), 2)
    c = np.where(rng.random((N, 8, B0)) < 0.5, near, rng.integers(0, B0, (N, 8, B0)))
    c = np.where(rng.random((N, 8, B0)) < QC, c, -1)
    return x, p, c, rng.integers(0, 256, (N, 8, 16, DA)), rng.integers(0, 4096, (N, 8, 16, 16)), v
def pack(x, p, c, d, w, v):
    return {"lab": np.ascontiguousarray(x.reshape(N, 128, B0)).astype(np.float32).astype(BF), "pth": np.ascontiguousarray(p.reshape(N, 128, B0)).astype(np.int32),
            "cov": np.ascontiguousarray(c).astype(np.int32), "act": np.ascontiguousarray(d.reshape(N, 128, DA)).astype(np.float32).astype(BF),
            "wts": np.ascontiguousarray(w.reshape(N, 128, 16)).astype(np.int32), "leaf": np.stack([gtable(a) for a in v])}
def setup_inputs(rng):
    return pack(*parts(rng))
def setup_inputs_spread(rng):
    x, p, c, d, w, v = parts(rng)
    x = np.where(rng.random((N, 8, 1, B0)) < 0.03, (256 * np.exp2(-7 * rng.random((N, 8, 1, B0))) * rng.random(x.shape)).astype(np.int64), x)
    d = (256 * np.exp2(-7 * rng.random((N, 8, 1, DA))) * rng.random(d.shape)).astype(np.int64)
    w = np.exp2(12 * rng.random(w.shape)).astype(np.int64) - 1
    p = np.where(rng.random((N, 8, 1, B0)) < 0.5, rng.integers(0, B0, p.shape), p)
    c = np.where(rng.random(c.shape) < 0.5, c, -1)
    v = (B0 * rng.random(v.shape) ** 3).astype(np.int64)
    return pack(x, p, c, d, w, v)
def setup_inputs_ends(rng):
    x = 255 * (rng.random((N, 8, 16, B0)) < 0.75).astype(np.int64); k = rng.random((N, 8, 1, B0))
    x = np.where(k < 0.01, 0, np.where(k > 0.95, 255, x))
    x[:, 1::2, :, B0 - 1] = 255; x[:, ::2, :, B0 - 1] = 0; x[:, :, :, 2:4] = 255
    d = 255 * (rng.random((N, 8, 16, DA)) < 0.85).astype(np.int64); d[..., 16] = 0; d[..., 0] = 255; d[..., DA - 1] = 255
    w = 4095 * rng.integers(0, 2, (N, 8, 16, 16)); w[..., 15] = 4095; w[..., 2] = 0; w[:, 1::2, :, 0] = 4095
    p = (B0 - 1) * rng.integers(0, 2, (N, 8, 16, B0)); p = np.where(rng.random(p.shape) < 0.28, rng.integers(0, B0, p.shape), p)
    c = np.where(rng.random((N, 8, B0)) < 0.06, B0 - 1, -1); c[:, :, 0] = -1; c[:, :, B0 - 1] = -1; c[:, 5, B0 - 1] = B0 - 1
    v = (B0 - 1) * rng.integers(0, 2, (N, 8, S)); v = np.where(rng.random(v.shape) < 0.3, rng.integers(0, B0, v.shape), v)
    return pack(x, p, c, d, w, v)
def setup_inputs_corners(rng):
    x, p, c, d, w, v = parts(rng); a = np.arange(B0); h = B0 >> 1
    for r in range(N):
        for g in range(8):
            k = (g + r) % 8
            if k == 0: p[r, g] = a
            elif k == 1:
                p[r, g] = np.where(((np.arange(16)[:, None] + a) & 1) == 0, 0, B0 - 1); c[r, g, 0] = -1; c[r, g, B0 - 1] = -1
                v[r, g] = np.where(rng.random(S) < 0.5, v[r, g], (B0 - 1) * rng.integers(0, 2, S))
            elif k == 2: w[r, g] = 0
            elif k == 3:
                c[r, g] = np.where(a >= h, a, -1); p[r, g, :, :h] = p[r, g, :, :h] % h
            elif k == 4:
                x[r, g] = np.where(rng.random((1, B0)) < 0.9, 100, x[r, g]); d[r, g] = np.where(rng.random((1, DA)) < 0.5, 0, d[r, g])
                c[r, g] = np.where(rng.random(B0) < 0.02, rng.integers(0, B0, B0), -1)
            elif k == 5:
                w[r, g] = 4095 * np.eye(16, dtype=np.int64)
                x[r, g] = rng.choice(np.array([0, 1, 2, 255]), (16, B0)); d[r, g] = rng.choice(np.array([0, 1, 255]), (16, DA))
                c[r, g] = np.where(rng.random(B0) < 0.03, c[r, g], -1)
            elif k == 6:
                o = int(rng.integers(0, B0)); v[r, g] = o; c[r, g, p[r, g, :, o]] = -1
            else:
                z = 16 - TS + rng.integers(0, 2, (1, B0)); z[:, B0 - 16:] = 0
                x[r, g] = 100 - (np.argsort(rng.random((16, B0)), axis=0) < z)
                c[r, g] = np.where(rng.random(B0) < 0.05, B0 - 1 - rng.integers(0, 16, B0), -1); c[r, g, B0 - 16:] = -1
    return pack(x, p, c, d, w, v)
def setup_inputs_crowd(rng):
    x, p, c, d, w, v = parts(rng); c[:] = -1
    for r in range(N):
        for g in range(8):
            k = (g + r) % 4; o = rng.permutation(B0)[:S + 4]; y, z, q, b = [int(e) for e in o[:4]]; v[r, g] = o[4:]
            p[r, g] = np.where((p[r, g] == y) | (p[r, g] == z) | (p[r, g] == b), q, p[r, g])
            x[r, g, :, z] = 0; x[r, g, :, b] = 0; c[r, g, y] = z; hit = np.zeros(S, bool)
            if k < 2: hit[:] = True
            if k == 0:
                i = int(rng.integers(0, S)); hit[i] = False
                h = 128 * int(np.sum(w[r, g, :, 0])) & 4095; n = TC + (rng.random(B0) < 0.25).astype(np.int64); n[(h * B0) >> 12] = TC
                low = np.argsort(rng.random((16, B0)), axis=0) < n
                x[r, g] = np.where(low, rng.integers(0, 129, (16, B0)), rng.integers(129, 256, (16, B0)))
                x[r, g, :, z] = 0; x[r, g, :, b] = 0; x[r, g, :, int(v[r, g, i])] = 128; d[r, g, :, h & (DA - 1)] = 0
            if k == 3: hit[0] = True
            if k >= 2:
                t = p[r, g, ::2]; t[:, v[r, g]] = b
            p[r, g, 15, v[r, g][hit]] = y
    return pack(x, p, c, d, w, v)
def setup_inputs_brims(rng):
    x, p, c, d, w, v = parts(rng); turn = int(rng.integers(0, 4))
    for r in range(N):
        for g in range(8):
            k = (g + turn) % 4; t = x[r, g]; u = p[r, g]
            if k == 0:
                b = np.where(rng.random((16, B0)) < 0.85, 192, 64 * rng.integers(0, 4, (16, B0))); b[15] = 1
                t[:] = np.where(rng.random((1, B0)) < 0.75, b, t); t[:, [0, B0 - 1]] = 0
                w[r, g] = 64 * rng.integers(56, 64, (16, 16)); w[r, g, 15] = 4095 * ((np.arange(16) + int(rng.integers(0, 2))) & 1)
                e = np.where(rng.random((16, DA)) < 0.9, 0, 64 * rng.integers(0, 4, (16, DA))); e[15] = rng.integers(0, 2, DA); e[:, [0, DA - 1]] = 0
                d[r, g] = e; c[r, g] = -1
            elif k == 1:
                t[:] = np.where(rng.random((1, B0)) < 0.5, 255 - (rng.random((16, B0)) < 0.2).astype(np.int64), t)
                w[r, g] = 4095 - rng.integers(0, 6, (16, 16)); d[r, g] = d[r, g] * (rng.random((1, DA)) < 0.5); c[r, g] = -1
            elif k == 2:
                o = 1 + rng.permutation(B0 - 1)[:S + 10]; y, z = int(o[0]), int(o[1]); few = o[2:10]; v[r, g] = o[10:]
                m = rng.random(S) < 0.75; m[int(rng.integers(0, S))] = False; wait = v[r, g][m]; go = v[r, g][~m]; n = len(wait)
                u[:] = np.where((u == y) | (u == z), 0, u); u[0, wait] = rng.choice(few, n); u[15, wait] = y; u[:, go] = z
                c[r, g] = -1; c[r, g, y] = z
                t[:, 0] = 255; t[:, y] = 100; t[:, z] = 50; t[:, few] = rng.integers(0, 32, (16, 8))
                t[:, wait] = np.where(rng.random((1, n)) < 0.5, 255, t[:, wait])
                t[0, wait] = np.where(rng.random(n) < 0.5, rng.integers(240, 256, n), rng.integers(0, 240, n)); t[0, go] = 0
                w[r, g, :, :2] = 0; w[r, g, 0, :2] = 16
                d[r, g] = d[r, g] * (rng.random((1, DA)) < 0.3)
    return pack(x, p, c, d, w, v)
def check_inputs(d):
    bad = []
    for k, lo, hi in (("lab", 0, 255), ("pth", 0, B0 - 1), ("cov", -1, B0 - 1), ("act", 0, 255), ("wts", 0, 4095), ("leaf", 0, B0 - 1)):
        a = np.asarray(d[k]).astype(np.float64)
        if not (np.min(a) >= lo and np.max(a) <= hi and np.all(a == np.floor(a))): bad.append("range of " + k)
    return bad
def pick(t, ix):
    return np.take_along_axis(t, ix[:, :, None, :], 3)
def reference(lab, pth, cov, act, wts, leaf):
    x = np.full((N, 8, 16, W), 256, np.int32); x[..., :B0] = lab.astype(np.float32).astype(np.int32).reshape(N, 8, 16, B0)
    p = np.zeros((N, 8, 16, W), np.int64); p[..., :B0] = pth.reshape(N, 8, 16, B0)
    c = np.full((N, 8, W), -1, np.int64); c[..., :B0] = cov
    d = act.astype(np.float32).astype(np.int32).reshape(N, 8, 16, DA)
    w = wts.astype(np.int32).reshape(N, 8, 16, 16).transpose(0, 1, 3, 2)
    v = np.stack([gentries(a) for a in leaf]).astype(np.int64)
    for t in range(RO):
        B = B0 + t * S
        xv = pick(x, v); pv = pick(p, v)
        flat = pv.reshape(N, 8, 16 * S); xp = pick(x, flat).reshape(N, 8, 16, 16, S)
        cp = np.take_along_axis(c, flat, 2); xc = pick(x, np.maximum(cp, 0)).reshape(N, 8, 16, 16, S)
        holds = (cp.reshape(N, 8, 16, S) >= 0) & (np.sum(xp >= xc, axis=2) >= TS)
        susp = np.any(holds, axis=2); live = ~susp; cnt = np.sum(susp, axis=2)
        h = np.matmul(w, xv) & 4095
        xn = np.abs(xv - pick(d, h[:, :, 0] & (DA - 1)))
        q = (h[:, :, 1] * B) >> 12
        e = np.stack([np.take_along_axis(x[(r + JUMPS[t]) % N], q[r][:, None, :], 2) for r in range(N)])
        low = np.sum(xp >= e[:, :, :, None, :], axis=2) < TE
        want = np.any(low, axis=2) & live & (e[:, :, 0] < 256)
        tg = np.where(want, np.take_along_axis(pv, np.argmax(low, axis=2)[:, :, None, :], 2)[:, :, 0], -1)
        cand = ((np.matmul(w, xn) & 4095) * B) >> 12
        xk = pick(x, cand.reshape(N, 8, 16 * S)).reshape(N, 8, 16, 16, S)
        fit = np.sum(xn[:, :, :, None, :] >= xk, axis=2) >= (TC + (cnt & 1))[:, :, None, None]
        cn = np.where(np.any(fit, axis=2), np.take_along_axis(cand, np.argmax(fit, axis=2)[:, :, None, :], 2)[:, :, 0], -1)
        new = np.broadcast_to(B + np.arange(S), (N, 8, S))
        for r in range(N):
            for g in range(8):
                s = np.nonzero(tg[r, g] >= 0)[0]
                u, first = np.unique(tg[r, g][s], return_index=True); s = s[first]
                x[r, g][:, u] = np.maximum(x[r, g][:, u], e[r, g][:, s])
        x[..., B:B + S] = np.where(live[:, :, None, :], xn, 256)
        p[..., B:B + S] = np.where(live[:, :, None, :], np.concatenate([new[:, :, None, :], pv[:, :, :15]], axis=2), 0)
        c[..., B:B + S] = np.where(live, cn, -1)
        v = np.where(live, new, v)
    return {"yx": x.reshape(N, 128, W).astype(np.float32).astype(BF), "yp": np.ascontiguousarray(p[..., B0:]).reshape(N, 128, RO * S).astype(np.float32),
            "yc": np.ascontiguousarray(c[..., B0:]).astype(np.float32), "yv": np.stack([gtable(a) for a in v]).astype(np.float32)}

@@ -1,0 +1,669 @@
+import numpy as np
+from concourse.mybir import AluOpType, ActivationFunctionType
+
+OP = AluOpType
+AF = ActivationFunctionType
+B0, S, RO, DA = 1152, 224, 3, 512
+JUMPS = [1, 5, 3]
+W = B0 + RO * S
+O = 32
+XW = O + W
+CADD = 131072.0 + 512.5
+FLOOR = -0.49609375
+SAMEW = True
+ACT_HOLD = [512, 1024, 1024]
+ACT_PATH = [0, 0, 0]
+VEC_SGN = [0, 0, 0]
+VEC_GAT = [0, 0, 0]
+ON_ACT = [1, 0, 0]
+LINK = 100.0
+
+BF, F32, F16, I32, U16 = "bfloat16", "float32", "float16", "int32", "uint16"
+SB = {
+    "X": ([128, XW], BF), "X2": ([128, W - S], BF), "XP": ([128, O + W - S], BF), "R0": ([128, B0], BF), "R1": ([128, B0 + S], BF),
+    "R2": ([128, B0 + 2 * S], BF), "AC": ([128, DA], BF), "PTH": ([128, B0], I32), "COVI": ([128, 128], I32),
+    "COVH": ([128, 128], F16), "COVL": ([128, 128], U16), "WI": ([128, 16], I32), "WH": ([128, 2, 16], BF),
+    "WM": ([128, 4, 16], BF), "LW": ([128, 4, 144], BF), "LFI": ([128, 16], I32), "LF0": ([128, 16], U16),
+    "LF": ([128, 16], F32), "LFU": ([128, 16], U16),
+    "IP": ([128, 8], I32), "COL": ([128, 16], F32), "IC": ([128, 144], F32), "IG": ([128, 144], F32),
+    "IS": ([128, 672], F32), "IA": ([128, 224], F32), "IJ": ([128, 48], F32),
+    "ROL": ([128, 16], U16), "SELB": ([128, 144], BF), "SELN": ([128, 144], BF), "SELH": ([128, 144], F16), "BLK1": ([128, 128], BF),
+    "BLKP": ([128, 128], BF), "BLKN": ([128, 128], BF), "BLKM": ([128, 128], BF), "CS1": ([128, 128], BF),
+    "CS2": ([128, 128], BF), "ONES": ([128, 512], BF), "TRI": ([128, 128], BF), "IDB": ([128, 128], BF),
+    "NIDB": ([128, 128], BF), "NI2": ([128, 128], BF), "E0": ([128, 128], F16), "IDH": ([128, 128], F16),
+    "SHF": ([128, 128], F16), "XH": ([128, 2, 144], F16),
+    "NEWN": ([128, 672], F16), "NEWL": ([128, 48], F16), "MASKD": ([128, 224], BF), "RST": ([128, 224], BF),
+    "XO": ([128, 2, 144], F16), "BLKH": ([128, 128], F16), "TGX": ([128, 224], F32), "XG": ([128, 1792], BF), "G8": ([128, 8], F16),
+    "XV": ([128, 224], BF), "PV": ([128, 224], F16), "PVT": ([128, 224], F32), "TOH": ([128, 224], F32),
+    "TOP": ([128, 224], F32), "HI": ([128, 32], I32), "HA": ([128, 16], I32), "HQ": ([128, 16], I32),
+    "AL": ([128, 16], U16), "QL": ([128, 16], U16), "POF": ([128, 256], U16), "DZ": ([128, 224], BF), "Z": ([128, 224], BF),
+    "ZT": ([128, 224], BF), "ZI": ([128, 224], I32), "ZJ": ([128, 224], I32), "COF": ([128, 224], U16), "CI": ([128, 224], I32),
+    "CMP": ([128, W - S], BF), "XC": ([128, 1024], BF), "CE": ([128, 224], F32), "E": ([128, 224], BF), "EM": ([128, 224], BF),
+    "PO": ([128, 3584], BF), "XK": ([128, 3584], BF), "SG": ([128, 3584], BF), "LOW": ([128, 224], BF), "HLD": ([128, 224], BF),
+    "SE": ([128, 224], F32), "SH": ([128, 224], F16), "FIT": ([128, 224], BF), "SH2": ([128, 224], F16),
+    "TGH": ([128, 16], F16), "TGU": ([128, 16], U16), "EQ": ([128, 224], BF), "SC": ([128, 224], BF), "OFF": ([128, 16], F32),
+    "OFU": ([128, 32], U16), "V": ([128, 224], BF), "JNK": ([128, 224], BF), "ACC": ([128, 8], F32), "PAR": ([128, 8], I32),
+    "BIA": ([128, 8], F32), "YP": ([128, 672], F32), "YC": ([128, 672], F32), "YV": ([128, 16], F32), "KB": ([128, 8], F32),
+}
+SCRATCH = {k: ("sbuf", v[0], v[1]) for k, v in SB.items()}
+for _n in ("PH1", "PD0", "PD1", "PC", "PP", "PM"):
+    SCRATCH[_n] = ("psum", [128, 512], F32)
+SCRATCH["PH0"] = ("psum", [128, 16, 2, 16], F32)
+SCRATCH["PX"] = ("psum", [128, 16, 2, 16], F32)
+NDMA = 32
+SEMAPHORES = (["cv", "ca", "cp", "cg"] + ["arr%d" % i for i in range(6)] + ["snt%d" % i for i in range(6)]
+              + ["d%d" % i for i in range(NDMA)])
+BIG = 1 << 30
+PLAN = {}
+SLACKS, SHAKE, TURNS = (0.0, 100.0, 250.0), (600.0, 2000.0, 1200.0, 5000.0), 2500
+CYC, PE, FIX, WAKE = 1.04, 0.52, 60.0, 60.0
+
+
+def rank_program(g, core, T, topo):
+    rank = T.rank_of(core)
+    if rank is None:
+        return
+    n = len(T.cores)
+    Q = {"v": g.vector, "a": g.scalar, "p": g.tensor, "g": g, "s": g.sync}
+    ops = []
+    total = {}
+    seen = {q: {} for q in Q}
+    hist = {}
+    nd = [0, 0]
+    ALL = slice(None)
+
+    def A(name, lo=None, hi=None, step=None, rows=None):
+        r = ALL if rows is None else slice(rows[0], rows[1])
+        if lo is None:
+            return (T[name][:] if rows is None else T[name][r], name, 0, BIG)
+        if step is None:
+            return (T[name][r, lo:hi], name, lo, hi)
+        return (T[name][r, lo:hi:step], name, lo, hi)
+
+    def M(name, *ix):
+        return (T[name][ix], name, 0, BIG)
+
+    def IND(win, off):
+        return (win[0].indirect(off[0]), win[1], win[2], win[3], off)
+
+    def need(q, sem, val):
+        if seen[q].get(sem, 0) < val:
+            Q[q].wait_ge(T.sem[sem], val)
+            seen[q][sem] = val
+
+    def size(o):
+        if len(o) > 4:
+            return 16 * size(o[4])
+        k = 1
+        for d in list(o[0].shape)[1:]:
+            k *= int(d)
+        return k
+
+    def cost(q, outs, ins, base):
+        k = max(size(x) for x in outs + ins)
+        if q == "p":
+            return max(64, size(outs[0])) * PE
+        if q == "g":
+            return 170 + 2 * k * CYC
+        if len(outs[0]) > 4:
+            return 50 + k * 3.8 * CYC
+        if any(len(x) > 4 for x in ins):
+            return 55 + k * 1.56 * CYC
+        if base == 0:
+            base = 0.5 if all(SCRATCH[x[1]][2] in (BF, F16, U16) for x in outs + ins if size(x) > 1) else 1
+        if base == 2 and any(SCRATCH[x[1]][0] == "psum" for x in ins):
+            base = 1
+        return FIX + max(64, k * base) * CYC
+
+    def add(q, outs, ins, fn, busy, lat, sem, inc, after=None):
+        dma = sem is not None
+        acc = [(o, True) for o in outs] + [(o, False) for o in ins]
+        acc += [(o[4], False) for o in outs + ins if len(o) > 4]
+        pre = {}
+        if after is not None:
+            pre[after] = False
+        me = len(ops)
+        for o, wr in acc:
+            ps = SCRATCH[o[1]][0] == "psum"
+            for lo, hi, w2, j in hist.get(o[1], []):
+                over = lo < o[3] and o[2] < hi
+                if not (ps or (over and (w2 or wr))):
+                    continue
+                if ops[j]["q"] == q and not dma and not ops[j]["dma"]:
+                    wait = q != "p" and over and w2 and (not wr or SAMEW)
+                else:
+                    wait = True
+                pre[j] = pre.get(j, False) or wait
+        ops.append({"q": q, "fn": fn, "busy": busy, "lat": lat, "sem": sem, "inc": inc, "pre": pre, "dma": dma})
+        for o, wr in acc:
+            h = hist.setdefault(o[1], [])
+            if SCRATCH[o[1]][0] == "psum":
+                h[:] = [e for e in h if ops[e[3]]["q"] == q and q != "p" and e[2]]
+            elif wr and len(o) == 4:
+                h[:] = [e for e in h if not (o[2] <= e[0] and e[1] <= o[3])]
+            h.append((o[2], o[3], wr, me))
+        return me
+
+    def op(q, outs, ins, fn, base=1):
+        ins = [x for x in ins if isinstance(x, tuple)]
+        c = cost(q, outs, ins, base)
+        add(q, outs, ins, fn, c, c, None, 1)
+
+    def dma(q, out, in_, after=None):
+        outs = [out] if isinstance(out, tuple) else []
+        ins = [in_] if isinstance(in_, tuple) else []
+        o = (outs + ins)[0]
+        sem = "d%d" % nd[0]
+        nd[0] += 1
+        by = size(o) * 128 * (2 if SCRATCH[o[1]][2] == BF else 4)
+        return add(q, outs, ins, lambda: Q[q].dma_start(ap(out), ap(in_)).then_inc(T.sem[sem], 16), 100,
+                   2000 + by / 150.0 + (len(ops) * 150 if after is not None else 0), sem, 16, after)
+
+    def emit():
+        m = len(ops)
+        nxt = [[] for _ in ops]
+        for i, o in enumerate(ops):
+            for j in o["pre"]:
+                nxt[j].append(i)
+
+        def plan(prio, back, slack):
+            out = [list(o["pre"]) for o in ops] if back else nxt
+            left = [len(nxt[i]) if back else len(ops[i]["pre"]) for i in range(m)]
+            can = [ops[i]["lat"] - ops[i]["busy"] if back else 0.0 for i in range(m)]
+            ready = {q: [] for q in "vapgsr"}
+            free = {q: 0.0 for q in ready}
+            for i in range(m):
+                if not left[i]:
+                    ready[ops[i]["q"]].append(i)
+            seq, at, end = [], [0.0] * m, 0.0
+            for _ in range(m):
+                best = None
+                for q, r in ready.items():
+                    if r:
+                        t0 = max(free[q], min([can[i] for i in r]))
+                        if best is None or t0 < best[0]:
+                            best = (t0, q)
+                t0, q = best
+                i = min([i for i in ready[q] if can[i] <= t0 + slack], key=lambda i: prio[i])
+                o = ops[i]
+                ready[q].remove(i)
+                t0 = max(free[q], can[i])
+                free[q] = t0 + o["busy"]
+                at[i] = free[q] if back else t0
+                end = max(end, t0 + o["lat"])
+                seq.append(i)
+                for k in out[i]:
+                    if back:
+                        d = at[i] + (ops[k]["lat"] + WAKE - ops[k]["busy"] if o["pre"][k] else 0)
+                    else:
+                        d = t0 + (o["lat"] + WAKE if ops[k]["pre"][i] else o["busy"])
+                    can[k] = max(can[k], d)
+                    left[k] -= 1
+                    if not left[k]:
+                        ready[ops[k]["q"]].append(k)
+            return seq, at, end
+
+        if m not in PLAN:
+            good = None
+            rnd = np.random.default_rng(7)
+            for turn in range(TURNS):
+                slack = SLACKS[turn % len(SLACKS)]
+                if turn < len(SLACKS):
+                    prio = list(range(m))
+                else:
+                    t1 = rnd.random() * good[0]
+                    w = (rnd.random(m) - 0.5) * SHAKE[turn % len(SHAKE)] * (rnd.random(m) < 0.3)
+                    prio = [x + (y if t1 - 4000 < z < t1 + 4000 else 0) for x, y, z in zip(good[3], w.tolist(), good[2])]
+                    slack = good[4] if turn % 8 else slack
+                for k in range(6 if turn < len(SLACKS) else 2 if turn % 5 == 0 else 1):
+                    if k:
+                        prio = [-x for x in plan([-x for x in at], True, slack)[1]]
+                    seq, at, end = plan(prio, False, slack)
+                    if good is None or end <= good[0]:
+                        good = (end, seq, at, prio if k or turn >= len(SLACKS) else at, slack)
+            PLAN[m] = good
+        val = [0] * m
+        for i in PLAN[m][1]:
+            o = ops[i]
+            q = o["q"]
+            if q != "r":
+                want = {}
+                for j, wait in o["pre"].items():
+                    if wait:
+                        sem = ops[j]["sem"] or "c" + ops[j]["q"]
+                        want[sem] = max(want.get(sem, 0), val[j])
+                for sem, v in want.items():
+                    need(q, sem, v)
+            if o["dma"]:
+                if q != "r":
+                    o["fn"]()
+                val[i] = total[o["sem"]] = o["inc"]
+            else:
+                o["fn"]().then_inc(T.sem["c" + q], 1)
+                val[i] = total["c" + q] = total.get("c" + q, 0) + 1
+        for sem, v in total.items():
+            need("s", sem, v)
+
+    def ap(x):
+        return x[0] if isinstance(x, tuple) else x
+
+    def cp(out, in_):
+        op("v", [out], [in_], lambda: g.vector.tensor_copy(out[0], in_[0]), 0)
+
+    def tt(out, a, b, o):
+        op("v", [out], [a, b], lambda: g.vector.tensor_tensor(out[0], a[0], b[0], o), 2)
+
+    def ts(out, a, s1, o1, s2=None, o2=None):
+        if o2 is None:
+            op("v", [out], [a, s1], lambda: g.vector.tensor_scalar(out[0], a[0], ap(s1), None, o1), 0)
+        else:
+            op("v", [out], [a, s1, s2], lambda: g.vector.tensor_scalar(out[0], a[0], ap(s1), ap(s2), o1, o2), 0)
+
+    def ms(out, c):
+        op("v", [out], [], lambda: g.vector.memset(out[0], c), 0)
+
+    def tr(out, in_):
+        op("v", [out], [in_], lambda: g.vector.transpose(out[0], in_[0]))
+
+    def scan(out, a, b, init, o0, o1):
+        op("v", [out], [a, b], lambda: g.vector.tensor_tensor_scan(out[0], a[0], b[0], init, o0, o1), 0)
+
+    def act(out, in_, f, bias=0.0, scale=1.0, accum=None):
+        outs = [out] if accum is None else [out, accum]
+        if accum is None:
+            op("a", outs, [in_, bias, scale], lambda: g.scalar.activation(out[0], in_[0], f, bias=ap(bias), scale=ap(scale)))
+        else:
+            op("a", outs, [in_, bias, scale],
+               lambda: g.scalar.activation(out[0], in_[0], f, bias=ap(bias), scale=ap(scale), accum_out=accum[0]))
+
+    def mm(out, l, r, start=True, stop=True):
+        op("p", [out], [l, r], lambda: g.tensor.matmul(out[0], l[0], r[0], start, stop))
+
+    def iota(out, pat, base, cm, fl=True):
+        if fl:
+            op("g", [out], [], lambda: g.iota(out[0], pat, base, cm, allow_small_or_imprecise_dtypes=True))
+        else:
+            op("g", [out], [], lambda: g.iota(out[0], pat, base, cm))
+
+    def asel(out, in_, pat, cmp_, fill, base, cm):
+        op("g", [out], [in_], lambda: g.affine_select(out[0], in_[0], pat, cmp_, fill, base, cm))
+
+    def push(t, lo, hi):
+        dst = T.cores[(rank - JUMPS[t]) % n]
+        rid, pid, _ = topo.addr(dst)
+        k = len(topo.engines(core, dst))
+        src = A("X", O + lo, O + hi)
+        arr, snt = "arr%d" % nd[1], "snt%d" % nd[1]
+        nd[1] += 1
+        lat = 2200 + (hi - lo) * 256 / LINK
+        me = add("g", [], [src], lambda: g.remote_dma(T["R%d" % t][:, lo:hi], src[0], T.sem[arr], T.sem[snt], pid, rid,
+                                                     topo.mask(core, dst)), 300, lat, snt, k)
+        k2 = len(topo.engines(T.cores[(rank + JUMPS[t]) % n], core))
+        add("r", [A("R%d" % t, lo, hi)], [], None, 0, lat - 300, arr, k2, after=me)
+
+    def col(j):
+        return A("COL", j, j + 1)
+
+    def kb(j):
+        return [0.5, CADD, CADD - 255.0, -float(O), 1.0 - O, -1.0, 256.0][j]
+
+    d = dma("s", A("X", O, O + B0 // 2), T.lab[:, 0:B0 // 2])
+    d = dma("s", A("WI"), T.wts[:], d)
+    d = dma("s", A("X", O + B0 // 2, O + B0), T.lab[:, B0 // 2:B0], d)
+    d = dma("s", A("LFI", 0, 14), T.leaf[:], d)
+    for gi in range(8):
+        c = dma("as"[gi // 6], A("COVI", 16 * gi, 16 * gi + 16, rows=(0, 72)), T.cov[gi], d if gi >= 6 else None)
+        if gi >= 6:
+            d = c
+    d = dma("s", A("X2", ACT_HOLD[0], B0), T.lab[:, ACT_HOLD[0]:B0], d)
+    d = dma("s", A("AC"), T.act[:], d)
+    d = dma("s", A("PTH"), T.pth[:], d)
+
+    iota(A("IP", 0, 1), [[0, 1]], 0, 1, False)
+    iota(A("IC"), [[1, 144]], 0, 0)
+    iota(A("IG"), [[1, 9], [0, 16]], 0, 0)
+    iota(A("IJ"), [[16, 48]], 0, 0)
+    ms(A("ONES"), 1.0)
+    ms(A("LW"), 0.0)
+    asel(A("IDB"), A("ONES", 0, 128), [[-1, 128]], OP.is_equal, 0.0, 0, 1)
+    ts(A("IP", 1, 2), A("IP", 0, 1), 15, OP.bitwise_and)
+    ts(A("IP", 2, 3), A("IP", 0, 1), 4, OP.arith_shift_right)
+    ts(A("IP", 3, 4), A("IP", 0, 1), 4, OP.arith_shift_right, 1, OP.bitwise_and)
+    ts(A("IP", 4, 5), A("IP", 0, 1), 111, OP.bitwise_and)
+    ms(A("X", 0, O), 512.0)
+    cp(A("COL", 0, 3), A("IP", 1, 4))
+    ts(col(5), A("IP", 4, 5), 16.0, OP.add)
+    ts(col(3), col(2), -1.0, OP.mult, 1.0, OP.add)
+    ts(A("BLK1"), A("IG", 0, 128), col(1), OP.is_equal)
+    ts(col(9), col(0), 7.0, OP.is_ge, -208.0, OP.mult)
+    asel(A("IDH"), A("ONES", 0, 128), [[-1, 128]], OP.is_equal, 0.0, 0, 1)
+    act(A("BLKM"), A("BLK1"), AF.Identity, scale=float(1 << 23))
+    act(A("NIDB"), A("IDB"), AF.Identity, scale=-1.0)
+    act(A("CS2"), A("ONES", 0, 128), AF.Identity, scale=-5.0 * 65536)
+    act(A("CS1"), A("ONES", 0, 128), AF.Identity, scale=-10.5 * 65536)
+    ts(col(10), col(0), 32.0, OP.mult, col(9), OP.add)
+    cp(M("WH", ALL, 0, ALL), A("WI"))
+    ts(A("ROL"), A("IC", 0, 16), col(10), OP.add, 223.0, OP.min)
+    tt(M("WH", ALL, 1, ALL), A("WI"), M("WH", ALL, 0, ALL), OP.subtract)
+    ts(A("LFU", 0, 14), A("LFI", 0, 14), float(O), OP.add)
+    for h in range(2):
+        ts(M("WM", ALL, slice(2 * h, 2 * h + 2), ALL), A("WH"), col(3 - h), OP.mult)
+    for p in range(4):
+        r = slice(32 * p, 32 * p + 32)
+        act(M("LW", r, ALL, slice(32 * p + 16, 32 * p + 32)), M("WM", r, ALL, ALL), AF.Identity)
+    ts(A("COVH", rows=(0, 72)), A("COVI", rows=(0, 72)), float(O), OP.add)
+    mm(A("PM", 0, 72), A("COVH", rows=(0, 72)), A("IDH", 0, 72, rows=(0, 72)))
+    cp(A("COVL", 0, 72), A("PM", 0, 72))
+    cp(A("LF0", 0, 14), A("LFI", 0, 14))
+    for h in range(2):
+        ts(M("XH", ALL, h, ALL), A("IC"), col(5), OP.is_equal, col(3 - h), OP.mult)
+    ts(col(4), col(1), 16.0, OP.mult, 15.0, OP.add)
+    ts(A("SELB"), A("IC"), col(4), OP.is_equal)
+    act(A("XP", 0, O), A("ONES", 0, O), AF.Identity)
+    ts(A("LF", 0, 14), A("LFI", 0, 14), float(O), OP.add)
+    ts(col(6), col(0), 1.0, OP.add)
+    ts(col(8), col(0), -4096.0, OP.mult, 4096.0, OP.add)
+    ts(A("NEWL", 0, 42), A("IJ", 0, 42), col(0), OP.add, float(O + B0), OP.add)
+    act(A("BLKN"), A("BLK1"), AF.Identity, scale=-131072.0)
+    act(A("BLKP"), A("BLK1"), AF.Identity, scale=4096.0)
+    act(A("SELN"), A("SELB"), AF.Identity, scale=-4096.0)
+    act(A("NI2"), A("IDB"), AF.Identity, scale=-2048.0)
+
+    push(0, 0, B0 // 2)
+    push(0, B0 // 2, B0)
+    iota(A("IS"), [[1, 672]], O + B0, 0)
+    iota(A("IA"), [[0, 14], [1, 16]], 0, 0)
+    act(A("MASKD"), A("IA"), AF.Relu, bias=col(8), scale=4096.0)
+    asel(A("TRI"), A("BLKN"), [[1, 128]], OP.is_gt, 0.0, 0, -1)
+    asel(A("TRI"), A("TRI"), [[1, 128]], OP.not_equal, 4096.0, 0, -1)
+    asel(A("SELH"), A("SELB"), [[1, 144]], OP.is_ge, 0.0, 0, 0)
+    asel(A("BLKH"), A("BLK1"), [[1, 128]], OP.is_ge, 0.0, 0, 0)
+    ts(col(11), col(1), col(3), OP.add)
+    for h in range(2):
+        ts(M("XO", ALL, h, ALL), A("IG"), col(11), OP.is_equal, col(3 - h), OP.mult)
+    for t in range(RO):
+        if t and VEC_SGN[t] == VEC_SGN[t - 1]:
+            continue
+        ts(col(7), col(0), 16.0 - 4 * VEC_SGN[t], OP.is_ge, -16.0, OP.mult)
+        ts(A("COL", 12 + t, 15), A("ONES", 0, 3 - t), -7.0, OP.mult, col(7), OP.add)
+    asel(A("RST"), A("ONES", 0, 224), [[0, 14], [1, 16]], OP.is_equal, 0.0, 0, 0)
+    asel(A("SHF"), A("BLK1"), [[1, 128]], OP.is_equal, 0.0, -1, -1)
+    asel(A("E0"), A("IDB"), [[0, 8], [1, 16]], OP.is_equal, 0.0, 0, 0)
+    asel(A("NEWN"), A("IS"), [[1, 672]], OP.is_ge, 0.0, 0, 0)
+    asel(A("G8"), A("BLK1", 0, 128, 16), [[1, 8]], OP.is_ge, 0.0, 0, 0)
+
+    def lw(h, hl, rho):
+        return M("LW", ALL, 2 * h + hl, slice(16 - 16 * rho, 144 - 16 * rho))
+
+    def px(h):
+        return M("PX", ALL, slice(0, 7), h, ALL)
+
+    PXA = M("PX", ALL, slice(0, 7), ALL, ALL)
+
+    def half(name, rho):
+        return A(name, 112 * rho, 112 * rho + 112)
+
+    def path_mm():
+        for h in range(2):
+            for rho in range(2):
+                mm(px(h), M("XH", ALL, h, slice(16 - 16 * rho, 144 - 16 * rho)), half("PV", rho), rho == 0, rho == 1)
+
+    def hold_gather(b, lo, hi):
+        tt(A("CMP", lo, hi), IND(A("X", 0, O + b), A("COVL", lo // 16, hi // 16)), A("X2", lo, hi), OP.is_le)
+
+    def ph0(w):
+        return M("PH0", ALL, slice(0, w // 32), ALL, ALL)
+
+    def hold_sum(lo, hi, bank, cs):
+        o = ph0(hi - lo) if bank == "PH0" else A(bank, 0, hi - lo)
+        mm(o, A(cs), A("ONES", 0, hi - lo), True, False)
+        mm(o, A("BLKM"), A("CMP", lo, hi), False, True)
+
+    def hold_max(lo, hi, bank):
+        o = ph0(hi - lo) if bank == "PH0" else A(bank, 0, hi - lo)
+        tt(A("XP", O + lo, O + hi), o, A("X", O + lo, O + hi), OP.max)
+
+    def hold_ag(b, lo, hi, bank):
+        act(A("XC", lo, hi), IND(A("X", 0, O + b), A("COVL", lo // 16, hi // 16)), AF.Identity)
+        mm(A(bank, 0, hi - lo), A("IDB"), A("X", O + lo, O + hi), True, False)
+        mm(A(bank, 0, hi - lo), A("NIDB"), A("XC", lo, hi), False, True)
+
+    def hold_as(lo, hi, bank):
+        act(A("CMP", lo, hi), A(bank, 0, hi - lo), AF.Sign, bias=kb(0))
+        hold_sum(lo, hi, bank, "CS2")
+
+    def sel_list(out, selname, src, first=True, last=True):
+        for a in range(16):
+            mm(out, A(selname, 15 - a, 143 - a), A(src, a, 224, 16), first and a == 0, last and a == 15)
+
+    def cover_a(t):
+        act(A("FIT"), A("PC", 0, 224), AF.Relu, bias=A("BIA", 0, 1))
+        mm(A("PC", 224, 448), A("BLKN"), A("HLD"), True, False)
+        mm(A("PC", 224, 448), A("TRI"), A("FIT"), False, True)
+        act(A("PC", 224, 448), A("PC", 224, 448), AF.Relu)
+
+    def cover_b(t):
+        tt(A("SH2"), A("PC", 224, 448), A("CI"), OP.min)
+        if t < RO - 1:
+            sel_list(A("PC", 448, 462), "SELH", "SH2")
+        mm(A("PC", 0, 224, rows=(0, 8)), A("G8"), A("SH2"))
+
+    def cover_c(t):
+        cp(A("COVL", 72 + 14 * t, 86 + 14 * t), A("PC", 448, 462))
+
+    def cover_d(t):
+        y = A("YC", S * t, S * t + S, rows=(0, 8))
+        act(y, A("PC", 0, 224, rows=(0, 8)), AF.Relu, bias=kb(4))
+        act(y, y, AF.Identity, bias=kb(5))
+
+    for t in range(RO):
+        b = B0 + t * S
+        last = t == RO - 1
+        XB = A("X", 0, O + b)
+        na = ACT_HOLD[t]
+        old = b - S if t else b
+        blocks = [(lo, min(lo + 512, old)) for lo in range(na, old, 512)]
+        act(A("XV"), IND(XB, A("LFU", 0, 14)), AF.Identity)
+        if t:
+            path_mm()
+            tr(A("TOP"), PXA)
+        for h in range(2):
+            for k in range(4):
+                mm(px(h), lw(h, k & 1, k >> 1), half("XV", k >> 1), k == 0, k == 3)
+        hold_ag(b, 0, 512, "PD0")
+        hold_gather(b, *blocks[0])
+        hold_sum(blocks[0][0], blocks[0][1], "PH0", "CS1")
+        tr(A("TOH"), PXA)
+        hold_as(0, 512, "PD0")
+        cp(A("HI"), IND(A("TOH", 0, 224), A("ROL", 0, 2)))
+        if t:
+            cover_b(t - 1)
+        ts(A("HA", 0, 14), A("HI", 0, 14), DA - 1, OP.bitwise_and)
+        ts(A("HQ", 0, 14), A("HI", 16, 30), 4095, OP.bitwise_and)
+        cp(A("AL", 0, 14), A("HA", 0, 14))
+        act(A("DZ"), IND(A("AC", 0, DA), A("AL", 0, 14)), AF.Identity)
+        mm(A("PM", 0, 224), A("IDB"), A("XV"), True, False)
+        mm(A("PM", 0, 224), A("NIDB"), A("DZ"), False, True)
+        act(A("Z"), A("PM", 0, 224), AF.Abs)
+        for h in range(2):
+            for hl in range(2):
+                mm(A("PM", 224, 448), lw(h, hl, h), A("Z"), h + hl == 0, h + hl == 2)
+        ts(A("QL", 0, 14), A("HQ", 0, 14), b / 4096.0, OP.mult, FLOOR, OP.add)
+        if na > 512:
+            hold_ag(b, 512, na, "PD1")
+        hold_max(blocks[0][0], blocks[0][1], "PH0")
+        if t:
+            cp(A("POF"), IND(A("TOP", 0, 224), A("ROL", 0, 16)))
+            cover_c(t - 1)
+            cover_d(t - 1)
+        else:
+            ts(A("PV"), IND(A("PTH", 0, B0), A("LF0", 0, 14)), float(O), OP.add)
+            path_mm()
+        hold_max(0, 512, "PD0")
+        cp(A("ZI"), A("PM", 224, 448))
+        if na > 512:
+            hold_as(512, na, "PD1")
+        if t:
+            hold_gather(b, old, b)
+            hold_sum(old, b, "PH1", "CS1")
+        ts(A("ZJ"), A("ZI"), 4095, OP.bitwise_and)
+        for blk in blocks[1:]:
+            hold_gather(b, *blk)
+            hold_sum(blk[0], blk[1], "PH0", "CS1")
+        ts(A("COF"), A("ZJ"), b / 4096.0, OP.mult, O + FLOOR, OP.add)
+
+        def gat(hf):
+            for c in range(112 * hf, 112 * hf + 112, 28):
+                if c >= S - 28 * VEC_GAT[t]:
+                    cp(A("XK", 16 * c, 16 * c + 448), IND(XB, A("COF", c, c + 28)))
+                else:
+                    act(A("XK", 16 * c, 16 * c + 448), IND(XB, A("COF", c, c + 28)), AF.Identity)
+
+        def dif(u):
+            hf, qd = u >> 2, u & 3
+            for j in range(4):
+                o = A("PD%d" % (u & 1), 112 * j, 112 * j + 112)
+                mm(o, A("IDB"), half("Z", hf), True, False)
+                mm(o, A("NIDB"), A("XK", 1792 * hf + 4 * qd + j, 1792 * hf + 1792, 16), False, True)
+
+        def sgn(u):
+            if (u & 3) >= 4 - VEC_SGN[t]:
+                ts(A("SG", 448 * u, 448 * u + 448), A("PD%d" % (u & 1), 0, 448), 0.0, OP.is_ge, 2.0, OP.mult)
+            else:
+                act(A("SG", 448 * u, 448 * u + 448), A("PD%d" % (u & 1), 0, 448), AF.Sign, bias=kb(0))
+
+        def cntm(u):
+            for j in range(4):
+                m = 4 * (u & 3) + j
+                mm(half("PC", u >> 2), A("SELB", 15 - m, 143 - m), A("SG", 448 * u + 112 * j, 448 * u + 112 * j + 112),
+                   m == 0, m == 15)
+
+        gat(0)
+        for blk in blocks[1:]:
+            hold_max(blk[0], blk[1], "PH0")
+        if t == 0:
+            tr(A("TOP"), PXA)
+            cp(A("POF"), IND(A("TOP", 0, 224), A("ROL", 0, 16)))
+        if na > 512:
+            hold_max(512, na, "PD1")
+        if t:
+            hold_max(old, b, "PH1")
+        ts(A("CI"), A("ZJ"), b / 4096.0, OP.mult, O + FLOOR, OP.add)
+        if ON_ACT[0]:
+            act(A("CE"), IND(A("R%d" % t, 0, b), A("QL", 0, 14)), AF.Identity, bias=CADD, scale=-1.0)
+        else:
+            ts(A("CE"), IND(A("R%d" % t, 0, b), A("QL", 0, 14)), -1.0, OP.mult, CADD, OP.add)
+        XPB = A("XP", 0, O + b)
+        gat(1)
+        act(A("EM"), A("CE"), AF.Relu, bias=kb(2), scale=-1.0)
+        act(A("E"), A("CE"), AF.Identity, bias=kb(1), scale=-1.0)
+        npa = ACT_PATH[t]
+        for k in range(16 - npa, 16):
+            j = k - 16 + npa
+            act(A("XG", S * j, S * j + S), IND(XPB, A("POF", 16 * k, 16 * k + 14)), AF.Identity)
+            o = A("PD%d" % (j >> 1 & 1), S * (j & 1), S * (j & 1) + S)
+            mm(o, A("IDB"), A("XG", S * j, S * j + S), True, False)
+            mm(o, A("NIDB"), A("E"), False, True)
+            if j & 1 or k == 15:
+                w = S * (j & 1)
+                act(A("PO", S * k - w, S * k + S), A(o[1], 0, w + S), AF.Identity, bias=CADD)
+        for k in range(16):
+            if k < 16 - npa:
+                tt(A("PO", S * k, S * k + S), IND(XPB, A("POF", 16 * k, 16 * k + 14)), A("CE"), OP.add)
+            mm(A("PP", 0, 224), A("SELB", 15 - k, 143 - k), A("PO", S * k, S * k + S), k == 0, k == 15)
+            if k == 8:
+                dif(0)
+                dif(1)
+                sgn(0)
+                sgn(1)
+            if k == 13:
+                dif(2)
+                sgn(2)
+        if ON_ACT[1]:
+            act(A("LOW"), A("PP", 0, 224), AF.Relu, bias=4096.0 + 15.0, scale=-1.0 / 512)
+            act(A("HLD"), A("PP", 0, 224), AF.Relu, bias=-1.0, scale=1.0 / 8388608)
+        else:
+            ts(A("LOW"), A("PP", 0, 224), 2097152.0 + 7.5 * 1024, OP.is_lt)
+            ts(A("HLD"), A("PP", 0, 224), 8388608.0, OP.is_ge)
+        dif(3)
+        sgn(3)
+        cntm(0)
+        mm(A("PP", 224, 448), A("BLKN"), A("EM"), True, False)
+        mm(A("PP", 224, 448), A("TRI"), A("LOW"), False, False)
+        mm(A("PP", 224, 448), A("BLKN"), A("HLD"), False, True)
+        mm(A("PM", 0, 224), A("BLKP"), A("HLD"))
+        mm(A("PM", 224, 448), A("NIDB"), A("Z"), True, False)
+        mm(A("PM", 224, 448), A("BLKN"), A("HLD"), False, True)
+        if ON_ACT[2]:
+            act(A("PP", 224, 448), A("PP", 224, 448), AF.Relu)
+            tt(A("SH"), A("PP", 224, 448), A("PV"), OP.min)
+        else:
+            tt(A("SE"), A("PP", 224, 448), A("PV"), OP.min)
+            ts(A("SH"), A("SE"), 0.0, OP.max)
+        act(A("ZT"), A("PM", 224, 448), AF.Relu, bias=kb(6))
+        act(A("JNK"), A("PM", 0, 224), AF.Sign, bias=kb(0), scale=-1.0, accum=A("ACC", 0, 1))
+        act(A("X", O + b, O + b + S), A("ZT"), AF.Identity, bias=kb(6), scale=-1.0)
+        if not last:
+            push(t + 1, b, b + S)
+        else:
+            dma("s", T.yx[:, b:W], A("X", O + b, O + W))
+        dif(4)
+        sgn(4)
+        mm(ph0(224), A("IDB"), A("MASKD"), True, False)
+        for h in range(2):
+            for rho in range(2):
+                mm(px(h), M("XO", ALL, h, slice(16 - 16 * rho, 144 - 16 * rho)), half("SH", rho), rho == 0, rho == 1)
+        for rho in range(2):
+            mm(M("PH0", ALL, slice(0, 7), rho, ALL), A("BLKH"), half("SH", rho), False, rho == 1)
+        tr(A("TGX"), PXA)
+        tt(A("EQ"), ph0(224), A("TGX"), OP.not_equal)
+        cp(A("TGU"), IND(A("TGX", 0, 224), A("ROL", 0, 1)))
+        dif(5)
+        sgn(5)
+        tt(A("V"), IND(XB, A("TGU", 0, 14)), A("E"), OP.max)
+        ts(A("PAR", 0, 1), A("ACC", 0, 1), -0.5, OP.mult, 112.0, OP.add)
+        dif(6)
+        sgn(6)
+        dif(7)
+        sgn(7)
+        mm(A("PP", 0, 14), A("IDH"), A("NEWL", 14 * t, 14 * t + 14), True, False)
+        sel_list(A("PP", 0, 14), "SELN", "HLD", False, True)
+        mm(A("PH1", 0, 224), A("E0"), A("NEWN", S * t, S * t + S), True, False)
+        mm(A("PH1", 0, 224), A("SHF"), A("PV"), False, False)
+        mm(A("PH1", 0, 224), A("BLKN"), A("HLD"), False, True)
+        if not last:
+            mm(A("PH1", 224, 448), A("NI2"), A("ONES", 0, 224), True, False)
+            mm(A("PH1", 224, 448), A("IDH"), A("PV"), False, False)
+            mm(A("PH1", 224, 448), A("NI2"), A("JNK"), False, True)
+        for u in range(1, 8):
+            cntm(u)
+        ts(A("PAR", 1, 2), A("PAR", 0, 1), 1, OP.bitwise_and)
+        scan(A("SC"), A("RST"), A("EQ"), 1.0, OP.max, OP.min)
+        ts(A("BIA", 0, 1), A("PAR", 1, 2), -2.0, OP.mult, col(12 + t), OP.add)
+        tt(A("OFF", 0, 14), A("SC", 15, 224, 16), A("TGX", 0, 224, 16), OP.mult)
+        tt(A("LF", 0, 14), A("PP", 0, 14), A("LF", 0, 14), OP.max)
+        ts(A("OFU", 0, 28, 2), A("OFF", 0, 14), col(6), OP.max)
+        if not last:
+            act(A("PVT"), A("PH1", 224, 448), AF.Relu)
+        act(A("YP", S * t, S * t + S), A("PH1", 0, 224), AF.Relu, bias=kb(3))
+        cover_a(t)
+        if not last:
+            cp(A("LFU", 0, 14), A("LF", 0, 14))
+        else:
+            ts(A("YV", 0, 14), A("LF", 0, 14), -float(O), OP.add)
+        for bb in range(13, -1, -1):
+            j = 4 * (bb % 7) + 2 * (bb // 7)
+            cp(IND(XB, A("OFU", j, j + 1)), A("V", 16 * bb, 16 * bb + 16))
+        if not last:
+            dma("s", A("X2", ACT_HOLD[t + 1], b + S), A("X", O + ACT_HOLD[t + 1], O + b + S))
+            push(t + 1, 0, b)
+            tt(A("PV"), A("PH1", 0, 224), A("PVT"), OP.max)
+        else:
+            dma("s", T.yx[:, 0:b // 2], A("X", O, O + b // 2))
+            dma("a", T.yx[:, b // 2:b], A("X", O + b // 2, O + b))
+            dma("s", T.yv[:], A("YV", 0, 14))
+            cover_b(t)
+            cover_d(t)
+        dma("s", T.yp[:, S * t:S * t + S], A("YP", S * t, S * t + S))
+    dma("s", T.yc[:], A("YC", rows=(0, 8)))
+    emit()

@@ -6,17 +6,19 @@ AF = ActivationFunctionType
 B0, S, RO, DA = 1152, 224, 3, 512
 JUMPS = [1, 5, 3]
 W = B0 + RO * S
-O = 32
+O = 48
 XW = O + W
 CADD = 131072.0 + 512.5
 FLOOR = -0.49609375
 SAMEW = True
-ACT_HOLD = [512, 1024, 1024]
+ACT_HOLD = [512, 768, 896]
 ACT_PATH = [0, 0, 0]
 VEC_SGN = [0, 0, 0]
 VEC_GAT = [0, 0, 0]
-ON_ACT = [1, 0, 0]
-LINK = 100.0
+ON_ACT = [0, 0, 0]
+LINK = 70.0
+CUT = [224, 288]
+VIA = [(2, 1, B0, B0 + S), (3, 1, 0, CUT[0]), (5, 2, B0 + S, B0 + 2 * S), (6, 2, 0, CUT[1])]
 
 BF, F32, F16, I32, U16 = "bfloat16", "float32", "float16", "int32", "uint16"
 SB = {
@@ -32,16 +34,16 @@ SB = {
     "CS2": ([128, 128], BF), "ONES": ([128, 512], BF), "TRI": ([128, 128], BF), "IDB": ([128, 128], BF),
     "NIDB": ([128, 128], BF), "NI2": ([128, 128], BF), "E0": ([128, 128], F16), "IDH": ([128, 128], F16),
     "SHF": ([128, 128], F16), "XH": ([128, 2, 144], F16),
-    "NEWN": ([128, 672], F16), "NEWL": ([128, 48], F16), "MASKD": ([128, 224], BF), "RST": ([128, 224], BF),
-    "XO": ([128, 2, 144], F16), "BLKH": ([128, 128], F16), "TGX": ([128, 224], F32), "XG": ([128, 1792], BF), "G8": ([128, 8], F16),
+    "NEWN": ([128, 672], F16), "NEWL": ([128, 48], F16), "MASKD": ([128, 224], BF), "RST": ([128, 336], BF),
+    "XO": ([128, 2, 144], F16), "BLKH": ([128, 128], F16), "TGX": ([128, 7, 2, 16], F32), "XG": ([128, 1792], BF), "G8": ([128, 8], F16),
     "XV": ([128, 224], BF), "PV": ([128, 224], F16), "PVT": ([128, 224], F32), "TOH": ([128, 224], F32),
     "TOP": ([128, 224], F32), "HI": ([128, 32], I32), "HA": ([128, 16], I32), "HQ": ([128, 16], I32),
     "AL": ([128, 16], U16), "QL": ([128, 16], U16), "POF": ([128, 256], U16), "DZ": ([128, 224], BF), "Z": ([128, 224], BF),
-    "ZT": ([128, 224], BF), "ZI": ([128, 224], I32), "ZJ": ([128, 224], I32), "COF": ([128, 224], U16), "CI": ([128, 224], I32),
+    "ZT": ([128, 224], BF), "ZI": ([128, 224], I32), "ZJ": ([128, 224], I32), "COF": ([128, 224], U16), "CI": ([128, 224], F16),
     "CMP": ([128, W - S], BF), "XC": ([128, 1024], BF), "CE": ([128, 224], F32), "E": ([128, 224], BF), "EM": ([128, 224], BF),
     "PO": ([128, 3584], BF), "XK": ([128, 3584], BF), "SG": ([128, 3584], BF), "LOW": ([128, 224], BF), "HLD": ([128, 224], BF),
-    "SE": ([128, 224], F32), "SH": ([128, 224], F16), "FIT": ([128, 224], BF), "SH2": ([128, 224], F16),
-    "TGH": ([128, 16], F16), "TGU": ([128, 16], U16), "EQ": ([128, 224], BF), "SC": ([128, 224], BF), "OFF": ([128, 16], F32),
+    "SE": ([128, 224], F32), "SH": ([128, 7, 2, 16], F16), "FIT": ([128, 224], BF), "SH2": ([128, 224], F16),
+    "TGH": ([128, 16], F16), "TGU": ([128, 16], U16), "EQ": ([128, 336], BF), "SC": ([128, 336], BF), "OFF": ([128, 24], F32),
     "OFU": ([128, 32], U16), "V": ([128, 224], BF), "JNK": ([128, 224], BF), "ACC": ([128, 8], F32), "PAR": ([128, 8], I32),
     "BIA": ([128, 8], F32), "YP": ([128, 672], F32), "YC": ([128, 672], F32), "YV": ([128, 16], F32), "KB": ([128, 8], F32),
 }
@@ -51,19 +53,45 @@ for _n in ("PH1", "PD0", "PD1", "PC", "PP", "PM"):
 SCRATCH["PH0"] = ("psum", [128, 16, 2, 16], F32)
 SCRATCH["PX"] = ("psum", [128, 16, 2, 16], F32)
 NDMA = 32
-SEMAPHORES = (["cv", "ca", "cp", "cg"] + ["arr%d" % i for i in range(6)] + ["snt%d" % i for i in range(6)]
+SEMAPHORES = (["cv", "ca", "cp", "cg"] + ["arr%d" % i for i in range(8)] + ["snt%d" % i for i in range(8)]
               + ["d%d" % i for i in range(NDMA)])
 BIG = 1 << 30
 PLAN = {}
-SLACKS, SHAKE, TURNS = (0.0, 100.0, 250.0), (600.0, 2000.0, 1200.0, 5000.0), 2500
-CYC, PE, FIX, WAKE = 1.04, 0.52, 60.0, 60.0
+CASES = [(dict(zip("vapgsr", f)), w) for f, w in (((0.82, 0.82, 0.9, 1, 1, 1), 120.0), ((1, 1.08, 1.5, 1, 1, 0.85), 60.0),
+                                                  ((1.05, 0.95, 0.8, 1, 1, 1.3), 90.0), ((1, 1, 1, 1, 1, 1.05), 70.0))]
+SWAPS, HEAT = 9000, 600.0
+SLACKS, SHAKE, TURNS = ((0.0, 0.0), (130.0, 0.0), (300.0, 0.0), (130.0, 130.0), (300.0, 130.0), (300.0, 60.0)), (700.0, 600.0, 2000.0, 1200.0, 5000.0), 300
+CYC, PE, FIX, WAKE = 1.04, 0.52, 60.0, 80.0
+
+
+def helper(T, topo, rank):
+    core, n = T.cores[rank], len(T.cores)
+    return [c for c in topo.cores_of(core) if topo.die(c) != topo.die(core) and T.rank_of(c) is None
+            and all(topo.may_write(c, T.cores[(rank - j) % n]) for j in JUMPS)][0]
+
+
+def hand_on(g, core, T, topo, rank):
+    n = len(T.cores)
+    for i, t, lo, hi in VIA:
+        dst = T.cores[(rank - JUMPS[t]) % n]
+        src = T.cores[rank]
+        k = len([e for e in topo.engines(src, core) if e not in topo.engines(src, dst)])
+        rid, pid, _ = topo.addr(dst)
+        g.wait_ge(T.sem["arr%d" % i], k)
+        g.remote_dma(T["R%d" % t][:, lo:hi], T["R%d" % t][:, lo:hi], T.sem["arr%d" % i], T.sem["snt%d" % i], pid, rid,
+                     topo.mask(core, dst))
+    for i, t, lo, hi in VIA:
+        g.wait_ge(T.sem["snt%d" % i], len(topo.engines(core, T.cores[(rank - JUMPS[t]) % n])))
 
 
 def rank_program(g, core, T, topo):
     rank = T.rank_of(core)
-    if rank is None:
-        return
     n = len(T.cores)
+    if rank is None:
+        for r in range(n):
+            if helper(T, topo, r) == core:
+                hand_on(g, core, T, topo, r)
+        return
     Q = {"v": g.vector, "a": g.scalar, "p": g.tensor, "g": g, "s": g.sync}
     ops = []
     total = {}
@@ -155,7 +183,7 @@ def rank_program(g, core, T, topo):
         o = (outs + ins)[0]
         sem = "d%d" % nd[0]
         nd[0] += 1
-        by = size(o) * 128 * (2 if SCRATCH[o[1]][2] == BF else 4)
+        by = size(o) * int(o[0].shape[0]) * (2 if SCRATCH[o[1]][2] == BF else 4)
         return add(q, outs, ins, lambda: Q[q].dma_start(ap(out), ap(in_)).then_inc(T.sem[sem], 16), 100,
                    2000 + by / 150.0 + (len(ops) * 150 if after is not None else 0), sem, 16, after)
 
@@ -184,7 +212,7 @@ def rank_program(g, core, T, topo):
                         if best is None or t0 < best[0]:
                             best = (t0, q)
                 t0, q = best
-                i = min([i for i in ready[q] if can[i] <= t0 + slack], key=lambda i: prio[i])
+                i = min([i for i in ready[q] if can[i] <= t0 + slack[q == "v"]], key=lambda i: prio[i])
                 o = ops[i]
                 ready[q].remove(i)
                 t0 = max(free[q], can[i])
@@ -203,6 +231,37 @@ def rank_program(g, core, T, topo):
                         ready[ops[k]["q"]].append(k)
             return seq, at, end
 
+        def replay(seq, f, wake, trace=False):
+            free, done, go, end = {q: 0.0 for q in f}, [0.0] * m, [0.0] * m, 0.0
+            why, prev, top = [None] * m, {}, 0
+            for i in seq:
+                q, pre, busy, lat, isd = flat[i]
+                t0 = free[q]
+                w = prev.get(q)
+                for j, wait in pre:
+                    d = done[j] + wake if wait else go[j]
+                    if d > t0:
+                        t0, w = d, j
+                why[i] = w
+                prev[q] = i
+                if isd:
+                    go[i] = free[q] = t0 + busy
+                    d = done[i] = t0 + lat * (f["r"] if q != "s" else 1)
+                else:
+                    d = go[i] = free[q] = done[i] = t0 + busy * f[q]
+                if d > end:
+                    end, top = d, i
+            if not trace:
+                return end
+            path = []
+            while why[top] is not None:
+                if why[top] not in ops[top]["pre"]:
+                    path.append((why[top], top))
+                top = why[top]
+            return path
+
+        flat = [(o["q"], list(o["pre"].items()), o["busy"], o["lat"], o["dma"]) for o in ops]
+
         if m not in PLAN:
             good = None
             rnd = np.random.default_rng(7)
@@ -214,14 +273,41 @@ def rank_program(g, core, T, topo):
                     t1 = rnd.random() * good[0]
                     w = (rnd.random(m) - 0.5) * SHAKE[turn % len(SHAKE)] * (rnd.random(m) < 0.3)
                     prio = [x + (y if t1 - 4000 < z < t1 + 4000 else 0) for x, y, z in zip(good[3], w.tolist(), good[2])]
-                    slack = good[4] if turn % 8 else slack
+                    slack = good[4] if turn % 7 else slack
                 for k in range(6 if turn < len(SLACKS) else 2 if turn % 5 == 0 else 1):
                     if k:
                         prio = [-x for x in plan([-x for x in at], True, slack)[1]]
                     seq, at, end = plan(prio, False, slack)
+                    if good is not None and end > 1.06 * good[0]:
+                        continue
+                    end = (end + sum(replay(seq, *c) for c in CASES)) / (1 + len(CASES))
                     if good is None or end <= good[0]:
                         good = (end, seq, at, prio if k or turn >= len(SLACKS) else at, slack)
-            PLAN[m] = good
+            best = now = (sum(replay(good[1], *c) for c in CASES), good[1])
+            for turn in range(SWAPS):
+                seq = now[1]
+                path = replay(seq, *CASES[turn % len(CASES)], True)
+                if not path:
+                    continue
+                i, j = path[int(rnd.integers(len(path)))]
+                a, b = seq.index(i), seq.index(j)
+                for _ in range(int(rnd.integers(3))):
+                    e = [x for x in range(a - 1, max(a - 40, -1), -1) if ops[seq[x]]["q"] == ops[j]["q"]]
+                    a = e[0] if e else a
+                lift = {j}
+                for x in range(b - 1, a - 1, -1):
+                    if any(k in lift for k in nxt[seq[x]]):
+                        lift.add(seq[x])
+                if seq[a] in lift:
+                    continue
+                mid = seq[a:b + 1]
+                new = seq[:a] + [x for x in mid if x in lift] + [x for x in mid if x not in lift] + seq[b + 1:]
+                end = sum(replay(new, *c) for c in CASES)
+                if end <= now[0] + HEAT * (1 - turn / SWAPS) * rnd.random():
+                    now = (end, new)
+                    if end < best[0]:
+                        best = now
+            PLAN[m] = (best[0] / len(CASES), best[1])
         val = [0] * m
         for i in PLAN[m][1]:
             o = ops[i]
@@ -301,6 +387,20 @@ def rank_program(g, core, T, topo):
         k2 = len(topo.engines(T.cores[(rank + JUMPS[t]) % n], core))
         add("r", [A("R%d" % t, lo, hi)], [], None, 0, lat - 300, arr, k2, after=me)
 
+    def push_via(t, lo, hi):
+        mate = helper(T, topo, rank)
+        rid, pid, _ = topo.addr(mate)
+        dst = T.cores[(rank - JUMPS[t]) % n]
+        eng = [e for e in topo.engines(core, mate) if e not in topo.engines(core, dst)]
+        src = A("X", O + lo, O + hi)
+        arr, snt = "arr%d" % nd[1], "snt%d" % nd[1]
+        nd[1] += 1
+        lat = 2200 + (hi - lo) * 256 / LINK
+        me = add("g", [], [src], lambda: g.remote_dma(T["R%d" % t][:, lo:hi], src[0], T.sem[arr], T.sem[snt], pid, rid,
+                                                     sum(1 << e for e in eng)), 300, lat, snt, len(eng))
+        k2 = len(topo.engines(helper(T, topo, (rank + JUMPS[t]) % n), core))
+        add("r", [A("R%d" % t, lo, hi)], [], None, 0, 2 * lat - 300, arr, k2, after=me)
+
     def col(j):
         return A("COL", j, j + 1)
 
@@ -315,7 +415,7 @@ def rank_program(g, core, T, topo):
         c = dma("as"[gi // 6], A("COVI", 16 * gi, 16 * gi + 16, rows=(0, 72)), T.cov[gi], d if gi >= 6 else None)
         if gi >= 6:
             d = c
-    d = dma("s", A("X2", ACT_HOLD[0], B0), T.lab[:, ACT_HOLD[0]:B0], d)
+    cp(A("X2", ACT_HOLD[0], B0), A("X", O + ACT_HOLD[0], O + B0))
     d = dma("s", A("AC"), T.act[:], d)
     d = dma("s", A("PTH"), T.pth[:], d)
 
@@ -350,7 +450,7 @@ def rank_program(g, core, T, topo):
         ts(M("WM", ALL, slice(2 * h, 2 * h + 2), ALL), A("WH"), col(3 - h), OP.mult)
     for p in range(4):
         r = slice(32 * p, 32 * p + 32)
-        act(M("LW", r, ALL, slice(32 * p + 16, 32 * p + 32)), M("WM", r, ALL, ALL), AF.Identity)
+        act((T.LW[r, :, 32 * p + 16:32 * p + 32], "LW", p, p + 1), M("WM", r, ALL, ALL), AF.Identity)
     ts(A("COVH", rows=(0, 72)), A("COVI", rows=(0, 72)), float(O), OP.add)
     mm(A("PM", 0, 72), A("COVH", rows=(0, 72)), A("IDH", 0, 72, rows=(0, 72)))
     cp(A("COVL", 0, 72), A("PM", 0, 72))
@@ -362,6 +462,7 @@ def rank_program(g, core, T, topo):
     act(A("XP", 0, O), A("ONES", 0, O), AF.Identity)
     ts(A("LF", 0, 14), A("LFI", 0, 14), float(O), OP.add)
     ts(col(6), col(0), 1.0, OP.add)
+    ts(col(15), col(0), 17.0, OP.add)
     ts(col(8), col(0), -4096.0, OP.mult, 4096.0, OP.add)
     ts(A("NEWL", 0, 42), A("IJ", 0, 42), col(0), OP.add, float(O + B0), OP.add)
     act(A("BLKN"), A("BLK1"), AF.Identity, scale=-131072.0)
@@ -386,7 +487,7 @@ def rank_program(g, core, T, topo):
             continue
         ts(col(7), col(0), 16.0 - 4 * VEC_SGN[t], OP.is_ge, -16.0, OP.mult)
         ts(A("COL", 12 + t, 15), A("ONES", 0, 3 - t), -7.0, OP.mult, col(7), OP.add)
-    asel(A("RST"), A("ONES", 0, 224), [[0, 14], [1, 16]], OP.is_equal, 0.0, 0, 0)
+    asel(A("RST"), A("ONES", 0, 336), [[0, 21], [1, 16]], OP.is_equal, 0.0, 0, 0)
     asel(A("SHF"), A("BLK1"), [[1, 128]], OP.is_equal, 0.0, -1, -1)
     asel(A("E0"), A("IDB"), [[0, 8], [1, 16]], OP.is_equal, 0.0, 0, 0)
     asel(A("NEWN"), A("IS"), [[1, 672]], OP.is_ge, 0.0, 0, 0)
@@ -449,12 +550,11 @@ def rank_program(g, core, T, topo):
         mm(A("PC", 0, 224, rows=(0, 8)), A("G8"), A("SH2"))
 
     def cover_c(t):
-        cp(A("COVL", 72 + 14 * t, 86 + 14 * t), A("PC", 448, 462))
+        ts(A("COVL", 72 + 14 * t, 86 + 14 * t), A("PC", 448, 462), O - 1.0, OP.add)
 
     def cover_d(t):
         y = A("YC", S * t, S * t + S, rows=(0, 8))
-        act(y, A("PC", 0, 224, rows=(0, 8)), AF.Relu, bias=kb(4))
-        act(y, y, AF.Identity, bias=kb(5))
+        act(y, A("PC", 0, 224, rows=(0, 8)), AF.Identity, bias=-1.0)
 
     for t in range(RO):
         b = B0 + t * S
@@ -548,7 +648,7 @@ def rank_program(g, core, T, topo):
             hold_max(512, na, "PD1")
         if t:
             hold_max(old, b, "PH1")
-        ts(A("CI"), A("ZJ"), b / 4096.0, OP.mult, O + FLOOR, OP.add)
+        ts(A("CI"), A("COF"), 1.0 - O, OP.add)
         if ON_ACT[0]:
             act(A("CE"), IND(A("R%d" % t, 0, b), A("QL", 0, 14)), AF.Identity, bias=CADD, scale=-1.0)
         else:
@@ -604,7 +704,8 @@ def rank_program(g, core, T, topo):
         act(A("JNK"), A("PM", 0, 224), AF.Sign, bias=kb(0), scale=-1.0, accum=A("ACC", 0, 1))
         act(A("X", O + b, O + b + S), A("ZT"), AF.Identity, bias=kb(6), scale=-1.0)
         if not last:
-            push(t + 1, b, b + S)
+            push_via(t + 1, b, b + S)
+            dma("s", A("X2", b, b + S), A("X", O + b, O + b + S))
         else:
             dma("s", T.yx[:, b:W], A("X", O + b, O + W))
         dif(4)
@@ -612,12 +713,13 @@ def rank_program(g, core, T, topo):
         mm(ph0(224), A("IDB"), A("MASKD"), True, False)
         for h in range(2):
             for rho in range(2):
-                mm(px(h), M("XO", ALL, h, slice(16 - 16 * rho, 144 - 16 * rho)), half("SH", rho), rho == 0, rho == 1)
-        for rho in range(2):
-            mm(M("PH0", ALL, slice(0, 7), rho, ALL), A("BLKH"), half("SH", rho), False, rho == 1)
+                mm(px(h), M("XO", ALL, h, slice(16 - 16 * rho, 144 - 16 * rho)), M("SH", ALL, ALL, rho, ALL), rho == 0, rho == 1)
+        mm(ph0(224), A("BLKH"), A("SH"), False, True)
+        mm(M("PH0", ALL, slice(7, 14), 0, ALL), A("BLKH"), M("SH", ALL, ALL, 0, ALL))
         tr(A("TGX"), PXA)
-        tt(A("EQ"), ph0(224), A("TGX"), OP.not_equal)
-        cp(A("TGU"), IND(A("TGX", 0, 224), A("ROL", 0, 1)))
+        tt(A("EQ", 0, 224), ph0(224), A("TGX"), OP.not_equal)
+        tt(A("EQ", 224, 336), M("PH0", ALL, slice(7, 14), 0, ALL), M("TGX", ALL, ALL, 1, ALL), OP.not_equal)
+        cp(A("TGU", 0, 14), M("TGX", ALL, ALL, ALL, 0))
         dif(5)
         sgn(5)
         tt(A("V"), IND(XB, A("TGU", 0, 14)), A("E"), OP.max)
@@ -640,9 +742,13 @@ def rank_program(g, core, T, topo):
         ts(A("PAR", 1, 2), A("PAR", 0, 1), 1, OP.bitwise_and)
         scan(A("SC"), A("RST"), A("EQ"), 1.0, OP.max, OP.min)
         ts(A("BIA", 0, 1), A("PAR", 1, 2), -2.0, OP.mult, col(12 + t), OP.add)
-        tt(A("OFF", 0, 14), A("SC", 15, 224, 16), A("TGX", 0, 224, 16), OP.mult)
+        tt(A("OFF", 16, 23), A("SC", 239, 336, 16), M("TGX", ALL, ALL, 1, 0), OP.mult)
+        tt(A("OFF", 0, 7), A("SC", 15, 224, 32), M("TGX", ALL, ALL, 0, 0), OP.mult)
+        tt(A("OFF", 8, 15), A("SC", 31, 224, 32), A("OFF", 16, 23), OP.mult)
         tt(A("LF", 0, 14), A("PP", 0, 14), A("LF", 0, 14), OP.max)
-        ts(A("OFU", 0, 28, 2), A("OFF", 0, 14), col(6), OP.max)
+        for rho in range(2):
+            ts((T.OFU[:, rho:14:2], "OFU", 0, 14) if rho else (T.OFU[:, 0:14:2], "OFU", 14, 15), A("OFF", 8 * rho, 8 * rho + 7),
+               col(6 + 9 * rho), OP.max)
         if not last:
             act(A("PVT"), A("PH1", 224, 448), AF.Relu)
         act(A("YP", S * t, S * t + S), A("PH1", 0, 224), AF.Relu, bias=kb(3))
@@ -651,12 +757,13 @@ def rank_program(g, core, T, topo):
             cp(A("LFU", 0, 14), A("LF", 0, 14))
         else:
             ts(A("YV", 0, 14), A("LF", 0, 14), -float(O), OP.add)
-        for bb in range(13, -1, -1):
-            j = 4 * (bb % 7) + 2 * (bb // 7)
-            cp(IND(XB, A("OFU", j, j + 1)), A("V", 16 * bb, 16 * bb + 16))
+        for bb in range(12, -1, -2):
+            cp(IND(XB, (T.OFU[:, bb:bb + 2], "OFU", 0, 15, )[:4] + ()), A("V", 16 * bb, 16 * bb + 32))
         if not last:
-            dma("s", A("X2", ACT_HOLD[t + 1], b + S), A("X", O + ACT_HOLD[t + 1], O + b + S))
-            push(t + 1, 0, b)
+            if ACT_HOLD[t + 1] < b:
+                cp(A("X2", ACT_HOLD[t + 1], b), A("X", O + ACT_HOLD[t + 1], O + b))
+            push_via(t + 1, 0, CUT[t])
+            push(t + 1, CUT[t], b)
             tt(A("PV"), A("PH1", 0, 224), A("PVT"), OP.max)
         else:
             dma("s", T.yx[:, 0:b // 2], A("X", O, O + b // 2))

@@ -10,42 +10,44 @@ O = 48
 XW = O + W
 CADD = 131072.0 + 512.5
 FLOOR = -0.49609375
-SAMEW = True
-ACT_HOLD = [512, 768, 896]
-ACT_PATH = [0, 0, 0]
-VEC_SGN = [0, 0, 0]
+MAGIC = 1.5 * 2 ** 23
+ACT_HOLD = [512, 512, 512]
+VEC_CMP = [8, 8, 8]
 VEC_GAT = [0, 0, 0]
-ON_ACT = [0, 0, 0]
-LINK = 70.0
-CUT = [224, 288]
-VIA = [(2, 1, B0, B0 + S), (3, 1, 0, CUT[0]), (5, 2, B0 + S, B0 + 2 * S), (6, 2, 0, CUT[1])]
+ON_ACT = [(1, 0, 0), (1, 0, 0), (1, 0, 0)]
+LINK = 80.0
+WRITES = [(0, 0, 576, 0), (0, 576, B0, 0),
+          (1, B0, B0 + S, 1), (1, 0, 224, 1), (1, 448, B0, 0), (1, 224, 448, 1),
+          (2, B0 + S, B0 + 2 * S, 1), (2, 0, 288, 1), (2, 576, B0 + S, 0), (2, 288, 576, 1)]
 
 BF, F32, F16, I32, U16 = "bfloat16", "float32", "float16", "int32", "uint16"
 SB = {
-    "X": ([128, XW], BF), "X2": ([128, W - S], BF), "XP": ([128, O + W - S], BF), "R0": ([128, B0], BF), "R1": ([128, B0 + S], BF),
+    "X": ([128, XW], BF), "X2": ([128, B0], BF), "XP": ([128, O + W - S], BF), "R0": ([128, B0], BF), "R1": ([128, B0 + S], BF),
     "R2": ([128, B0 + 2 * S], BF), "AC": ([128, DA], BF), "PTH": ([128, B0], I32), "COVI": ([128, 128], I32),
-    "COVH": ([128, 128], F16), "COVL": ([128, 128], U16), "WI": ([128, 16], I32), "WH": ([128, 2, 16], BF),
-    "WM": ([128, 4, 16], BF), "LW": ([128, 4, 144], BF), "LFI": ([128, 16], I32), "LF0": ([128, 16], U16),
-    "LF": ([128, 16], F32), "LFU": ([128, 16], U16),
+    "COVH": ([128, 128], F16), "COVL": ([128, 128], U16), "WI": ([128, 16], I32), "WG": ([128, 16], F32),
+    "WS": ([128, 16], F32), "LW": ([128, 288], F16), "LFI": ([128, 16], I32), "LF0": ([128, 16], U16),
+    "LF": ([128, 16], F32), "LFU": ([128, 16], U16), "AOF": ([128, 18], U16),
     "IP": ([128, 8], I32), "COL": ([128, 16], F32), "IC": ([128, 144], F32), "IG": ([128, 144], F32),
     "IS": ([128, 672], F32), "IA": ([128, 224], F32), "IJ": ([128, 48], F32),
     "ROL": ([128, 16], U16), "SELB": ([128, 144], BF), "SELN": ([128, 144], BF), "SELH": ([128, 144], F16), "BLK1": ([128, 128], BF),
-    "BLKP": ([128, 128], BF), "BLKN": ([128, 128], BF), "BLKM": ([128, 128], BF), "CS1": ([128, 128], BF),
+    "PI2": ([128, 128], BF), "BLKM": ([128, 128], BF), "CS1": ([128, 128], BF),
     "CS2": ([128, 128], BF), "ONES": ([128, 512], BF), "TRI": ([128, 128], BF), "IDB": ([128, 128], BF),
     "NIDB": ([128, 128], BF), "NI2": ([128, 128], BF), "E0": ([128, 128], F16), "IDH": ([128, 128], F16),
-    "SHF": ([128, 128], F16), "XH": ([128, 2, 144], F16),
-    "NEWN": ([128, 672], F16), "NEWL": ([128, 48], F16), "MASKD": ([128, 224], BF), "RST": ([128, 336], BF),
-    "XO": ([128, 2, 144], F16), "BLKH": ([128, 128], F16), "TGX": ([128, 7, 2, 16], F32), "XG": ([128, 1792], BF), "G8": ([128, 8], F16),
-    "XV": ([128, 224], BF), "PV": ([128, 224], F16), "PVT": ([128, 224], F32), "TOH": ([128, 224], F32),
+    "SHF": ([128, 128], F16), "XH": ([128, 288], F16), "SEL2": ([128, 144], BF),
+    "HLD": ([128, 224], BF), "BLKT": ([128, 128], BF),
+    "NEWN": ([128, 672], F16), "NEWL": ([128, 48], F32), "MASKD": ([128, 224], BF),
+    "ZL": ([128, 672], BF), "NEWH": ([128, 48], F16),
+    "XO": ([128, 288], F16), "BLKH": ([128, 128], F16), "TGX": ([128, 7, 2, 16], F32), "G8": ([128, 8], F16),
+    "XV": ([128, 224], BF), "PV": ([128, 224], F16), "TOH": ([128, 224], F32),
     "TOP": ([128, 224], F32), "HI": ([128, 32], I32), "HA": ([128, 16], I32), "HQ": ([128, 16], I32),
-    "AL": ([128, 16], U16), "QL": ([128, 16], U16), "POF": ([128, 256], U16), "DZ": ([128, 224], BF), "Z": ([128, 224], BF),
-    "ZT": ([128, 224], BF), "ZI": ([128, 224], I32), "ZJ": ([128, 224], I32), "COF": ([128, 224], U16), "CI": ([128, 224], F16),
+    "AL": ([128, 16], U16), "QL": ([128, 16], U16), "POF": ([128, 256], U16), "DZ": ([128, 224], BF), "Z": ([128, 672], BF),
+    "ZI": ([128, 224], I32), "ZJ": ([128, 224], I32), "COF": ([128, 224], U16), "CI": ([128, 672], F16),
     "CMP": ([128, W - S], BF), "XC": ([128, 1024], BF), "CE": ([128, 224], F32), "E": ([128, 224], BF), "EM": ([128, 224], BF),
-    "PO": ([128, 3584], BF), "XK": ([128, 3584], BF), "SG": ([128, 3584], BF), "LOW": ([128, 224], BF), "HLD": ([128, 224], BF),
-    "SE": ([128, 224], F32), "SH": ([128, 7, 2, 16], F16), "FIT": ([128, 224], BF), "SH2": ([128, 224], F16),
-    "TGH": ([128, 16], F16), "TGU": ([128, 16], U16), "EQ": ([128, 336], BF), "SC": ([128, 336], BF), "OFF": ([128, 24], F32),
-    "OFU": ([128, 32], U16), "V": ([128, 224], BF), "JNK": ([128, 224], BF), "ACC": ([128, 8], F32), "PAR": ([128, 8], I32),
-    "BIA": ([128, 8], F32), "YP": ([128, 672], F32), "YC": ([128, 672], F32), "YV": ([128, 16], F32), "KB": ([128, 8], F32),
+    "PO": ([128, 3584], BF), "XK": ([128, 7168], BF), "SG": ([128, 3584], BF), "LOW": ([128, 224], BF), "SUS": ([128, 672], BF),
+    "SH": ([128, 7, 2, 16], F16), "FIT": ([128, 224], BF), "SH2": ([128, 224], F16),
+    "EQ": ([128, 336], BF), "SC": ([128, 336], BF), "RST": ([128, 336], BF), "OFF": ([128, 24], F32),
+    "OFU": ([128, 16], U16), "TGU": ([128, 16], U16), "V": ([128, 224], BF), "SGN": ([128, 672], BF),
+    "YP": ([128, 672], F32), "YC": ([128, 672], F32), "YV": ([128, 16], F32),
 }
 SCRATCH = {k: ("sbuf", v[0], v[1]) for k, v in SB.items()}
 for _n in ("PH1", "PD0", "PD1", "PC", "PP", "PM"):
@@ -53,15 +55,17 @@ for _n in ("PH1", "PD0", "PD1", "PC", "PP", "PM"):
 SCRATCH["PH0"] = ("psum", [128, 16, 2, 16], F32)
 SCRATCH["PX"] = ("psum", [128, 16, 2, 16], F32)
 NDMA = 32
-SEMAPHORES = (["cv", "ca", "cp", "cg"] + ["arr%d" % i for i in range(8)] + ["snt%d" % i for i in range(8)]
+SEMAPHORES = (["cv", "ca", "cp", "cg"] + ["arr%d" % i for i in range(len(WRITES))] + ["snt%d" % i for i in range(len(WRITES))]
               + ["d%d" % i for i in range(NDMA)])
 BIG = 1 << 30
 PLAN = {}
-CASES = [(dict(zip("vapgsr", f)), w) for f, w in (((0.82, 0.82, 0.9, 1, 1, 1), 120.0), ((1, 1.08, 1.5, 1, 1, 0.85), 60.0),
-                                                  ((1.05, 0.95, 0.8, 1, 1, 1.3), 90.0), ((1, 1, 1, 1, 1, 1.05), 70.0))]
-SWAPS, HEAT = 9000, 600.0
-SLACKS, SHAKE, TURNS = ((0.0, 0.0), (130.0, 0.0), (300.0, 0.0), (130.0, 130.0), (300.0, 130.0), (300.0, 60.0)), (700.0, 600.0, 2000.0, 1200.0, 5000.0), 300
-CYC, PE, FIX, WAKE = 1.04, 0.52, 60.0, 80.0
+CASES = [(dict(zip("vapgsr", f)), w) for f, w in (((0.85, 0.85, 0.9, 1, 1, 1), 200.0), ((1, 1.08, 1.4, 1, 1, 0.75), 80.0),
+                                                  ((1.1, 1.0, 0.8, 1, 1, 1.4), 120.0), ((1, 1, 1, 1, 1, 1.0), 140.0))]
+SWAPS, HEAT = 6000, 600.0
+TURNS = 150
+SLACKS, SHAKE = ((0.0, 0.0), (130.0, 0.0), (300.0, 0.0), (130.0, 130.0), (300.0, 130.0), (300.0, 60.0)), (700.0, 600.0, 2000.0, 1200.0, 5000.0)
+HOP, LOC, LOCR = 1500.0, 1400.0, 200.0
+CYC, PE, FIX, WAKE = 0.95, 0.58, 40.0, 130.0
 
 
 def helper(T, topo, rank):
@@ -72,6 +76,7 @@ def helper(T, topo, rank):
 
 def hand_on(g, core, T, topo, rank):
     n = len(T.cores)
+    VIA = [(i, t, lo, hi) for i, (t, lo, hi, via) in enumerate(WRITES) if via]
     for i, t, lo, hi in VIA:
         dst = T.cores[(rank - JUMPS[t]) % n]
         src = T.cores[rank]
@@ -82,6 +87,127 @@ def hand_on(g, core, T, topo, rank):
                      topo.mask(core, dst))
     for i, t, lo, hi in VIA:
         g.wait_ge(T.sem["snt%d" % i], len(topo.engines(core, T.cores[(rank - JUMPS[t]) % n])))
+
+
+def order(ops):
+    m = len(ops)
+    nxt = [[] for _ in ops]
+    for i, o in enumerate(ops):
+        for j in o["pre"]:
+            nxt[j].append(i)
+
+    def plan(prio, back, slack):
+        out = [list(o["pre"]) for o in ops] if back else nxt
+        left = [len(nxt[i]) if back else len(ops[i]["pre"]) for i in range(m)]
+        can = [ops[i]["lat"] - ops[i]["busy"] if back else 0.0 for i in range(m)]
+        ready = {q: [] for q in "vapgsr"}
+        free = {q: 0.0 for q in ready}
+        for i in range(m):
+            if not left[i]:
+                ready[ops[i]["q"]].append(i)
+        seq, at, end = [], [0.0] * m, 0.0
+        for _ in range(m):
+            best = None
+            for q, r in ready.items():
+                if r:
+                    t0 = max(free[q], min([can[i] for i in r]))
+                    if best is None or t0 < best[0]:
+                        best = (t0, q)
+            t0, q = best
+            i = min([i for i in ready[q] if can[i] <= t0 + slack[q == "v"]], key=lambda i: prio[i])
+            o = ops[i]
+            ready[q].remove(i)
+            t0 = max(free[q], can[i])
+            free[q] = t0 + o["busy"]
+            at[i] = free[q] if back else t0
+            end = max(end, t0 + o["lat"])
+            seq.append(i)
+            for k in out[i]:
+                if back:
+                    d = at[i] + (ops[k]["lat"] + WAKE - ops[k]["busy"] if o["pre"][k] else 0)
+                else:
+                    d = t0 + (o["lat"] + WAKE if ops[k]["pre"][i] else o["busy"])
+                can[k] = max(can[k], d)
+                left[k] -= 1
+                if not left[k]:
+                    ready[ops[k]["q"]].append(k)
+        return seq, at, end
+
+    def replay(seq, f, wake, trace=False):
+        free, done, go, end = {q: 0.0 for q in f}, [0.0] * m, [0.0] * m, 0.0
+        why, prev, top = [None] * m, {}, 0
+        for i in seq:
+            q, pre, busy, lat, isd = flat[i]
+            t0 = free[q]
+            w = prev.get(q)
+            for j, wait in pre:
+                d = done[j] + wake if wait else go[j]
+                if d > t0:
+                    t0, w = d, j
+            why[i] = w
+            prev[q] = i
+            if isd:
+                go[i] = free[q] = t0 + busy
+                d = done[i] = t0 + lat * (f["r"] if q != "s" else 1)
+            else:
+                d = go[i] = free[q] = done[i] = t0 + busy * f[q]
+            if d > end:
+                end, top = d, i
+        if not trace:
+            return end
+        path = []
+        while why[top] is not None:
+            if why[top] not in ops[top]["pre"]:
+                path.append((why[top], top))
+            top = why[top]
+        return path
+
+    flat = [(o["q"], list(o["pre"].items()), o["busy"], o["lat"], o["dma"]) for o in ops]
+    good = None
+    rnd = np.random.default_rng(7)
+    for turn in range(TURNS):
+        slack = SLACKS[turn % len(SLACKS)]
+        if turn < len(SLACKS):
+            prio = list(range(m))
+        else:
+            t1 = rnd.random() * good[0]
+            w = (rnd.random(m) - 0.5) * SHAKE[turn % len(SHAKE)] * (rnd.random(m) < 0.3)
+            prio = [x + (y if t1 - 4000 < z < t1 + 4000 else 0) for x, y, z in zip(good[3], w.tolist(), good[2])]
+            slack = good[4] if turn % 7 else slack
+        for k in range(6 if turn < len(SLACKS) else 2 if turn % 5 == 0 else 1):
+            if k:
+                prio = [-x for x in plan([-x for x in at], True, slack)[1]]
+            seq, at, end = plan(prio, False, slack)
+            if good is not None and end > 1.06 * good[0]:
+                continue
+            end = (end + sum(replay(seq, *c) for c in CASES)) / (1 + len(CASES))
+            if good is None or end <= good[0]:
+                good = (end, seq, at, prio if k or turn >= len(SLACKS) else at, slack)
+    best = now = (sum(replay(good[1], *c) for c in CASES), good[1])
+    for turn in range(SWAPS):
+        seq = now[1]
+        path = replay(seq, *CASES[turn % len(CASES)], True)
+        if not path:
+            continue
+        i, j = path[int(rnd.integers(len(path)))]
+        a, b = seq.index(i), seq.index(j)
+        for _ in range(int(rnd.integers(3))):
+            e = [x for x in range(a - 1, max(a - 40, -1), -1) if ops[seq[x]]["q"] == ops[j]["q"]]
+            a = e[0] if e else a
+        lift = {j}
+        for x in range(b - 1, a - 1, -1):
+            if any(k in lift for k in nxt[seq[x]]):
+                lift.add(seq[x])
+        if seq[a] in lift:
+            continue
+        mid = seq[a:b + 1]
+        new = seq[:a] + [x for x in mid if x in lift] + [x for x in mid if x not in lift] + seq[b + 1:]
+        end = sum(replay(new, *c) for c in CASES)
+        if end <= now[0] + HEAT * (1 - turn / SWAPS) * rnd.random():
+            now = (end, new)
+            if end < best[0]:
+                best = now
+    return best[0] / len(CASES), best[1]
 
 
 def rank_program(g, core, T, topo):
@@ -98,6 +224,9 @@ def rank_program(g, core, T, topo):
     seen = {q: {} for q in Q}
     hist = {}
     nd = [0, 0]
+    sent = [0, 0]
+    prev = [None]
+    pd = [0]
     ALL = slice(None)
 
     def A(name, lo=None, hi=None, step=None, rows=None):
@@ -130,7 +259,7 @@ def rank_program(g, core, T, topo):
     def cost(q, outs, ins, base):
         k = max(size(x) for x in outs + ins)
         if q == "p":
-            return max(64, size(outs[0])) * PE
+            return max(64, size(outs[0])) * PE * (4 if SCRATCH[ins[0][1]][2] == F32 else 1)
         if q == "g":
             return 170 + 2 * k * CYC
         if len(outs[0]) > 4:
@@ -158,7 +287,7 @@ def rank_program(g, core, T, topo):
                 if not (ps or (over and (w2 or wr))):
                     continue
                 if ops[j]["q"] == q and not dma and not ops[j]["dma"]:
-                    wait = q != "p" and over and w2 and (not wr or SAMEW)
+                    wait = q != "p" and over and (w2 or wr)
                 else:
                     wait = True
                 pre[j] = pre.get(j, False) or wait
@@ -184,130 +313,15 @@ def rank_program(g, core, T, topo):
         sem = "d%d" % nd[0]
         nd[0] += 1
         by = size(o) * int(o[0].shape[0]) * (2 if SCRATCH[o[1]][2] == BF else 4)
+        sent[0] = sent[1]
+        sent[1] += by
         return add(q, outs, ins, lambda: Q[q].dma_start(ap(out), ap(in_)).then_inc(T.sem[sem], 16), 100,
-                   2000 + by / 150.0 + (len(ops) * 150 if after is not None else 0), sem, 16, after)
+                   LOC + (by + (sent[0] if after is not None else 0)) / LOCR, sem, 16, after)
 
     def emit():
         m = len(ops)
-        nxt = [[] for _ in ops]
-        for i, o in enumerate(ops):
-            for j in o["pre"]:
-                nxt[j].append(i)
-
-        def plan(prio, back, slack):
-            out = [list(o["pre"]) for o in ops] if back else nxt
-            left = [len(nxt[i]) if back else len(ops[i]["pre"]) for i in range(m)]
-            can = [ops[i]["lat"] - ops[i]["busy"] if back else 0.0 for i in range(m)]
-            ready = {q: [] for q in "vapgsr"}
-            free = {q: 0.0 for q in ready}
-            for i in range(m):
-                if not left[i]:
-                    ready[ops[i]["q"]].append(i)
-            seq, at, end = [], [0.0] * m, 0.0
-            for _ in range(m):
-                best = None
-                for q, r in ready.items():
-                    if r:
-                        t0 = max(free[q], min([can[i] for i in r]))
-                        if best is None or t0 < best[0]:
-                            best = (t0, q)
-                t0, q = best
-                i = min([i for i in ready[q] if can[i] <= t0 + slack[q == "v"]], key=lambda i: prio[i])
-                o = ops[i]
-                ready[q].remove(i)
-                t0 = max(free[q], can[i])
-                free[q] = t0 + o["busy"]
-                at[i] = free[q] if back else t0
-                end = max(end, t0 + o["lat"])
-                seq.append(i)
-                for k in out[i]:
-                    if back:
-                        d = at[i] + (ops[k]["lat"] + WAKE - ops[k]["busy"] if o["pre"][k] else 0)
-                    else:
-                        d = t0 + (o["lat"] + WAKE if ops[k]["pre"][i] else o["busy"])
-                    can[k] = max(can[k], d)
-                    left[k] -= 1
-                    if not left[k]:
-                        ready[ops[k]["q"]].append(k)
-            return seq, at, end
-
-        def replay(seq, f, wake, trace=False):
-            free, done, go, end = {q: 0.0 for q in f}, [0.0] * m, [0.0] * m, 0.0
-            why, prev, top = [None] * m, {}, 0
-            for i in seq:
-                q, pre, busy, lat, isd = flat[i]
-                t0 = free[q]
-                w = prev.get(q)
-                for j, wait in pre:
-                    d = done[j] + wake if wait else go[j]
-                    if d > t0:
-                        t0, w = d, j
-                why[i] = w
-                prev[q] = i
-                if isd:
-                    go[i] = free[q] = t0 + busy
-                    d = done[i] = t0 + lat * (f["r"] if q != "s" else 1)
-                else:
-                    d = go[i] = free[q] = done[i] = t0 + busy * f[q]
-                if d > end:
-                    end, top = d, i
-            if not trace:
-                return end
-            path = []
-            while why[top] is not None:
-                if why[top] not in ops[top]["pre"]:
-                    path.append((why[top], top))
-                top = why[top]
-            return path
-
-        flat = [(o["q"], list(o["pre"].items()), o["busy"], o["lat"], o["dma"]) for o in ops]
-
         if m not in PLAN:
-            good = None
-            rnd = np.random.default_rng(7)
-            for turn in range(TURNS):
-                slack = SLACKS[turn % len(SLACKS)]
-                if turn < len(SLACKS):
-                    prio = list(range(m))
-                else:
-                    t1 = rnd.random() * good[0]
-                    w = (rnd.random(m) - 0.5) * SHAKE[turn % len(SHAKE)] * (rnd.random(m) < 0.3)
-                    prio = [x + (y if t1 - 4000 < z < t1 + 4000 else 0) for x, y, z in zip(good[3], w.tolist(), good[2])]
-                    slack = good[4] if turn % 7 else slack
-                for k in range(6 if turn < len(SLACKS) else 2 if turn % 5 == 0 else 1):
-                    if k:
-                        prio = [-x for x in plan([-x for x in at], True, slack)[1]]
-                    seq, at, end = plan(prio, False, slack)
-                    if good is not None and end > 1.06 * good[0]:
-                        continue
-                    end = (end + sum(replay(seq, *c) for c in CASES)) / (1 + len(CASES))
-                    if good is None or end <= good[0]:
-                        good = (end, seq, at, prio if k or turn >= len(SLACKS) else at, slack)
-            best = now = (sum(replay(good[1], *c) for c in CASES), good[1])
-            for turn in range(SWAPS):
-                seq = now[1]
-                path = replay(seq, *CASES[turn % len(CASES)], True)
-                if not path:
-                    continue
-                i, j = path[int(rnd.integers(len(path)))]
-                a, b = seq.index(i), seq.index(j)
-                for _ in range(int(rnd.integers(3))):
-                    e = [x for x in range(a - 1, max(a - 40, -1), -1) if ops[seq[x]]["q"] == ops[j]["q"]]
-                    a = e[0] if e else a
-                lift = {j}
-                for x in range(b - 1, a - 1, -1):
-                    if any(k in lift for k in nxt[seq[x]]):
-                        lift.add(seq[x])
-                if seq[a] in lift:
-                    continue
-                mid = seq[a:b + 1]
-                new = seq[:a] + [x for x in mid if x in lift] + [x for x in mid if x not in lift] + seq[b + 1:]
-                end = sum(replay(new, *c) for c in CASES)
-                if end <= now[0] + HEAT * (1 - turn / SWAPS) * rnd.random():
-                    now = (end, new)
-                    if end < best[0]:
-                        best = now
-            PLAN[m] = (best[0] / len(CASES), best[1])
+            PLAN[m] = order(ops)
         val = [0] * m
         for i in PLAN[m][1]:
             o = ops[i]
@@ -354,16 +368,15 @@ def rank_program(g, core, T, topo):
     def scan(out, a, b, init, o0, o1):
         op("v", [out], [a, b], lambda: g.vector.tensor_tensor_scan(out[0], a[0], b[0], init, o0, o1), 0)
 
-    def act(out, in_, f, bias=0.0, scale=1.0, accum=None):
-        outs = [out] if accum is None else [out, accum]
-        if accum is None:
-            op("a", outs, [in_, bias, scale], lambda: g.scalar.activation(out[0], in_[0], f, bias=ap(bias), scale=ap(scale)))
-        else:
-            op("a", outs, [in_, bias, scale],
-               lambda: g.scalar.activation(out[0], in_[0], f, bias=ap(bias), scale=ap(scale), accum_out=accum[0]))
+    def act(out, in_, f, bias=0.0, scale=1.0):
+        op("a", [out], [in_, bias, scale], lambda: g.scalar.activation(out[0], in_[0], f, bias=ap(bias), scale=ap(scale)))
 
     def mm(out, l, r, start=True, stop=True):
         op("p", [out], [l, r], lambda: g.tensor.matmul(out[0], l[0], r[0], start, stop))
+
+    def mms(out, *pairs):
+        for i, (l, r) in enumerate(pairs):
+            mm(out, l, r, i == 0, i == len(pairs) - 1)
 
     def iota(out, pat, base, cm, fl=True):
         if fl:
@@ -374,38 +387,29 @@ def rank_program(g, core, T, topo):
     def asel(out, in_, pat, cmp_, fill, base, cm):
         op("g", [out], [in_], lambda: g.affine_select(out[0], in_[0], pat, cmp_, fill, base, cm))
 
-    def push(t, lo, hi):
-        dst = T.cores[(rank - JUMPS[t]) % n]
-        rid, pid, _ = topo.addr(dst)
-        k = len(topo.engines(core, dst))
-        src = A("X", O + lo, O + hi)
-        arr, snt = "arr%d" % nd[1], "snt%d" % nd[1]
-        nd[1] += 1
-        lat = 2200 + (hi - lo) * 256 / LINK
-        me = add("g", [], [src], lambda: g.remote_dma(T["R%d" % t][:, lo:hi], src[0], T.sem[arr], T.sem[snt], pid, rid,
-                                                     topo.mask(core, dst)), 300, lat, snt, k)
-        k2 = len(topo.engines(T.cores[(rank + JUMPS[t]) % n], core))
-        add("r", [A("R%d" % t, lo, hi)], [], None, 0, lat - 300, arr, k2, after=me)
+    def push(count):
+        for _ in range(count):
+            push_one(nd[1], *WRITES[nd[1]])
+            nd[1] += 1
 
-    def push_via(t, lo, hi):
-        mate = helper(T, topo, rank)
-        rid, pid, _ = topo.addr(mate)
+    def push_one(i, t, lo, hi, via):
         dst = T.cores[(rank - JUMPS[t]) % n]
-        eng = [e for e in topo.engines(core, mate) if e not in topo.engines(core, dst)]
+        to = helper(T, topo, rank) if via else dst
+        rid, pid, _ = topo.addr(to)
+        eng = [e for e in topo.engines(core, to) if not via or e not in topo.engines(core, dst)]
         src = A("X", O + lo, O + hi)
-        arr, snt = "arr%d" % nd[1], "snt%d" % nd[1]
-        nd[1] += 1
-        lat = 2200 + (hi - lo) * 256 / LINK
+        arr, snt = "arr%d" % i, "snt%d" % i
+        by = (hi - lo) * 256 / LINK
+        ahead = sum((w[2] - w[1]) * 256 / LINK for w in WRITES[:i] if w[0] == t and w[3] == via and w[1] < B0 + (t - 1) * S or w[0] == t == 0)
         me = add("g", [], [src], lambda: g.remote_dma(T["R%d" % t][:, lo:hi], src[0], T.sem[arr], T.sem[snt], pid, rid,
-                                                     sum(1 << e for e in eng)), 300, lat, snt, len(eng))
-        k2 = len(topo.engines(helper(T, topo, (rank + JUMPS[t]) % n), core))
-        add("r", [A("R%d" % t, lo, hi)], [], None, 0, 2 * lat - 300, arr, k2, after=me)
+                                                     sum(1 << e for e in eng)), 300, HOP + by, snt, len(eng), prev[0])
+        prev[0] = me
+        frm = (rank + JUMPS[t]) % n
+        k2 = len(topo.engines(helper(T, topo, frm) if via else T.cores[frm], core))
+        add("r", [A("R%d" % t, lo, hi)], [], None, 0, HOP + by + (HOP + by if via else 0) + ahead * 0.7 - 300, arr, k2, after=me)
 
     def col(j):
         return A("COL", j, j + 1)
-
-    def kb(j):
-        return [0.5, CADD, CADD - 255.0, -float(O), 1.0 - O, -1.0, 256.0][j]
 
     d = dma("s", A("X", O, O + B0 // 2), T.lab[:, 0:B0 // 2])
     d = dma("s", A("WI"), T.wts[:], d)
@@ -415,25 +419,31 @@ def rank_program(g, core, T, topo):
         c = dma("as"[gi // 6], A("COVI", 16 * gi, 16 * gi + 16, rows=(0, 72)), T.cov[gi], d if gi >= 6 else None)
         if gi >= 6:
             d = c
-    cp(A("X2", ACT_HOLD[0], B0), A("X", O + ACT_HOLD[0], O + B0))
+    if ACT_HOLD[0] < B0:
+        d = dma("s", A("X2", ACT_HOLD[0], B0), T.lab[:, ACT_HOLD[0]:B0], d)
     d = dma("s", A("AC"), T.act[:], d)
     d = dma("s", A("PTH"), T.pth[:], d)
 
     iota(A("IP", 0, 1), [[0, 1]], 0, 1, False)
-    iota(A("IC"), [[1, 144]], 0, 0)
     iota(A("IG"), [[1, 9], [0, 16]], 0, 0)
-    iota(A("IJ"), [[16, 48]], 0, 0)
+    iota(A("IC"), [[1, 144]], 0, 0)
     ms(A("ONES"), 1.0)
-    ms(A("LW"), 0.0)
     asel(A("IDB"), A("ONES", 0, 128), [[-1, 128]], OP.is_equal, 0.0, 0, 1)
     ts(A("IP", 1, 2), A("IP", 0, 1), 15, OP.bitwise_and)
     ts(A("IP", 2, 3), A("IP", 0, 1), 4, OP.arith_shift_right)
     ts(A("IP", 3, 4), A("IP", 0, 1), 4, OP.arith_shift_right, 1, OP.bitwise_and)
     ts(A("IP", 4, 5), A("IP", 0, 1), 111, OP.bitwise_and)
     ms(A("X", 0, O), 512.0)
-    cp(A("COL", 0, 3), A("IP", 1, 4))
-    ts(col(5), A("IP", 4, 5), 16.0, OP.add)
-    ts(col(3), col(2), -1.0, OP.mult, 1.0, OP.add)
+    cp(A("COL", 0, 4), A("IP", 1, 5))
+    act(col(5), col(3), AF.Identity, bias=16.0)
+    act(col(3), col(2), AF.Identity, bias=1.0, scale=-1.0)
+    act(col(11), col(1), AF.Identity, bias=col(3))
+    ts(A("AOF"), A("ONES", 0, 18), col(0), OP.mult)
+    for h in range(2):
+        ts(A("XO", 144 * h, 144 * h + 144), A("IG"), col(11), OP.is_equal, col(3 - h), OP.mult)
+    ts(A("WG"), A("WI"), 2048.0, OP.is_gt, -4096.0, OP.mult)
+    tt(A("WS"), A("WI"), A("WG"), OP.add)
+    tt(A("LW"), IND(A("WS"), A("AOF")), A("XO"), OP.mult)
     ts(A("BLK1"), A("IG", 0, 128), col(1), OP.is_equal)
     ts(col(9), col(0), 7.0, OP.is_ge, -208.0, OP.mult)
     asel(A("IDH"), A("ONES", 0, 128), [[-1, 128]], OP.is_equal, 0.0, 0, 1)
@@ -441,336 +451,223 @@ def rank_program(g, core, T, topo):
     act(A("NIDB"), A("IDB"), AF.Identity, scale=-1.0)
     act(A("CS2"), A("ONES", 0, 128), AF.Identity, scale=-5.0 * 65536)
     act(A("CS1"), A("ONES", 0, 128), AF.Identity, scale=-10.5 * 65536)
-    ts(col(10), col(0), 32.0, OP.mult, col(9), OP.add)
-    cp(M("WH", ALL, 0, ALL), A("WI"))
+    act(col(10), col(0), AF.Identity, bias=col(9), scale=32.0)
     ts(A("ROL"), A("IC", 0, 16), col(10), OP.add, 223.0, OP.min)
-    tt(M("WH", ALL, 1, ALL), A("WI"), M("WH", ALL, 0, ALL), OP.subtract)
     ts(A("LFU", 0, 14), A("LFI", 0, 14), float(O), OP.add)
-    for h in range(2):
-        ts(M("WM", ALL, slice(2 * h, 2 * h + 2), ALL), A("WH"), col(3 - h), OP.mult)
-    for p in range(4):
-        r = slice(32 * p, 32 * p + 32)
-        act((T.LW[r, :, 32 * p + 16:32 * p + 32], "LW", p, p + 1), M("WM", r, ALL, ALL), AF.Identity)
     ts(A("COVH", rows=(0, 72)), A("COVI", rows=(0, 72)), float(O), OP.add)
     mm(A("PM", 0, 72), A("COVH", rows=(0, 72)), A("IDH", 0, 72, rows=(0, 72)))
     cp(A("COVL", 0, 72), A("PM", 0, 72))
     cp(A("LF0", 0, 14), A("LFI", 0, 14))
     for h in range(2):
-        ts(M("XH", ALL, h, ALL), A("IC"), col(5), OP.is_equal, col(3 - h), OP.mult)
-    ts(col(4), col(1), 16.0, OP.mult, 15.0, OP.add)
+        ts(A("XH", 144 * h, 144 * h + 144), A("IC"), col(5), OP.is_equal, col(3 - h), OP.mult)
+    act(col(4), col(1), AF.Identity, bias=15.0, scale=16.0)
     ts(A("SELB"), A("IC"), col(4), OP.is_equal)
     act(A("XP", 0, O), A("ONES", 0, O), AF.Identity)
-    ts(A("LF", 0, 14), A("LFI", 0, 14), float(O), OP.add)
-    ts(col(6), col(0), 1.0, OP.add)
-    ts(col(15), col(0), 17.0, OP.add)
-    ts(col(8), col(0), -4096.0, OP.mult, 4096.0, OP.add)
-    ts(A("NEWL", 0, 42), A("IJ", 0, 42), col(0), OP.add, float(O + B0), OP.add)
-    act(A("BLKN"), A("BLK1"), AF.Identity, scale=-131072.0)
-    act(A("BLKP"), A("BLK1"), AF.Identity, scale=4096.0)
-    act(A("SELN"), A("SELB"), AF.Identity, scale=-4096.0)
+    act(col(6), col(0), AF.Identity, bias=1.0)
+    act(col(7), col(0), AF.Identity, bias=17.0)
+    act(col(8), col(0), AF.Identity, bias=4096.0, scale=-4096.0)
+    act(col(12), col(0), AF.Identity, bias=-4096.0, scale=-2048.0)
+    act(A("BLKT"), A("BLK1"), AF.Identity, scale=-2048.0)
+    act(A("SELN"), A("SELB"), AF.Identity, scale=-128.0)
     act(A("NI2"), A("IDB"), AF.Identity, scale=-2048.0)
+    act(A("PI2"), A("IDB"), AF.Identity, scale=2048.0)
+    act(A("SEL2"), A("SELB"), AF.Identity, scale=2.0)
 
-    push(0, 0, B0 // 2)
-    push(0, B0 // 2, B0)
-    iota(A("IS"), [[1, 672]], O + B0, 0)
+    push(len([w for w in WRITES if w[0] == 0]))
     iota(A("IA"), [[0, 14], [1, 16]], 0, 0)
+    iota(A("IJ"), [[16, 48]], B0 - 2048, 0)
     act(A("MASKD"), A("IA"), AF.Relu, bias=col(8), scale=4096.0)
-    asel(A("TRI"), A("BLKN"), [[1, 128]], OP.is_gt, 0.0, 0, -1)
-    asel(A("TRI"), A("TRI"), [[1, 128]], OP.not_equal, 4096.0, 0, -1)
+    act(A("NEWL", 0, 42), A("IJ", 0, 42), AF.Identity, bias=col(0))
+    asel(A("NEWH", 0, 42), A("NEWL", 0, 42), [[1, 42]], OP.is_ge, 0.0, 0, 0)
+    asel(A("LF", 0, 14), A("LFI", 0, 14), [[1, 14]], OP.is_ge, 0.0, 0, 0)
+    asel(A("TRI"), A("BLKT"), [[1, 128]], OP.is_gt, 0.0, 0, -1)
+    asel(A("TRI"), A("TRI"), [[1, 128]], OP.not_equal, 2048.0, 0, -1)
     asel(A("SELH"), A("SELB"), [[1, 144]], OP.is_ge, 0.0, 0, 0)
     asel(A("BLKH"), A("BLK1"), [[1, 128]], OP.is_ge, 0.0, 0, 0)
-    ts(col(11), col(1), col(3), OP.add)
-    for h in range(2):
-        ts(M("XO", ALL, h, ALL), A("IG"), col(11), OP.is_equal, col(3 - h), OP.mult)
-    for t in range(RO):
-        if t and VEC_SGN[t] == VEC_SGN[t - 1]:
-            continue
-        ts(col(7), col(0), 16.0 - 4 * VEC_SGN[t], OP.is_ge, -16.0, OP.mult)
-        ts(A("COL", 12 + t, 15), A("ONES", 0, 3 - t), -7.0, OP.mult, col(7), OP.add)
+    kinds = sorted(set(VEC_CMP))
+    ms(A("ZL", 0, S * len(kinds)), 0.0)
+    for i, k in enumerate(kinds):
+        ts(col(13 + i), col(0), 16.0 - k, OP.is_ge, -16.0, OP.mult)
+        act(A("ZL", S * i + S - 1, S * i + S), col(13 + i), AF.Identity, bias=-8.5)
     asel(A("RST"), A("ONES", 0, 336), [[0, 21], [1, 16]], OP.is_equal, 0.0, 0, 0)
     asel(A("SHF"), A("BLK1"), [[1, 128]], OP.is_equal, 0.0, -1, -1)
     asel(A("E0"), A("IDB"), [[0, 8], [1, 16]], OP.is_equal, 0.0, 0, 0)
+    iota(A("IS"), [[1, 672]], B0, 0)
     asel(A("NEWN"), A("IS"), [[1, 672]], OP.is_ge, 0.0, 0, 0)
     asel(A("G8"), A("BLK1", 0, 128, 16), [[1, 8]], OP.is_ge, 0.0, 0, 0)
 
-    def lw(h, hl, rho):
-        return M("LW", ALL, 2 * h + hl, slice(16 - 16 * rho, 144 - 16 * rho))
+    def cross(name, h, rho):
+        return A(name, 144 * h + 16 - 16 * rho, 144 * h + 144 - 16 * rho)
 
     def px(h):
         return M("PX", ALL, slice(0, 7), h, ALL)
 
     PXA = M("PX", ALL, slice(0, 7), ALL, ALL)
 
-    def half(name, rho):
-        return A(name, 112 * rho, 112 * rho + 112)
+    def half(name, rho, lo=0):
+        return A(name, lo + 112 * rho, lo + 112 * rho + 112)
 
-    def path_mm():
+    def bk(bank, w):
+        return M(bank, ALL, slice(0, w // 32), ALL, ALL) if bank in ("PH0", "PX") else A(bank, 0, w)
+
+    def path_list():
         for h in range(2):
-            for rho in range(2):
-                mm(px(h), M("XH", ALL, h, slice(16 - 16 * rho, 144 - 16 * rho)), half("PV", rho), rho == 0, rho == 1)
+            mms(px(h), *[(cross("XH", h, rho), half("PV", rho)) for rho in range(2)])
+        tr(A("TOP"), PXA)
+        ts(A("POF"), IND(A("TOP", 0, 224), A("ROL", 0, 16)), float(O), OP.add)
 
-    def hold_gather(b, lo, hi):
-        tt(A("CMP", lo, hi), IND(A("X", 0, O + b), A("COVL", lo // 16, hi // 16)), A("X2", lo, hi), OP.is_le)
-
-    def ph0(w):
-        return M("PH0", ALL, slice(0, w // 32), ALL, ALL)
-
-    def hold_sum(lo, hi, bank, cs):
-        o = ph0(hi - lo) if bank == "PH0" else A(bank, 0, hi - lo)
-        mm(o, A(cs), A("ONES", 0, hi - lo), True, False)
-        mm(o, A("BLKM"), A("CMP", lo, hi), False, True)
+    def hold_v(lo, hi, bank):
+        own = A("X2", lo, hi) if lo < B0 else A("X", O + lo, O + hi)
+        tt(A("CMP", lo, hi), IND(A("X", 0, O + max(lo, B0)), A("COVL", lo // 16, hi // 16)), own, OP.is_le)
+        mms(bk(bank, hi - lo), (A("CS1"), A("ONES", 0, hi - lo)), (A("BLKM"), A("CMP", lo, hi)))
 
     def hold_max(lo, hi, bank):
-        o = ph0(hi - lo) if bank == "PH0" else A(bank, 0, hi - lo)
-        tt(A("XP", O + lo, O + hi), o, A("X", O + lo, O + hi), OP.max)
+        tt(A("XP", O + lo, O + hi), bk(bank, hi - lo), A("X", O + lo, O + hi), OP.max)
 
-    def hold_ag(b, lo, hi, bank):
-        act(A("XC", lo, hi), IND(A("X", 0, O + b), A("COVL", lo // 16, hi // 16)), AF.Identity)
-        mm(A(bank, 0, hi - lo), A("IDB"), A("X", O + lo, O + hi), True, False)
-        mm(A(bank, 0, hi - lo), A("NIDB"), A("XC", lo, hi), False, True)
+    def hold_a(lo, hi, bank):
+        act(A("XC", lo, hi), IND(A("X", 0, O + B0), A("COVL", lo // 16, hi // 16)), AF.Identity)
+        mms(bk(bank, hi - lo), (A("IDB"), A("X", O + lo, O + hi)), (A("NIDB"), A("XC", lo, hi)))
+        act(A("CMP", lo, hi), bk(bank, hi - lo), AF.Sign, bias=0.5)
+        mms(bk(bank, hi - lo), (A("CS2"), A("ONES", 0, hi - lo)), (A("BLKM"), A("CMP", lo, hi)))
 
-    def hold_as(lo, hi, bank):
-        act(A("CMP", lo, hi), A(bank, 0, hi - lo), AF.Sign, bias=kb(0))
-        hold_sum(lo, hi, bank, "CS2")
+    def sel_list(selname, src, lo=0):
+        return [(A(selname, 15 - a, 143 - a), A(src, lo + a, lo + S, 16)) for a in range(16)]
 
-    def sel_list(out, selname, src, first=True, last=True):
-        for a in range(16):
-            mm(out, A(selname, 15 - a, 143 - a), A(src, a, 224, 16), first and a == 0, last and a == 15)
-
-    def cover_a(t):
-        act(A("FIT"), A("PC", 0, 224), AF.Relu, bias=A("BIA", 0, 1))
-        mm(A("PC", 224, 448), A("BLKN"), A("HLD"), True, False)
-        mm(A("PC", 224, 448), A("TRI"), A("FIT"), False, True)
-        act(A("PC", 224, 448), A("PC", 224, 448), AF.Relu)
-
-    def cover_b(t):
-        tt(A("SH2"), A("PC", 224, 448), A("CI"), OP.min)
-        if t < RO - 1:
-            sel_list(A("PC", 448, 462), "SELH", "SH2")
-        mm(A("PC", 0, 224, rows=(0, 8)), A("G8"), A("SH2"))
-
-    def cover_c(t):
-        ts(A("COVL", 72 + 14 * t, 86 + 14 * t), A("PC", 448, 462), O - 1.0, OP.add)
-
-    def cover_d(t):
-        y = A("YC", S * t, S * t + S, rows=(0, 8))
-        act(y, A("PC", 0, 224, rows=(0, 8)), AF.Identity, bias=-1.0)
-
+    ts(A("PV"), IND(A("PTH", 0, B0), A("LF0", 0, 14)), 0.0, OP.add)
     for t in range(RO):
         b = B0 + t * S
         last = t == RO - 1
         XB = A("X", 0, O + b)
         na = ACT_HOLD[t]
         old = b - S if t else b
-        blocks = [(lo, min(lo + 512, old)) for lo in range(na, old, 512)]
+        Z, SUS, CI, xk = A("Z", S * t, S * t + S), A("SUS", S * t, S * t + S), A("CI", S * t, S * t + S), 3584 * (t & 1)
         act(A("XV"), IND(XB, A("LFU", 0, 14)), AF.Identity)
-        if t:
-            path_mm()
-            tr(A("TOP"), PXA)
         for h in range(2):
-            for k in range(4):
-                mm(px(h), lw(h, k & 1, k >> 1), half("XV", k >> 1), k == 0, k == 3)
-        hold_ag(b, 0, 512, "PD0")
-        hold_gather(b, *blocks[0])
-        hold_sum(blocks[0][0], blocks[0][1], "PH0", "CS1")
+            mms(px(h), *[(cross("LW", h, rho), half("XV", rho)) for rho in range(2)])
         tr(A("TOH"), PXA)
-        hold_as(0, 512, "PD0")
+        if t == 0:
+            path_list()
         cp(A("HI"), IND(A("TOH", 0, 224), A("ROL", 0, 2)))
-        if t:
-            cover_b(t - 1)
         ts(A("HA", 0, 14), A("HI", 0, 14), DA - 1, OP.bitwise_and)
         ts(A("HQ", 0, 14), A("HI", 16, 30), 4095, OP.bitwise_and)
         cp(A("AL", 0, 14), A("HA", 0, 14))
-        act(A("DZ"), IND(A("AC", 0, DA), A("AL", 0, 14)), AF.Identity)
-        mm(A("PM", 0, 224), A("IDB"), A("XV"), True, False)
-        mm(A("PM", 0, 224), A("NIDB"), A("DZ"), False, True)
-        act(A("Z"), A("PM", 0, 224), AF.Abs)
-        for h in range(2):
-            for hl in range(2):
-                mm(A("PM", 224, 448), lw(h, hl, h), A("Z"), h + hl == 0, h + hl == 2)
         ts(A("QL", 0, 14), A("HQ", 0, 14), b / 4096.0, OP.mult, FLOOR, OP.add)
+        if na:
+            hold_a(0, min(na, 512), "PH0")
+            hold_max(0, min(na, 512), "PH0")
         if na > 512:
-            hold_ag(b, 512, na, "PD1")
-        hold_max(blocks[0][0], blocks[0][1], "PH0")
-        if t:
-            cp(A("POF"), IND(A("TOP", 0, 224), A("ROL", 0, 16)))
-            cover_c(t - 1)
-            cover_d(t - 1)
-        else:
-            ts(A("PV"), IND(A("PTH", 0, B0), A("LF0", 0, 14)), float(O), OP.add)
-            path_mm()
-        hold_max(0, 512, "PD0")
+            hold_a(512, na, "PX")
+            hold_max(512, na, "PX")
+        for lo, hi in [(x, min(x + 512, B0)) for x in range(na, B0, 512)] + [(x, x + S) for x in range(B0, old, S)]:
+            hold_v(lo, hi, "PP")
+            hold_max(lo, hi, "PP")
+        act(A("DZ"), IND(A("AC", 0, DA), A("AL", 0, 14)), AF.Identity)
+        mms(A("PM", 0, 224), (A("IDB"), A("XV")), (A("NIDB"), A("DZ")))
+        act(Z, A("PM", 0, 224), AF.Abs)
+        mms(A("PM", 224, 448), *[(cross("LW", h, h), Z) for h in range(2)])
         cp(A("ZI"), A("PM", 224, 448))
-        if na > 512:
-            hold_as(512, na, "PD1")
-        if t:
-            hold_gather(b, old, b)
-            hold_sum(old, b, "PH1", "CS1")
         ts(A("ZJ"), A("ZI"), 4095, OP.bitwise_and)
-        for blk in blocks[1:]:
-            hold_gather(b, *blk)
-            hold_sum(blk[0], blk[1], "PH0", "CS1")
         ts(A("COF"), A("ZJ"), b / 4096.0, OP.mult, O + FLOOR, OP.add)
-
-        def gat(hf):
-            for c in range(112 * hf, 112 * hf + 112, 28):
-                if c >= S - 28 * VEC_GAT[t]:
-                    cp(A("XK", 16 * c, 16 * c + 448), IND(XB, A("COF", c, c + 28)))
-                else:
-                    act(A("XK", 16 * c, 16 * c + 448), IND(XB, A("COF", c, c + 28)), AF.Identity)
-
-        def dif(u):
-            hf, qd = u >> 2, u & 3
-            for j in range(4):
-                o = A("PD%d" % (u & 1), 112 * j, 112 * j + 112)
-                mm(o, A("IDB"), half("Z", hf), True, False)
-                mm(o, A("NIDB"), A("XK", 1792 * hf + 4 * qd + j, 1792 * hf + 1792, 16), False, True)
-
-        def sgn(u):
-            if (u & 3) >= 4 - VEC_SGN[t]:
-                ts(A("SG", 448 * u, 448 * u + 448), A("PD%d" % (u & 1), 0, 448), 0.0, OP.is_ge, 2.0, OP.mult)
-            else:
-                act(A("SG", 448 * u, 448 * u + 448), A("PD%d" % (u & 1), 0, 448), AF.Sign, bias=kb(0))
-
-        def cntm(u):
-            for j in range(4):
-                m = 4 * (u & 3) + j
-                mm(half("PC", u >> 2), A("SELB", 15 - m, 143 - m), A("SG", 448 * u + 112 * j, 448 * u + 112 * j + 112),
-                   m == 0, m == 15)
-
-        gat(0)
-        for blk in blocks[1:]:
-            hold_max(blk[0], blk[1], "PH0")
-        if t == 0:
-            tr(A("TOP"), PXA)
-            cp(A("POF"), IND(A("TOP", 0, 224), A("ROL", 0, 16)))
-        if na > 512:
-            hold_max(512, na, "PD1")
+        ts(CI, A("COF"), 1.0 - O, OP.add)
         if t:
-            hold_max(old, b, "PH1")
-        ts(A("CI"), A("COF"), 1.0 - O, OP.add)
-        if ON_ACT[0]:
+            hold_v(old, b, "PM")
+            hold_max(old, b, "PM")
+
+        for c in range(0, S, 28):
+            o = A("XK", xk + 16 * c, xk + 16 * c + 448)
+            if c >= S - 28 * VEC_GAT[t]:
+                cp(o, IND(XB, A("COF", c, c + 28)))
+            else:
+                act(o, IND(XB, A("COF", c, c + 28)), AF.Identity)
+        if ON_ACT[t][0]:
             act(A("CE"), IND(A("R%d" % t, 0, b), A("QL", 0, 14)), AF.Identity, bias=CADD, scale=-1.0)
         else:
             ts(A("CE"), IND(A("R%d" % t, 0, b), A("QL", 0, 14)), -1.0, OP.mult, CADD, OP.add)
-        XPB = A("XP", 0, O + b)
-        gat(1)
-        act(A("EM"), A("CE"), AF.Relu, bias=kb(2), scale=-1.0)
-        act(A("E"), A("CE"), AF.Identity, bias=kb(1), scale=-1.0)
-        npa = ACT_PATH[t]
-        for k in range(16 - npa, 16):
-            j = k - 16 + npa
-            act(A("XG", S * j, S * j + S), IND(XPB, A("POF", 16 * k, 16 * k + 14)), AF.Identity)
-            o = A("PD%d" % (j >> 1 & 1), S * (j & 1), S * (j & 1) + S)
-            mm(o, A("IDB"), A("XG", S * j, S * j + S), True, False)
-            mm(o, A("NIDB"), A("E"), False, True)
-            if j & 1 or k == 15:
-                w = S * (j & 1)
-                act(A("PO", S * k - w, S * k + S), A(o[1], 0, w + S), AF.Identity, bias=CADD)
-        for k in range(16):
-            if k < 16 - npa:
-                tt(A("PO", S * k, S * k + S), IND(XPB, A("POF", 16 * k, 16 * k + 14)), A("CE"), OP.add)
-            mm(A("PP", 0, 224), A("SELB", 15 - k, 143 - k), A("PO", S * k, S * k + S), k == 0, k == 15)
-            if k == 8:
-                dif(0)
-                dif(1)
-                sgn(0)
-                sgn(1)
-            if k == 13:
-                dif(2)
-                sgn(2)
-        if ON_ACT[1]:
-            act(A("LOW"), A("PP", 0, 224), AF.Relu, bias=4096.0 + 15.0, scale=-1.0 / 512)
-            act(A("HLD"), A("PP", 0, 224), AF.Relu, bias=-1.0, scale=1.0 / 8388608)
-        else:
-            ts(A("LOW"), A("PP", 0, 224), 2097152.0 + 7.5 * 1024, OP.is_lt)
-            ts(A("HLD"), A("PP", 0, 224), 8388608.0, OP.is_ge)
-        dif(3)
-        sgn(3)
-        cntm(0)
-        mm(A("PP", 224, 448), A("BLKN"), A("EM"), True, False)
-        mm(A("PP", 224, 448), A("TRI"), A("LOW"), False, False)
-        mm(A("PP", 224, 448), A("BLKN"), A("HLD"), False, True)
-        mm(A("PM", 0, 224), A("BLKP"), A("HLD"))
-        mm(A("PM", 224, 448), A("NIDB"), A("Z"), True, False)
-        mm(A("PM", 224, 448), A("BLKN"), A("HLD"), False, True)
-        if ON_ACT[2]:
-            act(A("PP", 224, 448), A("PP", 224, 448), AF.Relu)
-            tt(A("SH"), A("PP", 224, 448), A("PV"), OP.min)
-        else:
-            tt(A("SE"), A("PP", 224, 448), A("PV"), OP.min)
-            ts(A("SH"), A("SE"), 0.0, OP.max)
-        act(A("ZT"), A("PM", 224, 448), AF.Relu, bias=kb(6))
-        act(A("JNK"), A("PM", 0, 224), AF.Sign, bias=kb(0), scale=-1.0, accum=A("ACC", 0, 1))
-        act(A("X", O + b, O + b + S), A("ZT"), AF.Identity, bias=kb(6), scale=-1.0)
-        if not last:
-            push_via(t + 1, b, b + S)
-            dma("s", A("X2", b, b + S), A("X", O + b, O + b + S))
-        else:
-            dma("s", T.yx[:, b:W], A("X", O + b, O + W))
-        dif(4)
-        sgn(4)
-        mm(ph0(224), A("IDB"), A("MASKD"), True, False)
+        act(A("E"), A("CE"), AF.Identity, bias=CADD, scale=-1.0)
+        if t:
+            act(A("EM"), A("CE"), AF.Relu, bias=CADD - 255.0, scale=-1.0)
+        for k in range(15, -1, -1):
+            win = A("XP", 0, O + B0 + S * max(0, t - k))
+            tt(A("PO", S * k, S * k + S), IND(win, A("POF", 16 * k, 16 * k + 14)), A("CE"), OP.add)
+            mm(A("PP", 0, 224), A("SELB", 15 - k, 143 - k), A("PO", S * k, S * k + S), k == 15, k == 0)
+        ts(A("LOW"), A("PP", 0, 224), 2097152.0 + 7.5 * 1024, OP.is_lt, 2.0, OP.mult)
+        ts(A("HLD"), A("PP", 0, 224), 8388608.0, OP.is_ge, 2.0, OP.mult)
+        mms(A("PM", 0, 224), (A("IDH"), A("PV")), *([(A("BLKT"), A("EM"))] if t else []),
+            (A("TRI"), A("LOW")), (A("BLKT"), A("HLD")))
+        mm(A("PP", 0, 224), A("BLK1"), A("HLD"))
+        ts(A("SH"), A("PM", 0, 224), O - 4096.0, OP.add, 0.0, OP.max)
+        act(SUS, A("PP", 0, 224), AF.Sign, bias=-0.5)
         for h in range(2):
-            for rho in range(2):
-                mm(px(h), M("XO", ALL, h, slice(16 - 16 * rho, 144 - 16 * rho)), M("SH", ALL, ALL, rho, ALL), rho == 0, rho == 1)
-        mm(ph0(224), A("BLKH"), A("SH"), False, True)
+            mms(px(h), *[(cross("XO", h, rho), M("SH", ALL, ALL, rho, ALL)) for rho in range(2)])
+        mms(bk("PH0", 224), (A("IDB"), A("MASKD")), (A("BLKH"), A("SH")))
         mm(M("PH0", ALL, slice(7, 14), 0, ALL), A("BLKH"), M("SH", ALL, ALL, 0, ALL))
         tr(A("TGX"), PXA)
-        tt(A("EQ", 0, 224), ph0(224), A("TGX"), OP.not_equal)
+        tt(A("EQ", 0, 224), bk("PH0", 224), A("TGX"), OP.not_equal)
         tt(A("EQ", 224, 336), M("PH0", ALL, slice(7, 14), 0, ALL), M("TGX", ALL, ALL, 1, ALL), OP.not_equal)
-        cp(A("TGU", 0, 14), M("TGX", ALL, ALL, ALL, 0))
-        dif(5)
-        sgn(5)
-        tt(A("V"), IND(XB, A("TGU", 0, 14)), A("E"), OP.max)
-        ts(A("PAR", 0, 1), A("ACC", 0, 1), -0.5, OP.mult, 112.0, OP.add)
-        dif(6)
-        sgn(6)
-        dif(7)
-        sgn(7)
-        mm(A("PP", 0, 14), A("IDH"), A("NEWL", 14 * t, 14 * t + 14), True, False)
-        sel_list(A("PP", 0, 14), "SELN", "HLD", False, True)
-        mm(A("PH1", 0, 224), A("E0"), A("NEWN", S * t, S * t + S), True, False)
-        mm(A("PH1", 0, 224), A("SHF"), A("PV"), False, False)
-        mm(A("PH1", 0, 224), A("BLKN"), A("HLD"), False, True)
-        if not last:
-            mm(A("PH1", 224, 448), A("NI2"), A("ONES", 0, 224), True, False)
-            mm(A("PH1", 224, 448), A("IDH"), A("PV"), False, False)
-            mm(A("PH1", 224, 448), A("NI2"), A("JNK"), False, True)
-        for u in range(1, 8):
-            cntm(u)
-        ts(A("PAR", 1, 2), A("PAR", 0, 1), 1, OP.bitwise_and)
         scan(A("SC"), A("RST"), A("EQ"), 1.0, OP.max, OP.min)
-        ts(A("BIA", 0, 1), A("PAR", 1, 2), -2.0, OP.mult, col(12 + t), OP.add)
-        tt(A("OFF", 16, 23), A("SC", 239, 336, 16), M("TGX", ALL, ALL, 1, 0), OP.mult)
-        tt(A("OFF", 0, 7), A("SC", 15, 224, 32), M("TGX", ALL, ALL, 0, 0), OP.mult)
-        tt(A("OFF", 8, 15), A("SC", 31, 224, 32), A("OFF", 16, 23), OP.mult)
-        tt(A("LF", 0, 14), A("PP", 0, 14), A("LF", 0, 14), OP.max)
-        for rho in range(2):
-            ts((T.OFU[:, rho:14:2], "OFU", 0, 14) if rho else (T.OFU[:, 0:14:2], "OFU", 14, 15), A("OFF", 8 * rho, 8 * rho + 7),
-               col(6 + 9 * rho), OP.max)
+        tt(A("OFF", 0, 14), A("SC", 15, 224, 16), M("TGX", ALL, ALL, ALL, 0), OP.mult)
+        tt(A("OFF", 16, 23), A("SC", 239, 336, 16), A("OFF", 1, 14, 2), OP.mult)
+        ts((T.OFU[:, 0:14:2], "OFU", 14, 15), A("OFF", 0, 14, 2), col(6), OP.max)
+        ts((T.OFU[:, 1:14:2], "OFU", 0, 14), A("OFF", 16, 23), col(7), OP.max)
+        cp(A("TGU", 0, 14), M("TGX", ALL, ALL, ALL, 0))
+        tt(A("V"), IND(XB, A("TGU", 0, 14)), A("E"), OP.max)
+        mms(A("PM", 0, 224), (A("IDB"), Z), (A("PI2"), SUS))
+        ts(A("X", O + b, O + b + S), A("PM", 0, 224), 2048.0, OP.add, 256.0, OP.min)
         if not last:
-            act(A("PVT"), A("PH1", 224, 448), AF.Relu)
-        act(A("YP", S * t, S * t + S), A("PH1", 0, 224), AF.Relu, bias=kb(3))
-        cover_a(t)
-        if not last:
-            cp(A("LFU", 0, 14), A("LF", 0, 14))
+            push(1)
         else:
-            ts(A("YV", 0, 14), A("LF", 0, 14), -float(O), OP.add)
-        for bb in range(12, -1, -2):
-            cp(IND(XB, (T.OFU[:, bb:bb + 2], "OFU", 0, 15, )[:4] + ()), A("V", 16 * bb, 16 * bb + 32))
+            dma("s", T.yx[:, b:W], A("X", O + b, O + W))
+        scan(A("SGN", S * t, S * t + S), SUS, A("ZL", S * kinds.index(VEC_CMP[t]), S * kinds.index(VEC_CMP[t]) + S),
+             1.0, OP.mult, OP.add)
+        mms(A("PP", 448, 462), (A("IDH"), A("NEWH", 14 * t, 14 * t + 14)), *sel_list("SELN", "SUS", S * t))
+        mms(A("PP", 224, 448), (A("E0"), A("NEWN", S * t, S * t + S)), (A("SHF"), A("PV")), (A("NI2"), SUS))
         if not last:
-            if ACT_HOLD[t + 1] < b:
-                cp(A("X2", ACT_HOLD[t + 1], b), A("X", O + ACT_HOLD[t + 1], O + b))
-            push_via(t + 1, 0, CUT[t])
-            push(t + 1, CUT[t], b)
-            tt(A("PV"), A("PH1", 0, 224), A("PVT"), OP.max)
+            mms(A("PP", 0, 224), (A("NI2"), A("ONES", 0, 224)), (A("IDH"), A("PV")), (A("PI2"), SUS))
+        tt(A("YV" if last else "LF", 0, 14), A("PP", 448, 462), A("LF", 0, 14), OP.max)
+        act(A("YP", S * t, S * t + S), A("PP", 224, 448), AF.Relu, bias=-2048.0)
+        dma("s", T.yp[:, S * t:S * t + S], A("YP", S * t, S * t + S))
+        if not last:
+            ts(A("LFU", 0, 14), A("LF", 0, 14), float(O), OP.add)
+            tt(A("PV"), A("PP", 0, 224), A("YP", S * t, S * t + S), OP.max)
+            path_list()
+        for bb in range(12, -1, -2):
+            cp(IND(XB, (T.OFU[:, bb:bb + 2], "OFU", 0, 15)), A("V", 16 * bb, 16 * bb + 32))
+        if not last:
+            push(len([w for w in WRITES if w[0] == t + 1]) - 1)
+            lo = ACT_HOLD[t + 1]
+            if lo < B0:
+                asel(A("X2", lo, B0), A("X", O + lo, O + B0), [[1, B0 - lo]], OP.is_ge, 0.0, 0, 0)
         else:
             dma("s", T.yx[:, 0:b // 2], A("X", O, O + b // 2))
             dma("a", T.yx[:, b // 2:b], A("X", O + b // 2, O + b))
             dma("s", T.yv[:], A("YV", 0, 14))
-            cover_b(t)
-            cover_d(t)
-        dma("s", T.yp[:, S * t:S * t + S], A("YP", S * t, S * t + S))
+        ns = 16 - VEC_CMP[t]
+        if ns < 16:
+            mm(A("PH1", 0, 224), A("IDB"), Z)
+        for hf in range(2):
+            def xm(m):
+                return A("XK", xk + 1792 * hf + m, xk + 1792 * hf + 1792, 16)
+
+            def sg(m, k=1):
+                return A("SG", 1792 * hf + 112 * m, 1792 * hf + 112 * (m + k))
+            for m in range(0, ns, 4):
+                bank = "PD%d" % (pd[0] & 1)
+                pd[0] += 1
+                k = min(4, ns - m)
+                for j in range(k):
+                    mms(A(bank, 112 * j, 112 * j + 112), (A("IDB"), half("Z", hf, S * t)), (A("NIDB"), xm(m + j)))
+                act(sg(m, k), A(bank, 0, 112 * k), AF.Sign, bias=0.5)
+            for m in range(ns, 16):
+                tt(sg(m), xm(m), half("PH1", hf), OP.is_le)
+            mms(half("PC", hf), *[(A("SELB" if m < ns else "SEL2", 15 - m, 143 - m), sg(m)) for m in range(16)])
+        act(A("FIT"), A("PC", 0, 224), AF.Sign, bias=A("SGN", S * t + S - 1, S * t + S))
+        mms(A("PC", 224, 448), (A("IDH"), CI), (A("NI2"), SUS), (A("TRI"), A("FIT")))
+        ts(A("SH2"), A("PC", 224, 448), col(12), OP.add, 0.0, OP.max)
+        if not last:
+            mms(A("PC", 448, 462), *sel_list("SELH", "SH2"))
+        mm(A("PC", 0, 224, rows=(0, 8)), A("G8"), A("SH2"))
+        if not last:
+            ts(A("COVL", 72 + 14 * t, 86 + 14 * t), A("PC", 448, 462), O - 1.0, OP.add)
+        act(A("YC", S * t, S * t + S, rows=(0, 8)), A("PC", 0, 224, rows=(0, 8)), AF.Identity, bias=-1.0)
     dma("s", T.yc[:], A("YC", rows=(0, 8)))
     emit()

@@ -8,42 +8,50 @@ JUMPS = [1, 5, 3]
 W = B0 + RO * S
 O = 48
 XW = O + W
-CADD = 131072.0 + 512.5
+CADD = 131072.0 + 1536.0
+LOWT = 16 * (131072.0 + 1024.0) + 7.5 * 1024
 FLOOR = -0.49609375
 MAGIC = 1.5 * 2 ** 23
-ACT_HOLD = [512, 512, 512]
+ACT_HOLD = [640, 512, 512]
 VEC_CMP = [8, 8, 8]
-VEC_GAT = [0, 0, 0]
-ON_ACT = [(1, 0, 0), (1, 0, 0), (1, 0, 0)]
-LINK = 80.0
-WRITES = [(0, 0, 576, 0), (0, 576, B0, 0),
-          (1, B0, B0 + S, 1), (1, 0, 224, 1), (1, 448, B0, 0), (1, 224, 448, 1),
-          (2, B0 + S, B0 + 2 * S, 1), (2, 0, 288, 1), (2, 576, B0 + S, 0), (2, 288, 576, 1)]
+ACT_PATH = [5, 5, 5]
+ON_VEC = ["SUS", "YC2"]
+COPY_ON = "v"
+LISTS_FIRST = 0
+PE_HASH = [0, 0, 0]
+GW = 56
+SNAP = [0, 0, 0]
+ON_ACT = [1, 1, 1]
+LINK, FIRST, HOLD = 90.0, 1200.0, 5000.0
+WRITES = [(0, 0, 384, 0), (0, 384, B0, 0),
+          (1, B0, B0 + S, 1), (1, 0, 208, 1), (1, 352, B0, 0), (1, 208, 352, 1),
+          (2, B0 + S, B0 + 2 * S, 1), (2, 0, 256, 1), (2, 432, B0 + S, 0), (2, 256, 432, 1)]
 
 BF, F32, F16, I32, U16 = "bfloat16", "float32", "float16", "int32", "uint16"
 SB = {
-    "X": ([128, XW], BF), "X2": ([128, B0], BF), "XP": ([128, O + W - S], BF), "R0": ([128, B0], BF), "R1": ([128, B0 + S], BF),
+    "X": ([128, XW], BF), "X2": ([128, B0], BF), "XS": ([128, XW], BF), "XP": ([128, W - S], BF), "R0": ([128, B0], BF), "R1": ([128, B0 + S], BF),
     "R2": ([128, B0 + 2 * S], BF), "AC": ([128, DA], BF), "PTH": ([128, B0], I32), "COVI": ([128, 128], I32),
     "COVH": ([128, 128], F16), "COVL": ([128, 128], U16), "WI": ([128, 16], I32), "WG": ([128, 16], F32),
-    "WS": ([128, 16], F32), "LW": ([128, 288], F16), "LFI": ([128, 16], I32), "LF0": ([128, 16], U16),
+    "WS": ([128, 16], F32), "LW": ([128, 288], F16), "LFI": ([128, 16], I32), "IH": ([128, 160], F32),
     "LF": ([128, 16], F32), "LFU": ([128, 16], U16), "AOF": ([128, 18], U16),
-    "IP": ([128, 8], I32), "COL": ([128, 16], F32), "IC": ([128, 144], F32), "IG": ([128, 144], F32),
+    "IP": ([128, 8], I32), "COL": ([128, 16], F32), "IC": ([128, 16], F32), "IG": ([128, 144], F32),
     "IS": ([128, 672], F32), "IA": ([128, 224], F32), "IJ": ([128, 48], F32),
-    "ROL": ([128, 16], U16), "SELB": ([128, 144], BF), "SELN": ([128, 144], BF), "SELH": ([128, 144], F16), "BLK1": ([128, 128], BF),
-    "PI2": ([128, 128], BF), "BLKM": ([128, 128], BF), "CS1": ([128, 128], BF),
+    "ROL": ([128, 16], U16), "SELB": ([128, 144], BF), "SELN": ([128, 144], BF),
+    "PI2": ([128, 128], BF), "CA": ([128, 128], BF), "BLKM": ([128, 128], BF), "CS1": ([128, 128], BF),
     "CS2": ([128, 128], BF), "ONES": ([128, 512], BF), "TRI": ([128, 128], BF), "IDB": ([128, 128], BF),
-    "NIDB": ([128, 128], BF), "NI2": ([128, 128], BF), "E0": ([128, 128], F16), "IDH": ([128, 128], F16),
-    "SHF": ([128, 128], F16), "XH": ([128, 288], F16), "SEL2": ([128, 144], BF),
+    "NIDB": ([128, 128], BF), "NI2": ([128, 128], BF), "E0": ([128, 128], F16),
+    "SHF": ([128, 128], F16), "XH": ([128, 288], BF),
     "HLD": ([128, 224], BF), "BLKT": ([128, 128], BF),
-    "NEWN": ([128, 672], F16), "NEWL": ([128, 48], F32), "MASKD": ([128, 224], BF),
+    "NEWN": ([128, 672], F16), "MASKD": ([128, 224], BF),
     "ZL": ([128, 672], BF), "NEWH": ([128, 48], F16),
-    "XO": ([128, 288], F16), "BLKH": ([128, 128], F16), "TGX": ([128, 7, 2, 16], F32), "G8": ([128, 8], F16),
+    "XO": ([128, 288], F16), "BLKH": ([128, 144], F16), "TGX": ([128, 7, 2, 16], F32),
     "XV": ([128, 224], BF), "PV": ([128, 224], F16), "TOH": ([128, 224], F32),
-    "TOP": ([128, 224], F32), "HI": ([128, 32], I32), "HA": ([128, 16], I32), "HQ": ([128, 16], I32),
+    "TOP": ([128, 224], F32), "HI": ([128, 32], I32), "HI3": ([128, 2, 16], I32), "WL0": ([128, 144], F16), "WL1": ([128, 144], F16),
+    "HA": ([128, 16], I32), "HQ": ([128, 16], I32),
     "AL": ([128, 16], U16), "QL": ([128, 16], U16), "POF": ([128, 256], U16), "DZ": ([128, 224], BF), "Z": ([128, 672], BF),
     "ZI": ([128, 224], I32), "ZJ": ([128, 224], I32), "COF": ([128, 224], U16), "CI": ([128, 672], F16),
     "CMP": ([128, W - S], BF), "XC": ([128, 1024], BF), "CE": ([128, 224], F32), "E": ([128, 224], BF), "EM": ([128, 224], BF),
-    "PO": ([128, 3584], BF), "XK": ([128, 7168], BF), "SG": ([128, 3584], BF), "LOW": ([128, 224], BF), "SUS": ([128, 672], BF),
+    "PO": ([128, 3584], BF), "XG": ([128, 3584], BF), "XK": ([128, 7168], BF), "SG": ([128, 3584], BF), "LOW": ([128, 224], BF), "SUS": ([128, 672], BF),
     "SH": ([128, 7, 2, 16], F16), "FIT": ([128, 224], BF), "SH2": ([128, 224], F16),
     "EQ": ([128, 336], BF), "SC": ([128, 336], BF), "RST": ([128, 336], BF), "OFF": ([128, 24], F32),
     "OFU": ([128, 16], U16), "TGU": ([128, 16], U16), "V": ([128, 224], BF), "SGN": ([128, 672], BF),
@@ -59,28 +67,37 @@ SEMAPHORES = (["cv", "ca", "cp", "cg"] + ["arr%d" % i for i in range(len(WRITES)
               + ["d%d" % i for i in range(NDMA)])
 BIG = 1 << 30
 PLAN = {}
-CASES = [(dict(zip("vapgsr", f)), w) for f, w in (((0.85, 0.85, 0.9, 1, 1, 1), 200.0), ((1, 1.08, 1.4, 1, 1, 0.75), 80.0),
-                                                  ((1.1, 1.0, 0.8, 1, 1, 1.4), 120.0), ((1, 1, 1, 1, 1, 1.0), 140.0))]
-SWAPS, HEAT = 6000, 600.0
+CASES = [(dict(zip("vapgsrGS", f)), w) for f, w in (((0.9, 0.9, 0.9, 1, 0.7, 1.0, 0.8, 1.2), 150.0),
+                                                    ((0.9, 1.05, 0.9, 1, 1, 1.2, 1.0, 1.0), 200.0),
+                                                    ((1, 0.85, 1.2, 1, 1, 0.8, 1.2, 0.6), 90.0),
+                                                    ((0.85, 0.85, 0.8, 1, 1.3, 1.6, 1.0, 1.0), 250.0),
+                                                    ((1, 1, 1, 1, 1, 1.2, 1.33, 1.4), 120.0),
+                                                    ((0.85, 1.0, 1.1, 1, 0.8, 1.0, 0.75, 1.0), 120.0),
+                                                    ((1, 0.9, 0.8, 1, 1.2, 1.3, 1.1, 0.8), 60.0))]
+SWAPS, HEAT = 14000, 800.0
 TURNS = 150
 SLACKS, SHAKE = ((0.0, 0.0), (130.0, 0.0), (300.0, 0.0), (130.0, 130.0), (300.0, 130.0), (300.0, 60.0)), (700.0, 600.0, 2000.0, 1200.0, 5000.0)
-HOP, LOC, LOCR = 1500.0, 1400.0, 200.0
-CYC, PE, FIX, WAKE = 0.95, 0.58, 40.0, 130.0
+HOP, LOC, LOCR = 1100.0, 1300.0, 230.0
+CYC, PE, FIX, FIXA, WAKE = 0.94, 0.53, 20.0, 150.0, 120.0
 
 
-def helper(T, topo, rank):
+def helper(T, topo, rank, via):
     core, n = T.cores[rank], len(T.cores)
-    return [c for c in topo.cores_of(core) if topo.die(c) != topo.die(core) and T.rank_of(c) is None
-            and all(topo.may_write(c, T.cores[(rank - j) % n]) for j in JUMPS)][0]
+    return [c for c in topo.cores_of(core) if (topo.die(c) == topo.die(core)) == (via == 3) and T.rank_of(c) is None
+            and all(topo.may_write(c, T.cores[(rank - j) % n]) for j in JUMPS)][(via - 1) % 2]
 
 
-def hand_on(g, core, T, topo, rank):
+def first_step(topo, src, to, dst, via):
+    return [e for e in topo.engines(src, to) if (e in topo.engines(src, dst)) == (via in (0, 3))]
+
+
+def hand_on(g, core, T, topo, rank, way):
     n = len(T.cores)
-    VIA = [(i, t, lo, hi) for i, (t, lo, hi, via) in enumerate(WRITES) if via]
+    VIA = [(i, t, lo, hi) for i, (t, lo, hi, via) in enumerate(WRITES) if via == way]
     for i, t, lo, hi in VIA:
         dst = T.cores[(rank - JUMPS[t]) % n]
         src = T.cores[rank]
-        k = len([e for e in topo.engines(src, core) if e not in topo.engines(src, dst)])
+        k = len(first_step(topo, src, core, dst, way))
         rid, pid, _ = topo.addr(dst)
         g.wait_ge(T.sem["arr%d" % i], k)
         g.remote_dma(T["R%d" % t][:, lo:hi], T["R%d" % t][:, lo:hi], T.sem["arr%d" % i], T.sem["snt%d" % i], pid, rid,
@@ -100,7 +117,7 @@ def order(ops):
         out = [list(o["pre"]) for o in ops] if back else nxt
         left = [len(nxt[i]) if back else len(ops[i]["pre"]) for i in range(m)]
         can = [ops[i]["lat"] - ops[i]["busy"] if back else 0.0 for i in range(m)]
-        ready = {q: [] for q in "vapgsr"}
+        ready = {q: [] for q in "vapgsrh"}
         free = {q: 0.0 for q in ready}
         for i in range(m):
             if not left[i]:
@@ -134,10 +151,10 @@ def order(ops):
         return seq, at, end
 
     def replay(seq, f, wake, trace=False):
-        free, done, go, end = {q: 0.0 for q in f}, [0.0] * m, [0.0] * m, 0.0
+        free, done, go, end = {q: 0.0 for q in "vapgsrh"}, [0.0] * m, [0.0] * m, 0.0
         why, prev, top = [None] * m, {}, 0
         for i in seq:
-            q, pre, busy, lat, isd = flat[i]
+            q, pre, busy, lat, isd, kind = flat[i]
             t0 = free[q]
             w = prev.get(q)
             for j, wait in pre:
@@ -147,10 +164,10 @@ def order(ops):
             why[i] = w
             prev[q] = i
             if isd:
-                go[i] = free[q] = t0 + busy
-                d = done[i] = t0 + lat * (f["r"] if q != "s" else 1)
+                go[i] = free[q] = t0 + (busy * f["r"] if q in "rh" else busy)
+                d = done[i] = t0 + lat * (f["r"] if q in "grh" else f["s"])
             else:
-                d = go[i] = free[q] = done[i] = t0 + busy * f[q]
+                d = go[i] = free[q] = done[i] = t0 + (busy * f[q] if not kind else 55 + (busy - 55) * f[q] * f[kind])
             if d > end:
                 end, top = d, i
         if not trace:
@@ -162,7 +179,7 @@ def order(ops):
             top = why[top]
         return path
 
-    flat = [(o["q"], list(o["pre"].items()), o["busy"], o["lat"], o["dma"]) for o in ops]
+    flat = [(o["q"], list(o["pre"].items()), o["busy"], o["lat"], o["dma"], o["kind"]) for o in ops]
     good = None
     rnd = np.random.default_rng(7)
     for turn in range(TURNS):
@@ -207,7 +224,7 @@ def order(ops):
             now = (end, new)
             if end < best[0]:
                 best = now
-    return best[0] / len(CASES), best[1]
+    return best[0] / len(CASES), best[1], [replay(best[1], *c) for c in CASES]
 
 
 def rank_program(g, core, T, topo):
@@ -215,8 +232,9 @@ def rank_program(g, core, T, topo):
     n = len(T.cores)
     if rank is None:
         for r in range(n):
-            if helper(T, topo, r) == core:
-                hand_on(g, core, T, topo, r)
+            for way in sorted({w[3] for w in WRITES if w[3]}):
+                if helper(T, topo, r, way) == core:
+                    hand_on(g, core, T, topo, r, way)
         return
     Q = {"v": g.vector, "a": g.scalar, "p": g.tensor, "g": g, "s": g.sync}
     ops = []
@@ -270,15 +288,15 @@ def rank_program(g, core, T, topo):
             base = 0.5 if all(SCRATCH[x[1]][2] in (BF, F16, U16) for x in outs + ins if size(x) > 1) else 1
         if base == 2 and any(SCRATCH[x[1]][0] == "psum" for x in ins):
             base = 1
-        return FIX + max(64, k * base) * CYC
+        return (FIXA if q == "a" else FIX) + max(64, k * base) * CYC
 
-    def add(q, outs, ins, fn, busy, lat, sem, inc, after=None):
+    def add(q, outs, ins, fn, busy, lat, sem, inc, after=None, done=False):
         dma = sem is not None
         acc = [(o, True) for o in outs] + [(o, False) for o in ins]
         acc += [(o[4], False) for o in outs + ins if len(o) > 4]
         pre = {}
         if after is not None:
-            pre[after] = False
+            pre[after] = done
         me = len(ops)
         for o, wr in acc:
             ps = SCRATCH[o[1]][0] == "psum"
@@ -291,7 +309,8 @@ def rank_program(g, core, T, topo):
                 else:
                     wait = True
                 pre[j] = pre.get(j, False) or wait
-        ops.append({"q": q, "fn": fn, "busy": busy, "lat": lat, "sem": sem, "inc": inc, "pre": pre, "dma": dma})
+        kind = "S" if any(len(o) > 4 for o in outs) else "G" if any(len(o) > 4 for o in ins) else ""
+        ops.append({"q": q, "fn": fn, "busy": busy, "lat": lat, "sem": sem, "inc": inc, "pre": pre, "dma": dma, "kind": kind})
         for o, wr in acc:
             h = hist.setdefault(o[1], [])
             if SCRATCH[o[1]][0] == "psum":
@@ -304,9 +323,9 @@ def rank_program(g, core, T, topo):
     def op(q, outs, ins, fn, base=1):
         ins = [x for x in ins if isinstance(x, tuple)]
         c = cost(q, outs, ins, base)
-        add(q, outs, ins, fn, c, c, None, 1)
+        add(q, outs, ins, fn, c, c, None, 1, prev[0] if q == "g" else None)
 
-    def dma(q, out, in_, after=None):
+    def dma(q, out, in_, after=None, also=None):
         outs = [out] if isinstance(out, tuple) else []
         ins = [in_] if isinstance(in_, tuple) else []
         o = (outs + ins)[0]
@@ -315,6 +334,9 @@ def rank_program(g, core, T, topo):
         by = size(o) * int(o[0].shape[0]) * (2 if SCRATCH[o[1]][2] == BF else 4)
         sent[0] = sent[1]
         sent[1] += by
+        if also is not None:
+            return add(q, outs, ins, lambda: Q[q].dma_start(ap(out), ap(in_)).then_inc(T.sem[sem], 16), 100,
+                       LOC + by / LOCR, sem, 16, hist[also[1]][0][3], True)
         return add(q, outs, ins, lambda: Q[q].dma_start(ap(out), ap(in_)).then_inc(T.sem[sem], 16), 100,
                    LOC + (by + (sent[0] if after is not None else 0)) / LOCR, sem, 16, after)
 
@@ -326,7 +348,9 @@ def rank_program(g, core, T, topo):
         for i in PLAN[m][1]:
             o = ops[i]
             q = o["q"]
-            if q != "r":
+            if q == "g" and o["fn"] is None:
+                continue
+            if q not in "rh":
                 want = {}
                 for j, wait in o["pre"].items():
                     if wait:
@@ -335,7 +359,7 @@ def rank_program(g, core, T, topo):
                 for sem, v in want.items():
                     need(q, sem, v)
             if o["dma"]:
-                if q != "r":
+                if q not in "rh":
                     o["fn"]()
                 val[i] = total[o["sem"]] = o["inc"]
             else:
@@ -394,107 +418,110 @@ def rank_program(g, core, T, topo):
 
     def push_one(i, t, lo, hi, via):
         dst = T.cores[(rank - JUMPS[t]) % n]
-        to = helper(T, topo, rank) if via else dst
+        to = helper(T, topo, rank, via) if via else dst
         rid, pid, _ = topo.addr(to)
-        eng = [e for e in topo.engines(core, to) if not via or e not in topo.engines(core, dst)]
+        eng = first_step(topo, core, to, dst, via)
         src = A("X", O + lo, O + hi)
         arr, snt = "arr%d" % i, "snt%d" % i
         by = (hi - lo) * 256 / LINK
-        ahead = sum((w[2] - w[1]) * 256 / LINK for w in WRITES[:i] if w[0] == t and w[3] == via and w[1] < B0 + (t - 1) * S or w[0] == t == 0)
+        one = by / 4 if via == 3 else by
         me = add("g", [], [src], lambda: g.remote_dma(T["R%d" % t][:, lo:hi], src[0], T.sem[arr], T.sem[snt], pid, rid,
-                                                     sum(1 << e for e in eng)), 300, HOP + by, snt, len(eng), prev[0])
+                                                     sum(1 << e for e in eng)), 300 if i else FIRST, HOP + one,
+                 snt, len(eng), prev[0])
+        if i == 0:
+            for j in range(me):
+                if ops[j]["q"] == "g":
+                    ops[me]["pre"].setdefault(j, False)
         prev[0] = me
         frm = (rank + JUMPS[t]) % n
-        k2 = len(topo.engines(helper(T, topo, frm) if via else T.cores[frm], core))
-        add("r", [A("R%d" % t, lo, hi)], [], None, 0, HOP + by + (HOP + by if via else 0) + ahead * 0.7 - 300, arr, k2, after=me)
+        k2 = len(topo.engines(helper(T, topo, frm, via) if via else T.cores[frm], core))
+        add("h" if via in (1, 2) else "r", [A("R%d" % t, lo, hi)], [], None, one,
+            HOP + one + (HOP + by if via else 0) - 300,
+            arr, k2, after=me)
 
     def col(j):
         return A("COL", j, j + 1)
 
-    d = dma("s", A("X", O, O + B0 // 2), T.lab[:, 0:B0 // 2])
+    cut = WRITES[0][2]
+    for gi in range(6):
+        dma("a", A("COVI", 16 * gi, 16 * gi + 16, rows=(0, 72)), T.cov[gi])
+    d = dma("s", A("X", O, O + cut), T.lab[:, 0:cut])
     d = dma("s", A("WI"), T.wts[:], d)
-    d = dma("s", A("X", O + B0 // 2, O + B0), T.lab[:, B0 // 2:B0], d)
     d = dma("s", A("LFI", 0, 14), T.leaf[:], d)
-    for gi in range(8):
-        c = dma("as"[gi // 6], A("COVI", 16 * gi, 16 * gi + 16, rows=(0, 72)), T.cov[gi], d if gi >= 6 else None)
-        if gi >= 6:
-            d = c
+    for gi in range(6, 8):
+        d = dma("s", A("COVI", 16 * gi, 16 * gi + 16, rows=(0, 72)), T.cov[gi], d)
+    d = dma("s", A("X", O + cut, O + B0), T.lab[:, cut:B0], d)
     if ACT_HOLD[0] < B0:
-        d = dma("s", A("X2", ACT_HOLD[0], B0), T.lab[:, ACT_HOLD[0]:B0], d)
+        act(A("X2", ACT_HOLD[0], B0), A("X", O + ACT_HOLD[0], O + B0), AF.Identity)
     d = dma("s", A("AC"), T.act[:], d)
     d = dma("s", A("PTH"), T.pth[:], d)
 
-    iota(A("IP", 0, 1), [[0, 1]], 0, 1, False)
-    iota(A("IG"), [[1, 9], [0, 16]], 0, 0)
-    iota(A("IC"), [[1, 144]], 0, 0)
+    kinds = sorted(set(VEC_CMP))
+    iota(A("IP", 0, 2), [[16, 2]], 0, 1, False)
+    iota(A("IH"), [[1, 5], [100, 2], [0, 16]], -100, 0)
     ms(A("ONES"), 1.0)
-    asel(A("IDB"), A("ONES", 0, 128), [[-1, 128]], OP.is_equal, 0.0, 0, 1)
-    ts(A("IP", 1, 2), A("IP", 0, 1), 15, OP.bitwise_and)
-    ts(A("IP", 2, 3), A("IP", 0, 1), 4, OP.arith_shift_right)
-    ts(A("IP", 3, 4), A("IP", 0, 1), 4, OP.arith_shift_right, 1, OP.bitwise_and)
-    ts(A("IP", 4, 5), A("IP", 0, 1), 111, OP.bitwise_and)
+    ms(A("ZL", 0, S * len(kinds)), 0.0)
     ms(A("X", 0, O), 512.0)
-    cp(A("COL", 0, 4), A("IP", 1, 5))
-    act(col(5), col(3), AF.Identity, bias=16.0)
-    act(col(3), col(2), AF.Identity, bias=1.0, scale=-1.0)
-    act(col(11), col(1), AF.Identity, bias=col(3))
+    ms(A("CS1"), -10.5 * 65536)
+    ms(A("CS2"), -5.0 * 65536)
+    iota(A("IG"), [[1, 9], [0, 16]], 0, 0)
+    iota(A("IC"), [[1, 16]], 0, 0)
+    asel(A("IDB"), A("ONES", 0, 128), [[-1, 128]], OP.is_equal, 0.0, 0, 1)
+    ts(A("IP", 2, 3), A("IP", 0, 1), 15, OP.bitwise_and)
+    ts(A("IP", 3, 4), A("IP", 0, 1), 4, OP.arith_shift_right)
+    ts(A("IP", 4, 5), A("IP", 0, 1), 5, OP.arith_shift_right)
+    ts(A("IP", 5, 7), A("IP", 0, 2), 4, OP.arith_shift_right, 1, OP.bitwise_and)
+    cp(A("COL", 0, 5), A("IP", 2, 7))
     ts(A("AOF"), A("ONES", 0, 18), col(0), OP.mult)
     for h in range(2):
-        ts(A("XO", 144 * h, 144 * h + 144), A("IG"), col(11), OP.is_equal, col(3 - h), OP.mult)
+        ts(A("XO", 144 * h, 144 * h + 144), A("IH", 0, 144), col(2), OP.is_equal, col(4 - h), OP.mult)
     ts(A("WG"), A("WI"), 2048.0, OP.is_gt, -4096.0, OP.mult)
     tt(A("WS"), A("WI"), A("WG"), OP.add)
     tt(A("LW"), IND(A("WS"), A("AOF")), A("XO"), OP.mult)
-    ts(A("BLK1"), A("IG", 0, 128), col(1), OP.is_equal)
+    ts(A("BLKH"), A("IG"), col(1), OP.is_equal)
     ts(col(9), col(0), 7.0, OP.is_ge, -208.0, OP.mult)
-    asel(A("IDH"), A("ONES", 0, 128), [[-1, 128]], OP.is_equal, 0.0, 0, 1)
-    act(A("BLKM"), A("BLK1"), AF.Identity, scale=float(1 << 23))
+    ts(A("BLKM"), A("IG", 0, 128), col(1), OP.is_equal, float(1 << 23), OP.mult)
     act(A("NIDB"), A("IDB"), AF.Identity, scale=-1.0)
-    act(A("CS2"), A("ONES", 0, 128), AF.Identity, scale=-5.0 * 65536)
-    act(A("CS1"), A("ONES", 0, 128), AF.Identity, scale=-10.5 * 65536)
     act(col(10), col(0), AF.Identity, bias=col(9), scale=32.0)
-    ts(A("ROL"), A("IC", 0, 16), col(10), OP.add, 223.0, OP.min)
-    ts(A("LFU", 0, 14), A("LFI", 0, 14), float(O), OP.add)
+    ts(A("ROL"), A("IC"), col(10), OP.add, 223.0, OP.min)
+    cp(A("LFU", 0, 14), A("LFI", 0, 14))
     ts(A("COVH", rows=(0, 72)), A("COVI", rows=(0, 72)), float(O), OP.add)
-    mm(A("PM", 0, 72), A("COVH", rows=(0, 72)), A("IDH", 0, 72, rows=(0, 72)))
+    mm(A("PM", 0, 72), A("COVH", rows=(0, 72)), A("IDB", 0, 72, rows=(0, 72)))
     cp(A("COVL", 0, 72), A("PM", 0, 72))
-    cp(A("LF0", 0, 14), A("LFI", 0, 14))
-    for h in range(2):
-        ts(A("XH", 144 * h, 144 * h + 144), A("IC"), col(5), OP.is_equal, col(3 - h), OP.mult)
-    act(col(4), col(1), AF.Identity, bias=15.0, scale=16.0)
-    ts(A("SELB"), A("IC"), col(4), OP.is_equal)
-    act(A("XP", 0, O), A("ONES", 0, O), AF.Identity)
     act(col(6), col(0), AF.Identity, bias=1.0)
     act(col(7), col(0), AF.Identity, bias=17.0)
-    act(col(8), col(0), AF.Identity, bias=4096.0, scale=-4096.0)
     act(col(12), col(0), AF.Identity, bias=-4096.0, scale=-2048.0)
-    act(A("BLKT"), A("BLK1"), AF.Identity, scale=-2048.0)
-    act(A("SELN"), A("SELB"), AF.Identity, scale=-128.0)
-    act(A("NI2"), A("IDB"), AF.Identity, scale=-2048.0)
-    act(A("PI2"), A("IDB"), AF.Identity, scale=2048.0)
-    act(A("SEL2"), A("SELB"), AF.Identity, scale=2.0)
+    act(A("BLKT"), A("BLKM"), AF.Identity, scale=-1.0 / 4096)
+    act(A("CA"), A("IDB"), AF.Identity, bias=1024.0, scale=CADD - 131072.0)
 
     push(len([w for w in WRITES if w[0] == 0]))
+    prev[0] = add("g", [], [], None, HOLD, HOLD, None, 0, prev[0])
+    ms(A("XH"), 0.0)
+    ms(A("SELB"), 0.0)
+    for h in range(2):
+        act(A("XH", 16 + 128 * h, 144 + 128 * h), A("IDB"), AF.Identity, scale=col(4 - h))
+    cp(A("SELB", 15, 128, 16), A("BLKH", 15, 128, 16))
+    if any(PE_HASH):
+        for m in range(2):
+            ts(A("WL%d" % m), A("SELB"), A("WS", m, m + 1), OP.mult)
     iota(A("IA"), [[0, 14], [1, 16]], 0, 0)
     iota(A("IJ"), [[16, 48]], B0 - 2048, 0)
+    act(col(8), col(0), AF.Identity, bias=4096.0, scale=-4096.0)
     act(A("MASKD"), A("IA"), AF.Relu, bias=col(8), scale=4096.0)
-    act(A("NEWL", 0, 42), A("IJ", 0, 42), AF.Identity, bias=col(0))
-    asel(A("NEWH", 0, 42), A("NEWL", 0, 42), [[1, 42]], OP.is_ge, 0.0, 0, 0)
-    asel(A("LF", 0, 14), A("LFI", 0, 14), [[1, 14]], OP.is_ge, 0.0, 0, 0)
+    act(A("SELN"), A("SELB"), AF.Identity, scale=-128.0)
+    ts(A("NEWH", 0, 42), A("IJ", 0, 42), col(0), OP.add)
     asel(A("TRI"), A("BLKT"), [[1, 128]], OP.is_gt, 0.0, 0, -1)
     asel(A("TRI"), A("TRI"), [[1, 128]], OP.not_equal, 2048.0, 0, -1)
-    asel(A("SELH"), A("SELB"), [[1, 144]], OP.is_ge, 0.0, 0, 0)
-    asel(A("BLKH"), A("BLK1"), [[1, 128]], OP.is_ge, 0.0, 0, 0)
-    kinds = sorted(set(VEC_CMP))
-    ms(A("ZL", 0, S * len(kinds)), 0.0)
-    for i, k in enumerate(kinds):
-        ts(col(13 + i), col(0), 16.0 - k, OP.is_ge, -16.0, OP.mult)
-        act(A("ZL", S * i + S - 1, S * i + S), col(13 + i), AF.Identity, bias=-8.5)
+    asel(A("NI2"), A("ZL", 0, 128), [[1, 128]], OP.not_equal, -2048.0, 0, -1)
+    asel(A("PI2"), A("ZL", 0, 128), [[1, 128]], OP.not_equal, 2048.0, 0, -1)
     asel(A("RST"), A("ONES", 0, 336), [[0, 21], [1, 16]], OP.is_equal, 0.0, 0, 0)
-    asel(A("SHF"), A("BLK1"), [[1, 128]], OP.is_equal, 0.0, -1, -1)
+    asel(A("LF", 0, 14), A("LFI", 0, 14), [[1, 14]], OP.is_ge, 0.0, 0, 0)
+    for i, k in enumerate(kinds):
+        ts(col(13 + i), col(0), 16.0 - k, OP.is_ge, 1.0, OP.add)
+        act(A("ZL", S * i + S - 1, S * i + S), col(13 + i), AF.Identity, bias=7.5, scale=-16.0)
+    asel(A("SHF"), A("BLKH", 0, 128), [[1, 128]], OP.is_equal, 0.0, -1, -1)
     asel(A("E0"), A("IDB"), [[0, 8], [1, 16]], OP.is_equal, 0.0, 0, 0)
-    iota(A("IS"), [[1, 672]], B0, 0)
-    asel(A("NEWN"), A("IS"), [[1, 672]], OP.is_ge, 0.0, 0, 0)
-    asel(A("G8"), A("BLK1", 0, 128, 16), [[1, 8]], OP.is_ge, 0.0, 0, 0)
+
 
     def cross(name, h, rho):
         return A(name, 144 * h + 16 - 16 * rho, 144 * h + 144 - 16 * rho)
@@ -514,7 +541,7 @@ def rank_program(g, core, T, topo):
         for h in range(2):
             mms(px(h), *[(cross("XH", h, rho), half("PV", rho)) for rho in range(2)])
         tr(A("TOP"), PXA)
-        ts(A("POF"), IND(A("TOP", 0, 224), A("ROL", 0, 16)), float(O), OP.add)
+        cp(A("POF"), IND(A("TOP", 0, 224), A("ROL", 0, 16)))
 
     def hold_v(lo, hi, bank):
         own = A("X2", lo, hi) if lo < B0 else A("X", O + lo, O + hi)
@@ -522,7 +549,7 @@ def rank_program(g, core, T, topo):
         mms(bk(bank, hi - lo), (A("CS1"), A("ONES", 0, hi - lo)), (A("BLKM"), A("CMP", lo, hi)))
 
     def hold_max(lo, hi, bank):
-        tt(A("XP", O + lo, O + hi), bk(bank, hi - lo), A("X", O + lo, O + hi), OP.max)
+        tt(A("XP", lo, hi), bk(bank, hi - lo), A("X", O + lo, O + hi), OP.max)
 
     def hold_a(lo, hi, bank):
         act(A("XC", lo, hi), IND(A("X", 0, O + B0), A("COVL", lo // 16, hi // 16)), AF.Identity)
@@ -533,7 +560,7 @@ def rank_program(g, core, T, topo):
     def sel_list(selname, src, lo=0):
         return [(A(selname, 15 - a, 143 - a), A(src, lo + a, lo + S, 16)) for a in range(16)]
 
-    ts(A("PV"), IND(A("PTH", 0, B0), A("LF0", 0, 14)), 0.0, OP.add)
+    cp(A("PV"), IND(A("PTH", 0, B0), A("LFU", 0, 14)))
     for t in range(RO):
         b = B0 + t * S
         last = t == RO - 1
@@ -541,23 +568,31 @@ def rank_program(g, core, T, topo):
         na = ACT_HOLD[t]
         old = b - S if t else b
         Z, SUS, CI, xk = A("Z", S * t, S * t + S), A("SUS", S * t, S * t + S), A("CI", S * t, S * t + S), 3584 * (t & 1)
-        act(A("XV"), IND(XB, A("LFU", 0, 14)), AF.Identity)
-        for h in range(2):
-            mms(px(h), *[(cross("LW", h, rho), half("XV", rho)) for rho in range(2)])
-        tr(A("TOH"), PXA)
+        iota(A("IS", S * t, S * t + S), [[1, S]], b, 0)
+        asel(A("NEWN", S * t, S * t + S), A("IS", S * t, S * t + S), [[1, S]], OP.is_ge, 0.0, 0, 0)
+        act(A("XV"), IND(A("X", O, O + b), A("LFU", 0, 14)), AF.Identity)
+        if PE_HASH[t]:
+            for m in range(2):
+                mms(M("PX", ALL, 0, m, slice(0, 14)), *sel_list("WL%d" % m, "XV"))
+            cp(M("HI3", ALL, ALL, slice(0, 14)), M("PX", ALL, 0, ALL, slice(0, 14)))
+        else:
+            for h in range(2):
+                mms(px(h), *[(cross("LW", h, rho), half("XV", rho)) for rho in range(2)])
+            tr(A("TOH"), PXA)
+            cp(A("HI"), IND(A("TOH", 0, 224), A("ROL", 0, 2)))
         if t == 0:
             path_list()
-        cp(A("HI"), IND(A("TOH", 0, 224), A("ROL", 0, 2)))
-        ts(A("HA", 0, 14), A("HI", 0, 14), DA - 1, OP.bitwise_and)
-        ts(A("HQ", 0, 14), A("HI", 16, 30), 4095, OP.bitwise_and)
+        hi = [M("HI3", ALL, m, slice(0, 14)) if PE_HASH[t] else A("HI", 16 * m, 16 * m + 14) for m in range(2)]
+        ts(A("HA", 0, 14), hi[0], DA - 1, OP.bitwise_and)
+        ts(A("HQ", 0, 14), hi[1], 4095, OP.bitwise_and)
         cp(A("AL", 0, 14), A("HA", 0, 14))
         ts(A("QL", 0, 14), A("HQ", 0, 14), b / 4096.0, OP.mult, FLOOR, OP.add)
         if na:
             hold_a(0, min(na, 512), "PH0")
             hold_max(0, min(na, 512), "PH0")
         if na > 512:
-            hold_a(512, na, "PX")
-            hold_max(512, na, "PX")
+            hold_a(512, na, "PX" if t else "PD0")
+            hold_max(512, na, "PX" if t else "PD0")
         for lo, hi in [(x, min(x + 512, B0)) for x in range(na, B0, 512)] + [(x, x + S) for x in range(B0, old, S)]:
             hold_v(lo, hi, "PP")
             hold_max(lo, hi, "PP")
@@ -573,34 +608,57 @@ def rank_program(g, core, T, topo):
             hold_v(old, b, "PM")
             hold_max(old, b, "PM")
 
-        for c in range(0, S, 28):
-            o = A("XK", xk + 16 * c, xk + 16 * c + 448)
-            if c >= S - 28 * VEC_GAT[t]:
-                cp(o, IND(XB, A("COF", c, c + 28)))
-            else:
-                act(o, IND(XB, A("COF", c, c + 28)), AF.Identity)
-        if ON_ACT[t][0]:
+        src = XB
+        if SNAP[t]:
+            src = A("XS", 0, O + b)
+            asel(src, XB, [[1, O + b]], OP.is_ge, 0.0, 0, 0)
+        for c in range(0, S, GW):
+            act(A("XK", xk + 16 * c, xk + 16 * (c + GW)), IND(src, A("COF", c, c + GW)), AF.Identity)
+        if ON_ACT[t]:
             act(A("CE"), IND(A("R%d" % t, 0, b), A("QL", 0, 14)), AF.Identity, bias=CADD, scale=-1.0)
         else:
             ts(A("CE"), IND(A("R%d" % t, 0, b), A("QL", 0, 14)), -1.0, OP.mult, CADD, OP.add)
-        act(A("E"), A("CE"), AF.Identity, bias=CADD, scale=-1.0)
+        if LISTS_FIRST:
+            ops[-1]["pre"].setdefault(hist["COF"][0][3], False)
+        if "E" in ON_VEC:
+            ts(A("E"), A("CE"), -1.0, OP.mult, CADD, OP.add)
+        else:
+            act(A("E"), A("CE"), AF.Identity, bias=CADD, scale=-1.0)
         if t:
-            act(A("EM"), A("CE"), AF.Relu, bias=CADD - 255.0, scale=-1.0)
-        for k in range(15, -1, -1):
-            win = A("XP", 0, O + B0 + S * max(0, t - k))
-            tt(A("PO", S * k, S * k + S), IND(win, A("POF", 16 * k, 16 * k + 14)), A("CE"), OP.add)
-            mm(A("PP", 0, 224), A("SELB", 15 - k, 143 - k), A("PO", S * k, S * k + S), k == 15, k == 0)
-        ts(A("LOW"), A("PP", 0, 224), 2097152.0 + 7.5 * 1024, OP.is_lt, 2.0, OP.mult)
+            ts(A("EM"), A("E"), 255.5, OP.is_gt)
+            dma("s", T.yp[:, S * t - S:S * t], A("YP", S * t - S, S * t), also=A("CE"))
+        nv = 16 - ACT_PATH[t]
+        if nv < 16:
+            mms(bk("PH0", 224), (A("CA"), A("ONES", 0, 224)), (A("NIDB"), A("E")))
+        ks = list(range(nv - 1, t - 1, -1)) + list(range(15, nv - 1, -1)) + list(range(t - 1, -1, -1))
+        for k in ks:
+            src = IND(A("XP", 0, B0 + S * max(0, t - k)), A("POF", 16 * k, 16 * k + 14))
+            if k < nv:
+                tt(A("PO", S * k, S * k + S), src, A("CE"), OP.add)
+            else:
+                act(A("XG", S * k, S * k + S), src, AF.Identity)
+                tt(A("PO", S * k, S * k + S), A("XG", S * k, S * k + S), bk("PH0", 224), OP.add)
+            mm(A("PP", 0, 224), A("SELB", 15 - k, 143 - k), A("PO", S * k, S * k + S), k == ks[0], k == ks[-1])
+        ts(A("LOW"), A("PP", 0, 224), LOWT, OP.is_lt, 2.0, OP.mult)
         ts(A("HLD"), A("PP", 0, 224), 8388608.0, OP.is_ge, 2.0, OP.mult)
-        mms(A("PM", 0, 224), (A("IDH"), A("PV")), *([(A("BLKT"), A("EM"))] if t else []),
+        mms(A("PM", 0, 224), (A("IDB"), A("PV")), *([(A("BLKT"), A("EM"))] if t else []),
             (A("TRI"), A("LOW")), (A("BLKT"), A("HLD")))
-        mm(A("PP", 0, 224), A("BLK1"), A("HLD"))
+        mm(A("PP", 0, 224), A("BLKM"), A("HLD"))
         ts(A("SH"), A("PM", 0, 224), O - 4096.0, OP.add, 0.0, OP.max)
-        act(SUS, A("PP", 0, 224), AF.Sign, bias=-0.5)
+        if "SUS" in ON_VEC:
+            ts(SUS, A("PP", 0, 224), -1.0, OP.add, 1.0, OP.min)
+        else:
+            act(SUS, A("PP", 0, 224), AF.Sign, bias=-0.5)
+        mms(bk("PH0", 224), (A("IDB"), Z), (A("BLKM"), A("HLD")))
+        ts(A("X", O + b, O + b + S), bk("PH0", 224), 256.0, OP.min)
+        if not last:
+            push(len([w for w in WRITES if w[0] == t + 1 and w[1] >= b]))
+        else:
+            dma("s", T.yx[:, b:W], A("X", O + b, O + W))
         for h in range(2):
             mms(px(h), *[(cross("XO", h, rho), M("SH", ALL, ALL, rho, ALL)) for rho in range(2)])
-        mms(bk("PH0", 224), (A("IDB"), A("MASKD")), (A("BLKH"), A("SH")))
-        mm(M("PH0", ALL, slice(7, 14), 0, ALL), A("BLKH"), M("SH", ALL, ALL, 0, ALL))
+        mms(bk("PH0", 224), (A("IDB"), A("MASKD")), (A("BLKH", 0, 128), A("SH")))
+        mm(M("PH0", ALL, slice(7, 14), 0, ALL), A("BLKH", 0, 128), M("SH", ALL, ALL, 0, ALL))
         tr(A("TGX"), PXA)
         tt(A("EQ", 0, 224), bk("PH0", 224), A("TGX"), OP.not_equal)
         tt(A("EQ", 224, 336), M("PH0", ALL, slice(7, 14), 0, ALL), M("TGX", ALL, ALL, 1, ALL), OP.not_equal)
@@ -611,35 +669,40 @@ def rank_program(g, core, T, topo):
         ts((T.OFU[:, 1:14:2], "OFU", 0, 14), A("OFF", 16, 23), col(7), OP.max)
         cp(A("TGU", 0, 14), M("TGX", ALL, ALL, ALL, 0))
         tt(A("V"), IND(XB, A("TGU", 0, 14)), A("E"), OP.max)
-        mms(A("PM", 0, 224), (A("IDB"), Z), (A("PI2"), SUS))
-        ts(A("X", O + b, O + b + S), A("PM", 0, 224), 2048.0, OP.add, 256.0, OP.min)
-        if not last:
-            push(1)
-        else:
-            dma("s", T.yx[:, b:W], A("X", O + b, O + W))
         scan(A("SGN", S * t, S * t + S), SUS, A("ZL", S * kinds.index(VEC_CMP[t]), S * kinds.index(VEC_CMP[t]) + S),
              1.0, OP.mult, OP.add)
-        mms(A("PP", 448, 462), (A("IDH"), A("NEWH", 14 * t, 14 * t + 14)), *sel_list("SELN", "SUS", S * t))
+        mms(A("PP", 448, 462), (A("IDB"), A("NEWH", 14 * t, 14 * t + 14)), *sel_list("SELN", "SUS", S * t))
         mms(A("PP", 224, 448), (A("E0"), A("NEWN", S * t, S * t + S)), (A("SHF"), A("PV")), (A("NI2"), SUS))
         if not last:
-            mms(A("PP", 0, 224), (A("NI2"), A("ONES", 0, 224)), (A("IDH"), A("PV")), (A("PI2"), SUS))
+            mms(A("PP", 0, 224), (A("NI2"), A("ONES", 0, 224)), (A("IDB"), A("PV")), (A("PI2"), SUS))
         tt(A("YV" if last else "LF", 0, 14), A("PP", 448, 462), A("LF", 0, 14), OP.max)
-        act(A("YP", S * t, S * t + S), A("PP", 224, 448), AF.Relu, bias=-2048.0)
-        dma("s", T.yp[:, S * t:S * t + S], A("YP", S * t, S * t + S))
+        if "YP" in ON_VEC:
+            ts(A("YP", S * t, S * t + S), A("PP", 224, 448), -2048.0, OP.add, 0.0, OP.max)
+        else:
+            act(A("YP", S * t, S * t + S), A("PP", 224, 448), AF.Relu, bias=-2048.0)
+        if last:
+            dma("s", T.yp[:, S * t:S * t + S], A("YP", S * t, S * t + S))
         if not last:
-            ts(A("LFU", 0, 14), A("LF", 0, 14), float(O), OP.add)
+            cp(A("LFU", 0, 14), A("LF", 0, 14))
             tt(A("PV"), A("PP", 0, 224), A("YP", S * t, S * t + S), OP.max)
             path_list()
         for bb in range(12, -1, -2):
             cp(IND(XB, (T.OFU[:, bb:bb + 2], "OFU", 0, 15)), A("V", 16 * bb, 16 * bb + 32))
         if not last:
-            push(len([w for w in WRITES if w[0] == t + 1]) - 1)
+            push(len([w for w in WRITES if w[0] == t + 1 and w[1] < b]))
             lo = ACT_HOLD[t + 1]
-            if lo < B0:
+            if lo < B0 and COPY_ON == "v":
+                cp(A("X2", lo, B0), A("X", O + lo, O + B0))
+            elif lo < B0 and COPY_ON == "s":
+                dma("s", A("X2", lo, B0), A("X", O + lo, O + B0))
+            elif lo < B0 and COPY_ON == "a":
+                act(A("X2", lo, B0), A("X", O + lo, O + B0), AF.Identity)
+            elif lo < B0:
                 asel(A("X2", lo, B0), A("X", O + lo, O + B0), [[1, B0 - lo]], OP.is_ge, 0.0, 0, 0)
         else:
-            dma("s", T.yx[:, 0:b // 2], A("X", O, O + b // 2))
-            dma("a", T.yx[:, b // 2:b], A("X", O + b // 2, O + b))
+            sent[1] = 0
+            d = dma("s", T.yx[:, 0:b // 2], A("X", O, O + b // 2))
+            dma("s", T.yx[:, b // 2:b], A("X", O + b // 2, O + b), d)
             dma("s", T.yv[:], A("YV", 0, 14))
         ns = 16 - VEC_CMP[t]
         if ns < 16:
@@ -659,15 +722,19 @@ def rank_program(g, core, T, topo):
                 act(sg(m, k), A(bank, 0, 112 * k), AF.Sign, bias=0.5)
             for m in range(ns, 16):
                 tt(sg(m), xm(m), half("PH1", hf), OP.is_le)
-            mms(half("PC", hf), *[(A("SELB" if m < ns else "SEL2", 15 - m, 143 - m), sg(m)) for m in range(16)])
-        act(A("FIT"), A("PC", 0, 224), AF.Sign, bias=A("SGN", S * t + S - 1, S * t + S))
-        mms(A("PC", 224, 448), (A("IDH"), CI), (A("NI2"), SUS), (A("TRI"), A("FIT")))
+            mms(half("PC", hf), *[(A("SELB", 15 - m, 143 - m), sg(m)) for m in range(16)])
+        act(A("FIT"), A("PC", 0, 224), AF.Sign, bias=A("SGN", S * t + S - 1, S * t + S),
+            scale=col(13 + kinds.index(VEC_CMP[t])))
+        mms(A("PC", 224, 448), (A("IDB"), CI), (A("NI2"), SUS), (A("TRI"), A("FIT")))
         ts(A("SH2"), A("PC", 224, 448), col(12), OP.add, 0.0, OP.max)
         if not last:
-            mms(A("PC", 448, 462), *sel_list("SELH", "SH2"))
-        mm(A("PC", 0, 224, rows=(0, 8)), A("G8"), A("SH2"))
+            mms(A("PC", 448, 462), *sel_list("SELB", "SH2"))
+        mm(A("PC", 0, 224, rows=(0, 8)), A("BLKH", 0, 128, 16), A("SH2"))
         if not last:
             ts(A("COVL", 72 + 14 * t, 86 + 14 * t), A("PC", 448, 462), O - 1.0, OP.add)
-        act(A("YC", S * t, S * t + S, rows=(0, 8)), A("PC", 0, 224, rows=(0, 8)), AF.Identity, bias=-1.0)
+        if "YC" in ON_VEC or last and "YC2" in ON_VEC:
+            ts(A("YC", S * t, S * t + S, rows=(0, 8)), A("PC", 0, 224, rows=(0, 8)), -1.0, OP.add)
+        else:
+            act(A("YC", S * t, S * t + S, rows=(0, 8)), A("PC", 0, 224, rows=(0, 8)), AF.Identity, bias=-1.0)
     dma("s", T.yc[:], A("YC", rows=(0, 8)))
     emit()

import numpy as np
from concourse.mybir import AluOpType, ActivationFunctionType

OP = AluOpType
AF = ActivationFunctionType
B0, S, RO, DA = 1152, 224, 3, 512
JUMPS = [1, 5, 3]
W = B0 + RO * S
O = 48
XW = O + W
CADD = 131072.0 + 1536.0
LOWT = 16 * (131072.0 + 1024.0) + 7.5 * 1024
FLOOR = -0.49609375
MAGIC = 1.5 * 2 ** 23
ACT_HOLD = [640, 512, 512]
VEC_CMP = [8, 8, 8]
ACT_PATH = [5, 5, 5]
ON_VEC = ["SUS", "YC2"]
COPY_ON = "v"
LISTS_FIRST = 0
PE_HASH = [0, 0, 0]
GW = 56
SNAP = [0, 0, 0]
ON_ACT = [1, 1, 1]
LINK, FIRST, HOLD = 90.0, 1200.0, 5000.0
WRITES = [(0, 0, 384, 0), (0, 384, B0, 0),
          (1, B0, B0 + S, 1), (1, 0, 208, 1), (1, 352, B0, 0), (1, 208, 352, 1),
          (2, B0 + S, B0 + 2 * S, 1), (2, 0, 256, 1), (2, 432, B0 + S, 0), (2, 256, 432, 1)]

BF, F32, F16, I32, U16 = "bfloat16", "float32", "float16", "int32", "uint16"
SB = {
    "X": ([128, XW], BF), "X2": ([128, B0], BF), "XS": ([128, XW], BF), "XP": ([128, W - S], BF), "R0": ([128, B0], BF), "R1": ([128, B0 + S], BF),
    "R2": ([128, B0 + 2 * S], BF), "AC": ([128, DA], BF), "PTH": ([128, B0], I32), "COVI": ([128, 128], I32),
    "COVH": ([128, 128], F16), "COVL": ([128, 128], U16), "WI": ([128, 16], I32), "WG": ([128, 16], F32),
    "WS": ([128, 16], F32), "LW": ([128, 288], F16), "LFI": ([128, 16], I32), "IH": ([128, 160], F32),
    "LF": ([128, 16], F32), "LFU": ([128, 16], U16), "AOF": ([128, 18], U16),
    "IP": ([128, 8], I32), "COL": ([128, 16], F32), "IC": ([128, 16], F32), "IG": ([128, 144], F32),
    "IS": ([128, 672], F32), "IA": ([128, 224], F32), "IJ": ([128, 48], F32),
    "ROL": ([128, 16], U16), "SELB": ([128, 144], BF), "SELN": ([128, 144], BF),
    "PI2": ([128, 128], BF), "CA": ([128, 128], BF), "BLKM": ([128, 128], BF), "CS1": ([128, 128], BF),
    "CS2": ([128, 128], BF), "ONES": ([128, 512], BF), "TRI": ([128, 128], BF), "IDB": ([128, 128], BF),
    "NIDB": ([128, 128], BF), "NI2": ([128, 128], BF), "E0": ([128, 128], F16),
    "SHF": ([128, 128], F16), "XH": ([128, 288], BF),
    "HLD": ([128, 224], BF), "BLKT": ([128, 128], BF),
    "NEWN": ([128, 672], F16), "MASKD": ([128, 224], BF),
    "ZL": ([128, 672], BF), "NEWH": ([128, 48], F16),
    "XO": ([128, 288], F16), "BLKH": ([128, 144], F16), "TGX": ([128, 7, 2, 16], F32),
    "XV": ([128, 224], BF), "PV": ([128, 224], F16), "TOH": ([128, 224], F32),
    "TOP": ([128, 224], F32), "HI": ([128, 32], I32), "HI3": ([128, 2, 16], I32), "WL0": ([128, 144], F16), "WL1": ([128, 144], F16),
    "HA": ([128, 16], I32), "HQ": ([128, 16], I32),
    "AL": ([128, 16], U16), "QL": ([128, 16], U16), "POF": ([128, 256], U16), "DZ": ([128, 224], BF), "Z": ([128, 672], BF),
    "ZI": ([128, 224], I32), "ZJ": ([128, 224], I32), "COF": ([128, 224], U16), "CI": ([128, 672], F16),
    "CMP": ([128, W - S], BF), "XC": ([128, 1024], BF), "CE": ([128, 224], F32), "E": ([128, 224], BF), "EM": ([128, 224], BF),
    "PO": ([128, 3584], BF), "XG": ([128, 3584], BF), "XK": ([128, 7168], BF), "SG": ([128, 3584], BF), "LOW": ([128, 224], BF), "SUS": ([128, 672], BF),
    "SH": ([128, 7, 2, 16], F16), "FIT": ([128, 224], BF), "SH2": ([128, 224], F16),
    "EQ": ([128, 336], BF), "SC": ([128, 336], BF), "RST": ([128, 336], BF), "OFF": ([128, 24], F32),
    "OFU": ([128, 16], U16), "TGU": ([128, 16], U16), "V": ([128, 224], BF), "SGN": ([128, 672], BF),
    "YP": ([128, 672], F32), "YC": ([128, 672], F32), "YV": ([128, 16], F32),
}
SCRATCH = {k: ("sbuf", v[0], v[1]) for k, v in SB.items()}
for _n in ("PH1", "PD0", "PD1", "PC", "PP", "PM"):
    SCRATCH[_n] = ("psum", [128, 512], F32)
SCRATCH["PH0"] = ("psum", [128, 16, 2, 16], F32)
SCRATCH["PX"] = ("psum", [128, 16, 2, 16], F32)
NDMA = 32
SEMAPHORES = (["cv", "ca", "cp", "cg"] + ["arr%d" % i for i in range(len(WRITES))] + ["snt%d" % i for i in range(len(WRITES))]
              + ["d%d" % i for i in range(NDMA)])
BIG = 1 << 30
PLAN = {}
CASES = [(dict(zip("vapgsrGS", f)), w) for f, w in (((0.9, 0.9, 0.9, 1, 0.7, 1.0, 0.8, 1.2), 150.0),
                                                    ((0.9, 1.05, 0.9, 1, 1, 1.2, 1.0, 1.0), 200.0),
                                                    ((1, 0.85, 1.2, 1, 1, 0.8, 1.2, 0.6), 90.0),
                                                    ((0.85, 0.85, 0.8, 1, 1.3, 1.6, 1.0, 1.0), 250.0),
                                                    ((1, 1, 1, 1, 1, 1.2, 1.33, 1.4), 120.0),
                                                    ((0.85, 1.0, 1.1, 1, 0.8, 1.0, 0.75, 1.0), 120.0),
                                                    ((1, 0.9, 0.8, 1, 1.2, 1.3, 1.1, 0.8), 60.0))]
SWAPS, HEAT = 14000, 800.0
TURNS = 150
SLACKS, SHAKE = ((0.0, 0.0), (130.0, 0.0), (300.0, 0.0), (130.0, 130.0), (300.0, 130.0), (300.0, 60.0)), (700.0, 600.0, 2000.0, 1200.0, 5000.0)
HOP, LOC, LOCR = 1100.0, 1300.0, 230.0
CYC, PE, FIX, FIXA, WAKE = 0.94, 0.53, 20.0, 150.0, 120.0


def helper(T, topo, rank, via):
    core, n = T.cores[rank], len(T.cores)
    return [c for c in topo.cores_of(core) if (topo.die(c) == topo.die(core)) == (via == 3) and T.rank_of(c) is None
            and all(topo.may_write(c, T.cores[(rank - j) % n]) for j in JUMPS)][(via - 1) % 2]


def first_step(topo, src, to, dst, via):
    return [e for e in topo.engines(src, to) if (e in topo.engines(src, dst)) == (via in (0, 3))]


def hand_on(g, core, T, topo, rank, way):
    n = len(T.cores)
    VIA = [(i, t, lo, hi) for i, (t, lo, hi, via) in enumerate(WRITES) if via == way]
    for i, t, lo, hi in VIA:
        dst = T.cores[(rank - JUMPS[t]) % n]
        src = T.cores[rank]
        k = len(first_step(topo, src, core, dst, way))
        rid, pid, _ = topo.addr(dst)
        g.wait_ge(T.sem["arr%d" % i], k)
        g.remote_dma(T["R%d" % t][:, lo:hi], T["R%d" % t][:, lo:hi], T.sem["arr%d" % i], T.sem["snt%d" % i], pid, rid,
                     topo.mask(core, dst))
    for i, t, lo, hi in VIA:
        g.wait_ge(T.sem["snt%d" % i], len(topo.engines(core, T.cores[(rank - JUMPS[t]) % n])))


def order(ops):
    m = len(ops)
    nxt = [[] for _ in ops]
    for i, o in enumerate(ops):
        for j in o["pre"]:
            nxt[j].append(i)

    def plan(prio, back, slack):
        out = [list(o["pre"]) for o in ops] if back else nxt
        left = [len(nxt[i]) if back else len(ops[i]["pre"]) for i in range(m)]
        can = [ops[i]["lat"] - ops[i]["busy"] if back else 0.0 for i in range(m)]
        ready = {q: [] for q in "vapgsrh"}
        free = {q: 0.0 for q in ready}
        for i in range(m):
            if not left[i]:
                ready[ops[i]["q"]].append(i)
        seq, at, end = [], [0.0] * m, 0.0
        for _ in range(m):
            best = None
            for q, r in ready.items():
                if r:
                    t0 = max(free[q], min([can[i] for i in r]))
                    if best is None or t0 < best[0]:
                        best = (t0, q)
            t0, q = best
            i = min([i for i in ready[q] if can[i] <= t0 + slack[q == "v"]], key=lambda i: prio[i])
            o = ops[i]
            ready[q].remove(i)
            t0 = max(free[q], can[i])
            free[q] = t0 + o["busy"]
            at[i] = free[q] if back else t0
            end = max(end, t0 + o["lat"])
            seq.append(i)
            for k in out[i]:
                if back:
                    d = at[i] + (ops[k]["lat"] + WAKE - ops[k]["busy"] if o["pre"][k] else 0)
                else:
                    d = t0 + (o["lat"] + WAKE if ops[k]["pre"][i] else o["busy"])
                can[k] = max(can[k], d)
                left[k] -= 1
                if not left[k]:
                    ready[ops[k]["q"]].append(k)
        return seq, at, end

    def replay(seq, f, wake, trace=False):
        free, done, go, end = {q: 0.0 for q in "vapgsrh"}, [0.0] * m, [0.0] * m, 0.0
        why, prev, top = [None] * m, {}, 0
        for i in seq:
            q, pre, busy, lat, isd, kind = flat[i]
            t0 = free[q]
            w = prev.get(q)
            for j, wait in pre:
                d = done[j] + wake if wait else go[j]
                if d > t0:
                    t0, w = d, j
            why[i] = w
            prev[q] = i
            if isd:
                go[i] = free[q] = t0 + (busy * f["r"] if q in "rh" else busy)
                d = done[i] = t0 + lat * (f["r"] if q in "grh" else f["s"])
            else:
                d = go[i] = free[q] = done[i] = t0 + (busy * f[q] if not kind else 55 + (busy - 55) * f[q] * f[kind])
            if d > end:
                end, top = d, i
        if not trace:
            return end
        path = []
        while why[top] is not None:
            if why[top] not in ops[top]["pre"]:
                path.append((why[top], top))
            top = why[top]
        return path

    flat = [(o["q"], list(o["pre"].items()), o["busy"], o["lat"], o["dma"], o["kind"]) for o in ops]
    good = None
    rnd = np.random.default_rng(7)
    for turn in range(TURNS):
        slack = SLACKS[turn % len(SLACKS)]
        if turn < len(SLACKS):
            prio = list(range(m))
        else:
            t1 = rnd.random() * good[0]
            w = (rnd.random(m) - 0.5) * SHAKE[turn % len(SHAKE)] * (rnd.random(m) < 0.3)
            prio = [x + (y if t1 - 4000 < z < t1 + 4000 else 0) for x, y, z in zip(good[3], w.tolist(), good[2])]
            slack = good[4] if turn % 7 else slack
        for k in range(6 if turn < len(SLACKS) else 2 if turn % 5 == 0 else 1):
            if k:
                prio = [-x for x in plan([-x for x in at], True, slack)[1]]
            seq, at, end = plan(prio, False, slack)
            if good is not None and end > 1.06 * good[0]:
                continue
            end = (end + sum(replay(seq, *c) for c in CASES)) / (1 + len(CASES))
            if good is None or end <= good[0]:
                good = (end, seq, at, prio if k or turn >= len(SLACKS) else at, slack)
    best = now = (sum(replay(good[1], *c) for c in CASES), good[1])
    for turn in range(SWAPS):
        seq = now[1]
        path = replay(seq, *CASES[turn % len(CASES)], True)
        if not path:
            continue
        i, j = path[int(rnd.integers(len(path)))]
        a, b = seq.index(i), seq.index(j)
        for _ in range(int(rnd.integers(3))):
            e = [x for x in range(a - 1, max(a - 40, -1), -1) if ops[seq[x]]["q"] == ops[j]["q"]]
            a = e[0] if e else a
        lift = {j}
        for x in range(b - 1, a - 1, -1):
            if any(k in lift for k in nxt[seq[x]]):
                lift.add(seq[x])
        if seq[a] in lift:
            continue
        mid = seq[a:b + 1]
        new = seq[:a] + [x for x in mid if x in lift] + [x for x in mid if x not in lift] + seq[b + 1:]
        end = sum(replay(new, *c) for c in CASES)
        if end <= now[0] + HEAT * (1 - turn / SWAPS) * rnd.random():
            now = (end, new)
            if end < best[0]:
                best = now
    return best[0] / len(CASES), best[1], [replay(best[1], *c) for c in CASES]


def rank_program(g, core, T, topo):
    rank = T.rank_of(core)
    n = len(T.cores)
    if rank is None:
        for r in range(n):
            for way in sorted({w[3] for w in WRITES if w[3]}):
                if helper(T, topo, r, way) == core:
                    hand_on(g, core, T, topo, r, way)
        return
    Q = {"v": g.vector, "a": g.scalar, "p": g.tensor, "g": g, "s": g.sync}
    ops = []
    total = {}
    seen = {q: {} for q in Q}
    hist = {}
    nd = [0, 0]
    sent = [0, 0]
    prev = [None]
    pd = [0]
    ALL = slice(None)

    def A(name, lo=None, hi=None, step=None, rows=None):
        r = ALL if rows is None else slice(rows[0], rows[1])
        if lo is None:
            return (T[name][:] if rows is None else T[name][r], name, 0, BIG)
        if step is None:
            return (T[name][r, lo:hi], name, lo, hi)
        return (T[name][r, lo:hi:step], name, lo, hi)

    def M(name, *ix):
        return (T[name][ix], name, 0, BIG)

    def IND(win, off):
        return (win[0].indirect(off[0]), win[1], win[2], win[3], off)

    def need(q, sem, val):
        if seen[q].get(sem, 0) < val:
            Q[q].wait_ge(T.sem[sem], val)
            seen[q][sem] = val

    def size(o):
        if len(o) > 4:
            return 16 * size(o[4])
        k = 1
        for d in list(o[0].shape)[1:]:
            k *= int(d)
        return k

    def cost(q, outs, ins, base):
        k = max(size(x) for x in outs + ins)
        if q == "p":
            return max(64, size(outs[0])) * PE * (4 if SCRATCH[ins[0][1]][2] == F32 else 1)
        if q == "g":
            return 170 + 2 * k * CYC
        if len(outs[0]) > 4:
            return 50 + k * 3.8 * CYC
        if any(len(x) > 4 for x in ins):
            return 55 + k * 1.56 * CYC
        if base == 0:
            base = 0.5 if all(SCRATCH[x[1]][2] in (BF, F16, U16) for x in outs + ins if size(x) > 1) else 1
        if base == 2 and any(SCRATCH[x[1]][0] == "psum" for x in ins):
            base = 1
        return (FIXA if q == "a" else FIX) + max(64, k * base) * CYC

    def add(q, outs, ins, fn, busy, lat, sem, inc, after=None, done=False):
        dma = sem is not None
        acc = [(o, True) for o in outs] + [(o, False) for o in ins]
        acc += [(o[4], False) for o in outs + ins if len(o) > 4]
        pre = {}
        if after is not None:
            pre[after] = done
        me = len(ops)
        for o, wr in acc:
            ps = SCRATCH[o[1]][0] == "psum"
            for lo, hi, w2, j in hist.get(o[1], []):
                over = lo < o[3] and o[2] < hi
                if not (ps or (over and (w2 or wr))):
                    continue
                if ops[j]["q"] == q and not dma and not ops[j]["dma"]:
                    wait = q != "p" and over and (w2 or wr)
                else:
                    wait = True
                pre[j] = pre.get(j, False) or wait
        kind = "S" if any(len(o) > 4 for o in outs) else "G" if any(len(o) > 4 for o in ins) else ""
        ops.append({"q": q, "fn": fn, "busy": busy, "lat": lat, "sem": sem, "inc": inc, "pre": pre, "dma": dma, "kind": kind})
        for o, wr in acc:
            h = hist.setdefault(o[1], [])
            if SCRATCH[o[1]][0] == "psum":
                h[:] = [e for e in h if ops[e[3]]["q"] == q and q != "p" and e[2]]
            elif wr and len(o) == 4:
                h[:] = [e for e in h if not (o[2] <= e[0] and e[1] <= o[3])]
            h.append((o[2], o[3], wr, me))
        return me

    def op(q, outs, ins, fn, base=1):
        ins = [x for x in ins if isinstance(x, tuple)]
        c = cost(q, outs, ins, base)
        add(q, outs, ins, fn, c, c, None, 1, prev[0] if q == "g" else None)

    def dma(q, out, in_, after=None, also=None):
        outs = [out] if isinstance(out, tuple) else []
        ins = [in_] if isinstance(in_, tuple) else []
        o = (outs + ins)[0]
        sem = "d%d" % nd[0]
        nd[0] += 1
        by = size(o) * int(o[0].shape[0]) * (2 if SCRATCH[o[1]][2] == BF else 4)
        sent[0] = sent[1]
        sent[1] += by
        if also is not None:
            return add(q, outs, ins, lambda: Q[q].dma_start(ap(out), ap(in_)).then_inc(T.sem[sem], 16), 100,
                       LOC + by / LOCR, sem, 16, hist[also[1]][0][3], True)
        return add(q, outs, ins, lambda: Q[q].dma_start(ap(out), ap(in_)).then_inc(T.sem[sem], 16), 100,
                   LOC + (by + (sent[0] if after is not None else 0)) / LOCR, sem, 16, after)

    def emit():
        m = len(ops)
        if m not in PLAN:
            PLAN[m] = order(ops)
        val = [0] * m
        for i in PLAN[m][1]:
            o = ops[i]
            q = o["q"]
            if q == "g" and o["fn"] is None:
                continue
            if q not in "rh":
                want = {}
                for j, wait in o["pre"].items():
                    if wait:
                        sem = ops[j]["sem"] or "c" + ops[j]["q"]
                        want[sem] = max(want.get(sem, 0), val[j])
                for sem, v in want.items():
                    need(q, sem, v)
            if o["dma"]:
                if q not in "rh":
                    o["fn"]()
                val[i] = total[o["sem"]] = o["inc"]
            else:
                o["fn"]().then_inc(T.sem["c" + q], 1)
                val[i] = total["c" + q] = total.get("c" + q, 0) + 1
        for sem, v in total.items():
            need("s", sem, v)

    def ap(x):
        return x[0] if isinstance(x, tuple) else x

    def cp(out, in_):
        op("v", [out], [in_], lambda: g.vector.tensor_copy(out[0], in_[0]), 0)

    def tt(out, a, b, o):
        op("v", [out], [a, b], lambda: g.vector.tensor_tensor(out[0], a[0], b[0], o), 2)

    def ts(out, a, s1, o1, s2=None, o2=None):
        if o2 is None:
            op("v", [out], [a, s1], lambda: g.vector.tensor_scalar(out[0], a[0], ap(s1), None, o1), 0)
        else:
            op("v", [out], [a, s1, s2], lambda: g.vector.tensor_scalar(out[0], a[0], ap(s1), ap(s2), o1, o2), 0)

    def ms(out, c):
        op("v", [out], [], lambda: g.vector.memset(out[0], c), 0)

    def tr(out, in_):
        op("v", [out], [in_], lambda: g.vector.transpose(out[0], in_[0]))

    def scan(out, a, b, init, o0, o1):
        op("v", [out], [a, b], lambda: g.vector.tensor_tensor_scan(out[0], a[0], b[0], init, o0, o1), 0)

    def act(out, in_, f, bias=0.0, scale=1.0):
        op("a", [out], [in_, bias, scale], lambda: g.scalar.activation(out[0], in_[0], f, bias=ap(bias), scale=ap(scale)))

    def mm(out, l, r, start=True, stop=True):
        op("p", [out], [l, r], lambda: g.tensor.matmul(out[0], l[0], r[0], start, stop))

    def mms(out, *pairs):
        for i, (l, r) in enumerate(pairs):
            mm(out, l, r, i == 0, i == len(pairs) - 1)

    def iota(out, pat, base, cm, fl=True):
        if fl:
            op("g", [out], [], lambda: g.iota(out[0], pat, base, cm, allow_small_or_imprecise_dtypes=True))
        else:
            op("g", [out], [], lambda: g.iota(out[0], pat, base, cm))

    def asel(out, in_, pat, cmp_, fill, base, cm):
        op("g", [out], [in_], lambda: g.affine_select(out[0], in_[0], pat, cmp_, fill, base, cm))

    def push(count):
        for _ in range(count):
            push_one(nd[1], *WRITES[nd[1]])
            nd[1] += 1

    def push_one(i, t, lo, hi, via):
        dst = T.cores[(rank - JUMPS[t]) % n]
        to = helper(T, topo, rank, via) if via else dst
        rid, pid, _ = topo.addr(to)
        eng = first_step(topo, core, to, dst, via)
        src = A("X", O + lo, O + hi)
        arr, snt = "arr%d" % i, "snt%d" % i
        by = (hi - lo) * 256 / LINK
        one = by / 4 if via == 3 else by
        me = add("g", [], [src], lambda: g.remote_dma(T["R%d" % t][:, lo:hi], src[0], T.sem[arr], T.sem[snt], pid, rid,
                                                     sum(1 << e for e in eng)), 300 if i else FIRST, HOP + one,
                 snt, len(eng), prev[0])
        if i == 0:
            for j in range(me):
                if ops[j]["q"] == "g":
                    ops[me]["pre"].setdefault(j, False)
        prev[0] = me
        frm = (rank + JUMPS[t]) % n
        k2 = len(topo.engines(helper(T, topo, frm, via) if via else T.cores[frm], core))
        add("h" if via in (1, 2) else "r", [A("R%d" % t, lo, hi)], [], None, one,
            HOP + one + (HOP + by if via else 0) - 300,
            arr, k2, after=me)

    def col(j):
        return A("COL", j, j + 1)

    cut = WRITES[0][2]
    for gi in range(6):
        dma("a", A("COVI", 16 * gi, 16 * gi + 16, rows=(0, 72)), T.cov[gi])
    d = dma("s", A("X", O, O + cut), T.lab[:, 0:cut])
    d = dma("s", A("WI"), T.wts[:], d)
    d = dma("s", A("LFI", 0, 14), T.leaf[:], d)
    for gi in range(6, 8):
        d = dma("s", A("COVI", 16 * gi, 16 * gi + 16, rows=(0, 72)), T.cov[gi], d)
    d = dma("s", A("X", O + cut, O + B0), T.lab[:, cut:B0], d)
    if ACT_HOLD[0] < B0:
        act(A("X2", ACT_HOLD[0], B0), A("X", O + ACT_HOLD[0], O + B0), AF.Identity)
    d = dma("s", A("AC"), T.act[:], d)
    d = dma("s", A("PTH"), T.pth[:], d)

    kinds = sorted(set(VEC_CMP))
    iota(A("IP", 0, 2), [[16, 2]], 0, 1, False)
    iota(A("IH"), [[1, 5], [100, 2], [0, 16]], -100, 0)
    ms(A("ONES"), 1.0)
    ms(A("ZL", 0, S * len(kinds)), 0.0)
    ms(A("X", 0, O), 512.0)
    ms(A("CS1"), -10.5 * 65536)
    ms(A("CS2"), -5.0 * 65536)
    iota(A("IG"), [[1, 9], [0, 16]], 0, 0)
    iota(A("IC"), [[1, 16]], 0, 0)
    asel(A("IDB"), A("ONES", 0, 128), [[-1, 128]], OP.is_equal, 0.0, 0, 1)
    ts(A("IP", 2, 3), A("IP", 0, 1), 15, OP.bitwise_and)
    ts(A("IP", 3, 4), A("IP", 0, 1), 4, OP.arith_shift_right)
    ts(A("IP", 4, 5), A("IP", 0, 1), 5, OP.arith_shift_right)
    ts(A("IP", 5, 7), A("IP", 0, 2), 4, OP.arith_shift_right, 1, OP.bitwise_and)
    cp(A("COL", 0, 5), A("IP", 2, 7))
    ts(A("AOF"), A("ONES", 0, 18), col(0), OP.mult)
    for h in range(2):
        ts(A("XO", 144 * h, 144 * h + 144), A("IH", 0, 144), col(2), OP.is_equal, col(4 - h), OP.mult)
    ts(A("WG"), A("WI"), 2048.0, OP.is_gt, -4096.0, OP.mult)
    tt(A("WS"), A("WI"), A("WG"), OP.add)
    tt(A("LW"), IND(A("WS"), A("AOF")), A("XO"), OP.mult)
    ts(A("BLKH"), A("IG"), col(1), OP.is_equal)
    ts(col(9), col(0), 7.0, OP.is_ge, -208.0, OP.mult)
    ts(A("BLKM"), A("IG", 0, 128), col(1), OP.is_equal, float(1 << 23), OP.mult)
    act(A("NIDB"), A("IDB"), AF.Identity, scale=-1.0)
    act(col(10), col(0), AF.Identity, bias=col(9), scale=32.0)
    ts(A("ROL"), A("IC"), col(10), OP.add, 223.0, OP.min)
    cp(A("LFU", 0, 14), A("LFI", 0, 14))
    ts(A("COVH", rows=(0, 72)), A("COVI", rows=(0, 72)), float(O), OP.add)
    mm(A("PM", 0, 72), A("COVH", rows=(0, 72)), A("IDB", 0, 72, rows=(0, 72)))
    cp(A("COVL", 0, 72), A("PM", 0, 72))
    act(col(6), col(0), AF.Identity, bias=1.0)
    act(col(7), col(0), AF.Identity, bias=17.0)
    act(col(12), col(0), AF.Identity, bias=-4096.0, scale=-2048.0)
    act(A("BLKT"), A("BLKM"), AF.Identity, scale=-1.0 / 4096)
    act(A("CA"), A("IDB"), AF.Identity, bias=1024.0, scale=CADD - 131072.0)

    push(len([w for w in WRITES if w[0] == 0]))
    prev[0] = add("g", [], [], None, HOLD, HOLD, None, 0, prev[0])
    ms(A("XH"), 0.0)
    ms(A("SELB"), 0.0)
    for h in range(2):
        act(A("XH", 16 + 128 * h, 144 + 128 * h), A("IDB"), AF.Identity, scale=col(4 - h))
    cp(A("SELB", 15, 128, 16), A("BLKH", 15, 128, 16))
    if any(PE_HASH):
        for m in range(2):
            ts(A("WL%d" % m), A("SELB"), A("WS", m, m + 1), OP.mult)
    iota(A("IA"), [[0, 14], [1, 16]], 0, 0)
    iota(A("IJ"), [[16, 48]], B0 - 2048, 0)
    act(col(8), col(0), AF.Identity, bias=4096.0, scale=-4096.0)
    act(A("MASKD"), A("IA"), AF.Relu, bias=col(8), scale=4096.0)
    act(A("SELN"), A("SELB"), AF.Identity, scale=-128.0)
    ts(A("NEWH", 0, 42), A("IJ", 0, 42), col(0), OP.add)
    asel(A("TRI"), A("BLKT"), [[1, 128]], OP.is_gt, 0.0, 0, -1)
    asel(A("TRI"), A("TRI"), [[1, 128]], OP.not_equal, 2048.0, 0, -1)
    asel(A("NI2"), A("ZL", 0, 128), [[1, 128]], OP.not_equal, -2048.0, 0, -1)
    asel(A("PI2"), A("ZL", 0, 128), [[1, 128]], OP.not_equal, 2048.0, 0, -1)
    asel(A("RST"), A("ONES", 0, 336), [[0, 21], [1, 16]], OP.is_equal, 0.0, 0, 0)
    asel(A("LF", 0, 14), A("LFI", 0, 14), [[1, 14]], OP.is_ge, 0.0, 0, 0)
    for i, k in enumerate(kinds):
        ts(col(13 + i), col(0), 16.0 - k, OP.is_ge, 1.0, OP.add)
        act(A("ZL", S * i + S - 1, S * i + S), col(13 + i), AF.Identity, bias=7.5, scale=-16.0)
    asel(A("SHF"), A("BLKH", 0, 128), [[1, 128]], OP.is_equal, 0.0, -1, -1)
    asel(A("E0"), A("IDB"), [[0, 8], [1, 16]], OP.is_equal, 0.0, 0, 0)


    def cross(name, h, rho):
        return A(name, 144 * h + 16 - 16 * rho, 144 * h + 144 - 16 * rho)

    def px(h):
        return M("PX", ALL, slice(0, 7), h, ALL)

    PXA = M("PX", ALL, slice(0, 7), ALL, ALL)

    def half(name, rho, lo=0):
        return A(name, lo + 112 * rho, lo + 112 * rho + 112)

    def bk(bank, w):
        return M(bank, ALL, slice(0, w // 32), ALL, ALL) if bank in ("PH0", "PX") else A(bank, 0, w)

    def path_list():
        for h in range(2):
            mms(px(h), *[(cross("XH", h, rho), half("PV", rho)) for rho in range(2)])
        tr(A("TOP"), PXA)
        cp(A("POF"), IND(A("TOP", 0, 224), A("ROL", 0, 16)))

    def hold_v(lo, hi, bank):
        own = A("X2", lo, hi) if lo < B0 else A("X", O + lo, O + hi)
        tt(A("CMP", lo, hi), IND(A("X", 0, O + max(lo, B0)), A("COVL", lo // 16, hi // 16)), own, OP.is_le)
        mms(bk(bank, hi - lo), (A("CS1"), A("ONES", 0, hi - lo)), (A("BLKM"), A("CMP", lo, hi)))

    def hold_max(lo, hi, bank):
        tt(A("XP", lo, hi), bk(bank, hi - lo), A("X", O + lo, O + hi), OP.max)

    def hold_a(lo, hi, bank):
        act(A("XC", lo, hi), IND(A("X", 0, O + B0), A("COVL", lo // 16, hi // 16)), AF.Identity)
        mms(bk(bank, hi - lo), (A("IDB"), A("X", O + lo, O + hi)), (A("NIDB"), A("XC", lo, hi)))
        act(A("CMP", lo, hi), bk(bank, hi - lo), AF.Sign, bias=0.5)
        mms(bk(bank, hi - lo), (A("CS2"), A("ONES", 0, hi - lo)), (A("BLKM"), A("CMP", lo, hi)))

    def sel_list(selname, src, lo=0):
        return [(A(selname, 15 - a, 143 - a), A(src, lo + a, lo + S, 16)) for a in range(16)]

    cp(A("PV"), IND(A("PTH", 0, B0), A("LFU", 0, 14)))
    for t in range(RO):
        b = B0 + t * S
        last = t == RO - 1
        XB = A("X", 0, O + b)
        na = ACT_HOLD[t]
        old = b - S if t else b
        Z, SUS, CI, xk = A("Z", S * t, S * t + S), A("SUS", S * t, S * t + S), A("CI", S * t, S * t + S), 3584 * (t & 1)
        iota(A("IS", S * t, S * t + S), [[1, S]], b, 0)
        asel(A("NEWN", S * t, S * t + S), A("IS", S * t, S * t + S), [[1, S]], OP.is_ge, 0.0, 0, 0)
        act(A("XV"), IND(A("X", O, O + b), A("LFU", 0, 14)), AF.Identity)
        if PE_HASH[t]:
            for m in range(2):
                mms(M("PX", ALL, 0, m, slice(0, 14)), *sel_list("WL%d" % m, "XV"))
            cp(M("HI3", ALL, ALL, slice(0, 14)), M("PX", ALL, 0, ALL, slice(0, 14)))
        else:
            for h in range(2):
                mms(px(h), *[(cross("LW", h, rho), half("XV", rho)) for rho in range(2)])
            tr(A("TOH"), PXA)
            cp(A("HI"), IND(A("TOH", 0, 224), A("ROL", 0, 2)))
        if t == 0:
            path_list()
        hi = [M("HI3", ALL, m, slice(0, 14)) if PE_HASH[t] else A("HI", 16 * m, 16 * m + 14) for m in range(2)]
        ts(A("HA", 0, 14), hi[0], DA - 1, OP.bitwise_and)
        ts(A("HQ", 0, 14), hi[1], 4095, OP.bitwise_and)
        cp(A("AL", 0, 14), A("HA", 0, 14))
        ts(A("QL", 0, 14), A("HQ", 0, 14), b / 4096.0, OP.mult, FLOOR, OP.add)
        if na:
            hold_a(0, min(na, 512), "PH0")
            hold_max(0, min(na, 512), "PH0")
        if na > 512:
            hold_a(512, na, "PX" if t else "PD0")
            hold_max(512, na, "PX" if t else "PD0")
        for lo, hi in [(x, min(x + 512, B0)) for x in range(na, B0, 512)] + [(x, x + S) for x in range(B0, old, S)]:
            hold_v(lo, hi, "PP")
            hold_max(lo, hi, "PP")
        act(A("DZ"), IND(A("AC", 0, DA), A("AL", 0, 14)), AF.Identity)
        mms(A("PM", 0, 224), (A("IDB"), A("XV")), (A("NIDB"), A("DZ")))
        act(Z, A("PM", 0, 224), AF.Abs)
        mms(A("PM", 224, 448), *[(cross("LW", h, h), Z) for h in range(2)])
        cp(A("ZI"), A("PM", 224, 448))
        ts(A("ZJ"), A("ZI"), 4095, OP.bitwise_and)
        ts(A("COF"), A("ZJ"), b / 4096.0, OP.mult, O + FLOOR, OP.add)
        ts(CI, A("COF"), 1.0 - O, OP.add)
        if t:
            hold_v(old, b, "PM")
            hold_max(old, b, "PM")

        src = XB
        if SNAP[t]:
            src = A("XS", 0, O + b)
            asel(src, XB, [[1, O + b]], OP.is_ge, 0.0, 0, 0)
        for c in range(0, S, GW):
            act(A("XK", xk + 16 * c, xk + 16 * (c + GW)), IND(src, A("COF", c, c + GW)), AF.Identity)
        if ON_ACT[t]:
            act(A("CE"), IND(A("R%d" % t, 0, b), A("QL", 0, 14)), AF.Identity, bias=CADD, scale=-1.0)
        else:
            ts(A("CE"), IND(A("R%d" % t, 0, b), A("QL", 0, 14)), -1.0, OP.mult, CADD, OP.add)
        if LISTS_FIRST:
            ops[-1]["pre"].setdefault(hist["COF"][0][3], False)
        if "E" in ON_VEC:
            ts(A("E"), A("CE"), -1.0, OP.mult, CADD, OP.add)
        else:
            act(A("E"), A("CE"), AF.Identity, bias=CADD, scale=-1.0)
        if t:
            ts(A("EM"), A("E"), 255.5, OP.is_gt)
            dma("s", T.yp[:, S * t - S:S * t], A("YP", S * t - S, S * t), also=A("CE"))
        nv = 16 - ACT_PATH[t]
        if nv < 16:
            mms(bk("PH0", 224), (A("CA"), A("ONES", 0, 224)), (A("NIDB"), A("E")))
        ks = list(range(nv - 1, t - 1, -1)) + list(range(15, nv - 1, -1)) + list(range(t - 1, -1, -1))
        for k in ks:
            src = IND(A("XP", 0, B0 + S * max(0, t - k)), A("POF", 16 * k, 16 * k + 14))
            if k < nv:
                tt(A("PO", S * k, S * k + S), src, A("CE"), OP.add)
            else:
                act(A("XG", S * k, S * k + S), src, AF.Identity)
                tt(A("PO", S * k, S * k + S), A("XG", S * k, S * k + S), bk("PH0", 224), OP.add)
            mm(A("PP", 0, 224), A("SELB", 15 - k, 143 - k), A("PO", S * k, S * k + S), k == ks[0], k == ks[-1])
        ts(A("LOW"), A("PP", 0, 224), LOWT, OP.is_lt, 2.0, OP.mult)
        ts(A("HLD"), A("PP", 0, 224), 8388608.0, OP.is_ge, 2.0, OP.mult)
        mms(A("PM", 0, 224), (A("IDB"), A("PV")), *([(A("BLKT"), A("EM"))] if t else []),
            (A("TRI"), A("LOW")), (A("BLKT"), A("HLD")))
        mm(A("PP", 0, 224), A("BLKM"), A("HLD"))
        ts(A("SH"), A("PM", 0, 224), O - 4096.0, OP.add, 0.0, OP.max)
        if "SUS" in ON_VEC:
            ts(SUS, A("PP", 0, 224), -1.0, OP.add, 1.0, OP.min)
        else:
            act(SUS, A("PP", 0, 224), AF.Sign, bias=-0.5)
        mms(bk("PH0", 224), (A("IDB"), Z), (A("BLKM"), A("HLD")))
        ts(A("X", O + b, O + b + S), bk("PH0", 224), 256.0, OP.min)
        if not last:
            push(len([w for w in WRITES if w[0] == t + 1 and w[1] >= b]))
        else:
            dma("s", T.yx[:, b:W], A("X", O + b, O + W))
        for h in range(2):
            mms(px(h), *[(cross("XO", h, rho), M("SH", ALL, ALL, rho, ALL)) for rho in range(2)])
        mms(bk("PH0", 224), (A("IDB"), A("MASKD")), (A("BLKH", 0, 128), A("SH")))
        mm(M("PH0", ALL, slice(7, 14), 0, ALL), A("BLKH", 0, 128), M("SH", ALL, ALL, 0, ALL))
        tr(A("TGX"), PXA)
        tt(A("EQ", 0, 224), bk("PH0", 224), A("TGX"), OP.not_equal)
        tt(A("EQ", 224, 336), M("PH0", ALL, slice(7, 14), 0, ALL), M("TGX", ALL, ALL, 1, ALL), OP.not_equal)
        scan(A("SC"), A("RST"), A("EQ"), 1.0, OP.max, OP.min)
        tt(A("OFF", 0, 14), A("SC", 15, 224, 16), M("TGX", ALL, ALL, ALL, 0), OP.mult)
        tt(A("OFF", 16, 23), A("SC", 239, 336, 16), A("OFF", 1, 14, 2), OP.mult)
        ts((T.OFU[:, 0:14:2], "OFU", 14, 15), A("OFF", 0, 14, 2), col(6), OP.max)
        ts((T.OFU[:, 1:14:2], "OFU", 0, 14), A("OFF", 16, 23), col(7), OP.max)
        cp(A("TGU", 0, 14), M("TGX", ALL, ALL, ALL, 0))
        tt(A("V"), IND(XB, A("TGU", 0, 14)), A("E"), OP.max)
        scan(A("SGN", S * t, S * t + S), SUS, A("ZL", S * kinds.index(VEC_CMP[t]), S * kinds.index(VEC_CMP[t]) + S),
             1.0, OP.mult, OP.add)
        mms(A("PP", 448, 462), (A("IDB"), A("NEWH", 14 * t, 14 * t + 14)), *sel_list("SELN", "SUS", S * t))
        mms(A("PP", 224, 448), (A("E0"), A("NEWN", S * t, S * t + S)), (A("SHF"), A("PV")), (A("NI2"), SUS))
        if not last:
            mms(A("PP", 0, 224), (A("NI2"), A("ONES", 0, 224)), (A("IDB"), A("PV")), (A("PI2"), SUS))
        tt(A("YV" if last else "LF", 0, 14), A("PP", 448, 462), A("LF", 0, 14), OP.max)
        if "YP" in ON_VEC:
            ts(A("YP", S * t, S * t + S), A("PP", 224, 448), -2048.0, OP.add, 0.0, OP.max)
        else:
            act(A("YP", S * t, S * t + S), A("PP", 224, 448), AF.Relu, bias=-2048.0)
        if last:
            dma("s", T.yp[:, S * t:S * t + S], A("YP", S * t, S * t + S))
        if not last:
            cp(A("LFU", 0, 14), A("LF", 0, 14))
            tt(A("PV"), A("PP", 0, 224), A("YP", S * t, S * t + S), OP.max)
            path_list()
        for bb in range(12, -1, -2):
            cp(IND(XB, (T.OFU[:, bb:bb + 2], "OFU", 0, 15)), A("V", 16 * bb, 16 * bb + 32))
        if not last:
            push(len([w for w in WRITES if w[0] == t + 1 and w[1] < b]))
            lo = ACT_HOLD[t + 1]
            if lo < B0 and COPY_ON == "v":
                cp(A("X2", lo, B0), A("X", O + lo, O + B0))
            elif lo < B0 and COPY_ON == "s":
                dma("s", A("X2", lo, B0), A("X", O + lo, O + B0))
            elif lo < B0 and COPY_ON == "a":
                act(A("X2", lo, B0), A("X", O + lo, O + B0), AF.Identity)
            elif lo < B0:
                asel(A("X2", lo, B0), A("X", O + lo, O + B0), [[1, B0 - lo]], OP.is_ge, 0.0, 0, 0)
        else:
            sent[1] = 0
            d = dma("s", T.yx[:, 0:b // 2], A("X", O, O + b // 2))
            dma("s", T.yx[:, b // 2:b], A("X", O + b // 2, O + b), d)
            dma("s", T.yv[:], A("YV", 0, 14))
        ns = 16 - VEC_CMP[t]
        if ns < 16:
            mm(A("PH1", 0, 224), A("IDB"), Z)
        for hf in range(2):
            def xm(m):
                return A("XK", xk + 1792 * hf + m, xk + 1792 * hf + 1792, 16)

            def sg(m, k=1):
                return A("SG", 1792 * hf + 112 * m, 1792 * hf + 112 * (m + k))
            for m in range(0, ns, 4):
                bank = "PD%d" % (pd[0] & 1)
                pd[0] += 1
                k = min(4, ns - m)
                for j in range(k):
                    mms(A(bank, 112 * j, 112 * j + 112), (A("IDB"), half("Z", hf, S * t)), (A("NIDB"), xm(m + j)))
                act(sg(m, k), A(bank, 0, 112 * k), AF.Sign, bias=0.5)
            for m in range(ns, 16):
                tt(sg(m), xm(m), half("PH1", hf), OP.is_le)
            mms(half("PC", hf), *[(A("SELB", 15 - m, 143 - m), sg(m)) for m in range(16)])
        act(A("FIT"), A("PC", 0, 224), AF.Sign, bias=A("SGN", S * t + S - 1, S * t + S),
            scale=col(13 + kinds.index(VEC_CMP[t])))
        mms(A("PC", 224, 448), (A("IDB"), CI), (A("NI2"), SUS), (A("TRI"), A("FIT")))
        ts(A("SH2"), A("PC", 224, 448), col(12), OP.add, 0.0, OP.max)
        if not last:
            mms(A("PC", 448, 462), *sel_list("SELB", "SH2"))
        mm(A("PC", 0, 224, rows=(0, 8)), A("BLKH", 0, 128, 16), A("SH2"))
        if not last:
            ts(A("COVL", 72 + 14 * t, 86 + 14 * t), A("PC", 448, 462), O - 1.0, OP.add)
        if "YC" in ON_VEC or last and "YC2" in ON_VEC:
            ts(A("YC", S * t, S * t + S, rows=(0, 8)), A("PC", 0, 224, rows=(0, 8)), -1.0, OP.add)
        else:
            act(A("YC", S * t, S * t + S, rows=(0, 8)), A("PC", 0, 224, rows=(0, 8)), AF.Identity, bias=-1.0)
    dma("s", T.yc[:], A("YC", rows=(0, 8)))
    emit()
